import numpy as np
import ml_dtypes


def mxq(x, axis, fmt="e4m3"):
    dtype, down = {"e4m3": (ml_dtypes.float8_e4m3fn, 7), "e5m2": (ml_dtypes.float8_e5m2, 14)}[fmt]
    v = np.moveaxis(np.asarray(x, np.float32).astype(ml_dtypes.bfloat16).astype(np.float64), axis, -1)
    blocks = v.reshape(v.shape[:-1] + (-1, 32))
    amax = np.abs(blocks).max(-1, keepdims=True)
    byte = np.maximum(np.where(amax > 0, np.frexp(amax)[1] - 1 + 127, 0) - down, 1)
    scale = np.exp2(byte - 127.0)
    codes = (blocks / scale).astype(np.float32).astype(dtype).astype(np.float64)
    return np.moveaxis((codes * scale).reshape(v.shape), -1, axis)


WIDE = False


def mx_kscale(k):
    if not WIDE:
        return np.ones(k)
    levels = np.array([24, -24, 12, -12, 0])
    if k % 512:
        return np.exp2(np.random.permutation(np.resize(levels, k // 32))).repeat(32)
    a = np.empty((k // 512, 16))
    for p in range(k // 512):
        a[p, :8] = np.random.permutation(np.resize(levels, 8))
        for g in range(8):
            far = levels[np.abs(levels - a[p, g]) >= 10]
            a[p, g + 8] = far[np.random.randint(len(far))]
    return np.exp2(a.ravel()).repeat(32)


def f64(x):
    return np.asarray(x).astype(np.float64)


def striped(idx):
    return np.tile(idx.reshape(-1, 16).T, (8, 1)).astype(np.uint16)


def unstriped(offs):
    return offs[:16].T.reshape(-1).astype(np.int64)


E2M1 = np.array([0.0, 0.5, 1.0, 1.5, 2.0, 3.0, 4.0, 6.0, -0.0, -0.5, -1.0, -1.5, -2.0, -3.0, -4.0, -6.0])


def pack_weight(w, fmt):
    k, n = w.shape
    w = f64(np.asarray(w, np.float32).astype(ml_dtypes.bfloat16)).reshape(k // 32, 32, n)
    amax = np.abs(w).max(1)
    if fmt == "e4m3":
        byte = np.frexp(amax)[1] - 1 + 127 - 7
    else:
        mant, ex = np.frexp(amax / 6.0)
        byte = np.where(mant > 0.5, ex, ex - 1) + 127
    byte = np.clip(np.where(amax > 0, byte, 1), 1, 254)
    scaled = (w * np.exp2(127.0 - byte)[:, None, :]).reshape(k, n).astype(np.float32)
    by_word = np.ascontiguousarray(scaled.reshape(k // 512, 128, 4, n).transpose(0, 1, 3, 2))
    if fmt == "e4m3":
        words = by_word.astype(ml_dtypes.float8_e4m3fn).view(np.uint8)
    else:
        c = by_word.astype(ml_dtypes.float4_e2m1fn).view(np.uint8) & 0xF
        words = (c[..., 0::2] | (c[..., 1::2] << 4)).reshape(k // 512, 128, 2 * n)
    return np.ascontiguousarray(words), np.ascontiguousarray(byte.astype(np.uint8).reshape(k // 512, 16, n))


def unpack_weight(words, scales, fmt):
    g, _, n = scales.shape
    words = np.ascontiguousarray(words).reshape(g, 128, n, -1)
    if fmt == "e4m3":
        vals = words.view(ml_dtypes.float8_e4m3fn).astype(np.float64)
    else:
        nib = np.empty((g, 128, n, 4), np.uint8)
        nib[..., 0::2] = words & 0xF
        nib[..., 1::2] = words >> 4
        vals = E2M1[nib]
    vals = vals * np.repeat(np.exp2(scales.astype(np.float64) - 127.0), 8, axis=1)[..., None]
    return vals.transpose(0, 1, 3, 2).reshape(g * 512, n)


def pack_table4(v):
    words, scales = pack_weight(v, "e2m1")
    g, t = words.shape[0] // 2, v.shape[1]
    return np.ascontiguousarray(words.reshape(g, 2, 128, t, 2).transpose(0, 2, 3, 1, 4).reshape(g, 128, t, 4)), scales


def unpack_table4(words, scales):
    g, _, t, _ = words.shape
    return unpack_weight(words.reshape(g, 128, t, 2, 2).transpose(0, 3, 1, 2, 4).reshape(2 * g, 128, 2 * t), scales, "e2m1")


K, R, N, T, J = 1024, 512, 512, 2048, 512


def setup_inputs():
    n = np.random.standard_normal
    s = mx_kscale(K)[:, None]
    u = mx_kscale(R)[:, None]
    p_tab = pack_table4(n((K, T)) * s)
    p_wc = pack_weight(n((K, R)) / np.sqrt(K) / s * u.T, "e2m1")
    p_wd = pack_weight(n((R, N)) / np.sqrt(R) / u, "e4m3")
    return {
        "tab_words": p_tab[0],
        "tab_scales": p_tab[1],
        "c": (n((K, J)) * s).astype(np.float32),
        "w": (n((K, R)) / np.sqrt(K) / s * u.T).astype(np.float32),
        "wc_words": p_wc[0],
        "wc_scales": p_wc[1],
        "wd_words": p_wd[0],
        "wd_scales": p_wd[1],
        "offs": striped(np.concatenate([np.random.permutation(T)[:J] for _ in range(3)])),
    }


def reference(tab_words, tab_scales, c, w, wc_words, wc_scales, wd_words, wd_scales, offs):
    idx = unstriped(offs).reshape(3, J)
    tab_ = unpack_table4(tab_words, tab_scales)[:, idx]
    c_ = mxq(f64(c), 0, "e4m3")
    w_ = mxq(f64(w), 0, "e4m3")
    a0 = w_.T @ tab_[:, 0]
    a1 = w_.T @ tab_[:, 1]
    a2 = w_.T @ tab_[:, 2]
    wc_ = unpack_weight(wc_words, wc_scales, "e2m1")
    ac = wc_.T @ c_
    h = np.maximum(np.maximum(np.maximum(a0, a1), a2) + ac, 0.0)
    h_ = mxq(h, 0, "e4m3")
    wd_ = unpack_weight(wd_words, wd_scales, "e4m3")
    y = wd_.T @ h_
    return y

@@ -1,0 +1,297 @@
+from contextlib import ExitStack
+
+import concourse.mybir as mybir
+from concourse.masks import make_identity
+
+K, R, N, T, J = 1024, 512, 512, 2048, 512
+G = 3
+FLOPS = 2 * K * R * J * (G + 1) + 2 * R * N * J
+
+F32 = mybir.dt.float32
+BF16 = mybir.dt.bfloat16
+I32 = mybir.dt.int32
+U32 = mybir.dt.uint32
+U16 = mybir.dt.uint16
+U8 = mybir.dt.uint8
+FP8X4 = mybir.dt.float8_e4m3fn_x4
+FP4X4 = mybir.dt.float4_e2m1fn_x4
+ACT = mybir.ActivationFunctionType
+ALU = mybir.AluOpType
+
+P = 128
+PACK = 4
+K_PASS = P * PACK
+PASSES = K // K_PASS
+HALF = 256
+CHUNK = 128
+QUADS = 4
+SHIFT = 4
+
+
+def tile_list_pnet_none_kernel(
+    tc, tab_words, tab_scales, c, w, wc_words, wc_scales, wd_words, wd_scales, offs, out
+):
+    nc = tc.nc
+    with ExitStack() as ctx:
+        keep = ctx.enter_context(tc.tile_pool(name="keep", bufs=1))
+        psum = ctx.enter_context(tc.psum_pool(name="psum", bufs=8))
+
+        def sb(name, shape, dtype):
+            return keep.tile(shape, dtype, name=name, align_bytes=64)
+
+        def bank(name):
+            return psum.tile([P, 512], F32, name=name, tag="bank")
+
+        offsets = keep.tile([P, G * J // 16], U16, name="offsets")
+        nc.sync.dma_start(offsets[:], offs)
+
+        tab_s = sb("tab_s", [P, T // 4], I32)
+        nc.vector.memset(tab_s[:], 0)
+        for q in range(QUADS):
+            nc.sync.dma_start(tab_s[32 * q : 32 * q + 8, :], tab_scales[:, 4 * q : 4 * q + 4, :].bitcast(I32))
+
+        def load_f32(name, src, a, h):
+            raw = sb(name, [P, PACK, HALF], F32)
+            rows = src[a * K_PASS : (a + 1) * K_PASS, h * HALF : (h + 1) * HALF]
+            nc.sync.dma_start(raw[:], rows.rearrange("(p i) x -> p i x", i=PACK))
+            return raw
+
+        picked_s1 = sb("picked_s1", [P, G * J // 4], I32)
+        wc_s = sb("wc_s", [P, PASSES, R // 4], I32)
+        wd_s = sb("wd_s", [P, N // 4], I32)
+        nc.vector.memset(wc_s[:], 0)
+        nc.vector.memset(wd_s[:], 0)
+        nc.vector.memset(picked_s1[:], 0)
+
+        def load_wc_scales(q):
+            rows = wc_scales[:, 4 * q : 4 * q + 4, :].rearrange("a r n -> r a n")
+            nc.sync.dma_start(wc_s[32 * q : 32 * q + 4, :, :], rows.bitcast(I32))
+
+        def load_wd_scales(q):
+            nc.sync.dma_start(wd_s[32 * q : 32 * q + 4, :], wd_scales[0, 4 * q : 4 * q + 4, :].bitcast(I32))
+
+        w_raw = {}
+        c_raw = {}
+        for h in range(2):
+            w_raw[0, h] = load_f32("w_raw0%d" % h, w, 0, h)
+        tab_w = sb("tab_w", [P, T], I32)
+        nc.sync.dma_start(tab_w[:], tab_words[0].rearrange("p t b -> p (t b)").bitcast(I32))
+        for h in range(2):
+            w_raw[1, h] = load_f32("w_raw1%d" % h, w, 1, h)
+            load_wc_scales(2 * h)
+            load_wc_scales(2 * h + 1)
+        wc_w = sb("wc_w", [P, PASSES, R // 2], I32)
+        nc.sync.dma_start(wc_w[:], wc_words.rearrange("a p b -> p a b").bitcast(I32))
+        for a in range(PASSES):
+            c_raw[a, 0] = load_f32("c_raw%d0" % a, c, a, 0)
+            load_wd_scales(2 * a)
+            load_wd_scales(2 * a + 1)
+        wd_w = sb("wd_w", [P, N], I32)
+        nc.sync.dma_start(wd_w[:], wd_words[0].rearrange("p n b -> p (n b)").bitcast(I32))
+        for a in range(PASSES):
+            c_raw[a, 1] = load_f32("c_raw%d1" % a, c, a, 1)
+
+        ident = sb("ident", [P, P], F32)
+        make_identity(nc, ident[:])
+
+        picked_s0 = sb("picked_s0", [P, G * J], U8)
+        nc.vector.tensor_copy(picked_s0[:], tab_s[:].bitcast(U8).indirect(offsets[:]))
+        nc.gpsimd.dma_start(picked_s1[0 : P - SHIFT, :], picked_s0[SHIFT:P, :].bitcast(I32))
+        picked_s = [picked_s0[:], picked_s1[:].bitcast(U8)]
+
+        def round_and_interleave(raw, grouped):
+            nc.scalar.activation(
+                grouped.rearrange("p (y x i) -> p y i x", x=4, i=PACK),
+                raw[:].rearrange("p i (y x) -> p y i x", x=4),
+                ACT.Copy,
+            )
+
+        w_bf = [sb("w_bf%d" % a, [P, R * PACK], BF16) for a in range(PASSES)]
+        w_q = [sb("w_q%d" % a, [P, R], U32) for a in range(PASSES)]
+        w_s = [sb("w_s%d" % a, [P, R], U8) for a in range(PASSES)]
+
+        def quantize_w(a):
+            for h in range(2):
+                round_and_interleave(w_raw[a, h], w_bf[a][:, h * HALF * PACK : (h + 1) * HALF * PACK])
+            nc.vector.quantize_mx(out=w_q[a][:].bitcast(FP8X4), scales=w_s[a][:], in_=w_bf[a][:])
+
+        c_q = {}
+        c_s = {}
+
+        def quantize_c(h):
+            c_bf = sb("c_bf%d" % h, [P, PASSES, HALF * PACK], BF16)
+            c_q[h] = sb("c_q%d" % h, [P, PASSES * HALF], U32)
+            c_s[h] = sb("c_s%d" % h, [P, PASSES * HALF], U8)
+            for a in range(PASSES):
+                round_and_interleave(c_raw[a, h], c_bf[:, a, :])
+            nc.vector.quantize_mx(
+                out=c_q[h][:].bitcast(FP8X4), scales=c_s[h][:], in_=c_bf[:].rearrange("p a x -> p (a x)")
+            )
+
+        parted = {}
+
+        def gather_words(h):
+            pairs = {}
+            for g in range(G + 1):
+                if g < G:
+                    pairs[g] = sb("pairs%d%d" % (g, h), [P, HALF], U32)
+                    col = (g * J + h * HALF) // 16
+                    nc.vector.tensor_copy(
+                        pairs[g][:], tab_w[:].bitcast(U32).indirect(offsets[:, col : col + HALF // 16])
+                    )
+                if g > 0:
+                    parted[g - 1, h] = sb("parted%d%d" % (g - 1, h), [P, PASSES, 2 * HALF], U8)
+                    nc.vector.tensor_copy(
+                        parted[g - 1, h][:].bitcast(U16),
+                        pairs[g - 1][:].bitcast(U16).rearrange("p (j d) -> p d j", d=PASSES),
+                    )
+
+        sums = {}
+
+        def neighbour_pass(ch, g, a):
+            h, j0 = divmod(ch * CHUNK, HALF)
+            if a == 0:
+                sums[ch, g] = bank("sum%d%d" % (ch, g))
+            s0 = g * J + ch * CHUNK
+            nc.tensor.matmul_mx(
+                out=sums[ch, g][:],
+                lhsT=parted[g, h][:, a, 2 * j0 : 2 * (j0 + CHUNK)].bitcast(FP4X4),
+                lhsT_scale=picked_s[a][:, s0 : s0 + CHUNK],
+                rhs=w_q[a][:].bitcast(FP8X4),
+                rhs_scale=w_s[a][:],
+                start=(a == 0),
+                stop=(a == PASSES - 1),
+            )
+
+        def by_word(acc):
+            return acc[:].rearrange("j (p u e) -> j u p e", u=2, e=2)
+
+        def split(flat):
+            return flat[:].rearrange("j (u p e) -> j u p e", u=2, e=2)
+
+        best = {}
+
+        def take_first(ch):
+            best[ch] = sb("first%d" % ch, [P, R], F32)
+            nc.scalar.activation(split(best[ch]), by_word(sums[ch, 0]), ACT.Copy)
+
+        def take_max(ch, g):
+            more = sb("max%d%d" % (ch, g), [P, R], F32)
+            nc.vector.tensor_tensor(split(more), by_word(sums[ch, g]), split(best[ch]), ALU.max)
+            best[ch] = more
+
+        own = {}
+
+        def own_product(ch):
+            h, j0 = divmod(ch * CHUNK, HALF)
+            own[ch] = bank("own%d" % ch)
+            for a in range(PASSES):
+                cols = slice(a * HALF + j0, a * HALF + j0 + CHUNK)
+                nc.tensor.matmul_mx(
+                    out=own[ch][:],
+                    lhsT=c_q[h][:, cols].bitcast(FP8X4),
+                    lhsT_scale=c_s[h][:, cols],
+                    rhs=wc_w[:, a, :].bitcast(U8).bitcast(FP4X4),
+                    rhs_scale=wc_s[:, a, :].bitcast(U8),
+                    start=(a == 0),
+                    stop=(a == PASSES - 1),
+                )
+
+        z = {}
+
+        def add_own(ch):
+            z[ch] = sb("z%d" % ch, [P, R], BF16)
+            nc.vector.tensor_tensor(split(z[ch]), by_word(own[ch]), split(best[ch]), ALU.add)
+
+        h_bf = {}
+
+        def turn_and_relu(ch):
+            turned = bank("turned%d" % ch)
+            for u in range(2):
+                words = z[ch][:].bitcast(F32)[:, u * P : (u + 1) * P]
+                nc.tensor.transpose(turned[:, u * P : (u + 1) * P], words, ident[:])
+            h_bf[ch] = sb("h_bf%d" % ch, [P, CHUNK * PACK], BF16)
+            nc.scalar.activation(
+                h_bf[ch][:].rearrange("p (j u e) -> p j u e", u=2, e=2),
+                turned[:, 0 : 2 * P].bitcast(BF16).rearrange("p (u j e) -> p j u e", u=2, e=2),
+                ACT.Relu,
+            )
+
+        def second_layer(ch):
+            h_q = sb("h_q%d" % ch, [P, CHUNK], U32)
+            h_s = sb("h_s%d" % ch, [P, CHUNK], U8)
+            nc.vector.quantize_mx(out=h_q[:].bitcast(FP8X4), scales=h_s[:], in_=h_bf[ch][:])
+            pieces = [(0, 2, "v"), (2, 4, "s")] if ch == 3 else [(0, 4, "v" if ch == 2 else "s")]
+            for t0, t1, engine in pieces:
+                y_acc = bank("y_acc%d%d" % (ch, t0))
+                width = (t1 - t0) * CHUNK
+                for nt in range(t0, t1):
+                    cols = slice(nt * P, (nt + 1) * P)
+                    nc.tensor.matmul_mx(
+                        out=y_acc[:, (nt - t0) * CHUNK : (nt - t0 + 1) * CHUNK],
+                        lhsT=wd_w[:, cols].bitcast(FP8X4),
+                        lhsT_scale=wd_s[:].bitcast(U8)[:, cols],
+                        rhs=h_q[:].bitcast(FP8X4),
+                        rhs_scale=h_s[:],
+                        start=True,
+                        stop=True,
+                    )
+                y = sb("y%d%d" % (ch, t0), [P, width], F32)
+                rows = out[t0 * P : t1 * P, ch * CHUNK : (ch + 1) * CHUNK].rearrange("(t p) j -> p t j", p=P)
+                if engine == "v":
+                    nc.vector.tensor_copy(y[:], y_acc[:, 0:width])
+                    nc.sync.dma_start(rows, y[:].rearrange("p (t j) -> p t j", j=CHUNK))
+                elif ch == 3:
+                    nc.scalar.activation(y[:], y_acc[:, 0:width], ACT.Copy)
+                    nc.scalar.dma_start(rows, y[:].rearrange("p (t j) -> p t j", j=CHUNK))
+                else:
+                    nc.scalar.activation(y[:], y_acc[:, 0:width], ACT.Copy)
+                    nc.sync.dma_start(rows, y[:].rearrange("p (t j) -> p t j", j=CHUNK))
+
+        def neighbours(ch):
+            for g in range(G):
+                for a in range(PASSES):
+                    neighbour_pass(ch, g, a)
+
+        quantize_w(0)
+        gather_words(0)
+        for ch in (0, 1):
+            for g in range(G):
+                neighbour_pass(ch, g, 0)
+        quantize_w(1)
+        for ch in (0, 1):
+            for g in range(G):
+                neighbour_pass(ch, g, 1)
+        gather_words(1)
+        take_first(0)
+        take_first(1)
+        take_max(0, 1)
+        take_max(1, 1)
+        take_max(0, 2)
+        take_max(1, 2)
+        neighbours(2)
+        quantize_c(0)
+        own_product(0)
+        take_first(2)
+        take_max(2, 1)
+        add_own(0)
+        take_max(2, 2)
+        neighbours(3)
+        own_product(1)
+        quantize_c(1)
+        turn_and_relu(0)
+        take_first(3)
+        add_own(1)
+        take_max(3, 1)
+        own_product(2)
+        turn_and_relu(1)
+        take_max(3, 2)
+        second_layer(0)
+        add_own(2)
+        own_product(3)
+        turn_and_relu(2)
+        second_layer(1)
+        add_own(3)
+        turn_and_relu(3)
+        second_layer(2)
+        second_layer(3)

@@ -25,7 +25,12 @@ PASSES = K // K_PASS
 HALF = 256
 CHUNK = 128
 QUADS = 4
-SHIFT = 4
+SHIFT = 16
+YE = "svs"
+WV = [(0, 1)]
+CV = [(1, 0)]
+RV = [3]
+W1P = 1
 
 
 def tile_list_pnet_none_kernel(
@@ -34,77 +39,71 @@ def tile_list_pnet_none_kernel(
     nc = tc.nc
     with ExitStack() as ctx:
         keep = ctx.enter_context(tc.tile_pool(name="keep", bufs=1))
-        psum = ctx.enter_context(tc.psum_pool(name="psum", bufs=8))
+        psum = ctx.enter_context(tc.psum_pool(name="psum", bufs=1))
 
         def sb(name, shape, dtype):
             return keep.tile(shape, dtype, name=name, align_bytes=64)
 
+        taken = []
+
         def bank(name):
-            return psum.tile([P, 512], F32, name=name, tag="bank")
+            taken.append(name)
+            return psum.tile([P, 512], F32, name=name, tag="bank%d" % (len(taken) % 8))
 
         offsets = keep.tile([P, G * J // 16], U16, name="offsets")
         nc.sync.dma_start(offsets[:], offs)
 
         tab_s = sb("tab_s", [P, T // 4], I32)
         nc.vector.memset(tab_s[:], 0)
-        for q in range(QUADS):
-            nc.sync.dma_start(tab_s[32 * q : 32 * q + 8, :], tab_scales[:, 4 * q : 4 * q + 4, :].bitcast(I32))
+        nc.sync.dma_start(tab_s[0:P:4, :], tab_scales.rearrange("a q t -> (a q) t").bitcast(I32))
 
-        def load_f32(name, src, a, h):
-            raw = sb(name, [P, PACK, HALF], F32)
-            rows = src[a * K_PASS : (a + 1) * K_PASS, h * HALF : (h + 1) * HALF]
-            nc.sync.dma_start(raw[:], rows.rearrange("(p i) x -> p i x", i=PACK))
+        def load_f32(name, src, a, pieces=1):
+            raw = sb(name, [P, PACK, src.shape[1]], F32)
+            rows = src[a * K_PASS : (a + 1) * K_PASS, :].rearrange("(p i) x -> p i x", i=PACK)
+            step = src.shape[1] // pieces
+            for x in range(0, src.shape[1], step):
+                nc.sync.dma_start(raw[:, :, x : x + step], rows[:, :, x : x + step])
             return raw
 
-        picked_s1 = sb("picked_s1", [P, G * J // 4], I32)
+        planes = sb("planes", [P, PASSES, G * J // 4], I32)
         wc_s = sb("wc_s", [P, PASSES, R // 4], I32)
         wd_s = sb("wd_s", [P, N // 4], I32)
         nc.vector.memset(wc_s[:], 0)
         nc.vector.memset(wd_s[:], 0)
-        nc.vector.memset(picked_s1[:], 0)
+        nc.vector.memset(planes[:], 0)
 
-        def load_wc_scales(q):
-            rows = wc_scales[:, 4 * q : 4 * q + 4, :].rearrange("a r n -> r a n")
-            nc.sync.dma_start(wc_s[32 * q : 32 * q + 4, :, :], rows.bitcast(I32))
-
-        def load_wd_scales(q):
-            nc.sync.dma_start(wd_s[32 * q : 32 * q + 4, :], wd_scales[0, 4 * q : 4 * q + 4, :].bitcast(I32))
-
-        w_raw = {}
-        c_raw = {}
-        for h in range(2):
-            w_raw[0, h] = load_f32("w_raw0%d" % h, w, 0, h)
+        w_raw = [load_f32("w_raw0", w, 0)]
         tab_w = sb("tab_w", [P, T], I32)
         nc.sync.dma_start(tab_w[:], tab_words[0].rearrange("p t b -> p (t b)").bitcast(I32))
-        for h in range(2):
-            w_raw[1, h] = load_f32("w_raw1%d" % h, w, 1, h)
-            load_wc_scales(2 * h)
-            load_wc_scales(2 * h + 1)
+        w_raw.append(load_f32("w_raw1", w, 1, W1P))
+        c_raw = [load_f32("c_raw%d" % a, c, a) for a in range(PASSES)]
         wc_w = sb("wc_w", [P, PASSES, R // 2], I32)
         nc.sync.dma_start(wc_w[:], wc_words.rearrange("a p b -> p a b").bitcast(I32))
-        for a in range(PASSES):
-            c_raw[a, 0] = load_f32("c_raw%d0" % a, c, a, 0)
-            load_wd_scales(2 * a)
-            load_wd_scales(2 * a + 1)
+        for q in range(QUADS):
+            rows = wc_scales[:, 4 * q : 4 * q + 4, :].rearrange("a r n -> r a n")
+            nc.sync.dma_start(wc_s[32 * q : 32 * q + 4, :, :], rows.bitcast(I32))
         wd_w = sb("wd_w", [P, N], I32)
         nc.sync.dma_start(wd_w[:], wd_words[0].rearrange("p n b -> p (n b)").bitcast(I32))
-        for a in range(PASSES):
-            c_raw[a, 1] = load_f32("c_raw%d1" % a, c, a, 1)
-
+        for q in range(QUADS):
+            nc.sync.dma_start(wd_s[32 * q : 32 * q + 4, :], wd_scales[0, 4 * q : 4 * q + 4, :].bitcast(I32))
         ident = sb("ident", [P, P], F32)
         make_identity(nc, ident[:])
 
         picked_s0 = sb("picked_s0", [P, G * J], U8)
         nc.vector.tensor_copy(picked_s0[:], tab_s[:].bitcast(U8).indirect(offsets[:]))
-        nc.gpsimd.dma_start(picked_s1[0 : P - SHIFT, :], picked_s0[SHIFT:P, :].bitcast(I32))
-        picked_s = [picked_s0[:], picked_s1[:].bitcast(U8)]
+        for a in range(PASSES):
+            for r in range(4):
+                rows = picked_s0[64 * a + 4 * r : 64 * (a + 1) : 16, :]
+                nc.scalar.dma_start(planes[r:P:32, a, :], rows.bitcast(I32))
+        picked_s = [planes[:, a, :].bitcast(U8) for a in range(PASSES)]
 
-        def round_and_interleave(raw, grouped):
-            nc.scalar.activation(
-                grouped.rearrange("p (y x i) -> p y i x", x=4, i=PACK),
-                raw[:].rearrange("p i (y x) -> p y i x", x=4),
-                ACT.Copy,
-            )
+        def round_and_interleave(raw, h, grouped, on_vector):
+            dst = grouped.rearrange("p (y x i) -> p y i x", x=4, i=PACK)
+            src = raw[:, :, h * HALF : (h + 1) * HALF].rearrange("p i (y x) -> p y i x", x=4)
+            if on_vector:
+                nc.vector.tensor_copy(dst, src)
+            else:
+                nc.scalar.activation(dst, src, ACT.Copy)
 
         w_bf = [sb("w_bf%d" % a, [P, R * PACK], BF16) for a in range(PASSES)]
         w_q = [sb("w_q%d" % a, [P, R], U32) for a in range(PASSES)]
@@ -112,7 +111,7 @@ def tile_list_pnet_none_kernel(
 
         def quantize_w(a):
             for h in range(2):
-                round_and_interleave(w_raw[a, h], w_bf[a][:, h * HALF * PACK : (h + 1) * HALF * PACK])
+                round_and_interleave(w_raw[a], h, w_bf[a][:, h * HALF * PACK : (h + 1) * HALF * PACK], (a, h) in WV)
             nc.vector.quantize_mx(out=w_q[a][:].bitcast(FP8X4), scales=w_s[a][:], in_=w_bf[a][:])
 
         c_q = {}
@@ -123,7 +122,7 @@ def tile_list_pnet_none_kernel(
             c_q[h] = sb("c_q%d" % h, [P, PASSES * HALF], U32)
             c_s[h] = sb("c_s%d" % h, [P, PASSES * HALF], U8)
             for a in range(PASSES):
-                round_and_interleave(c_raw[a, h], c_bf[:, a, :])
+                round_and_interleave(c_raw[a], h, c_bf[:, a, :], (a, h) in CV)
             nc.vector.quantize_mx(
                 out=c_q[h][:].bitcast(FP8X4), scales=c_s[h][:], in_=c_bf[:].rearrange("p a x -> p (a x)")
             )
@@ -211,17 +210,18 @@ def tile_list_pnet_none_kernel(
                 words = z[ch][:].bitcast(F32)[:, u * P : (u + 1) * P]
                 nc.tensor.transpose(turned[:, u * P : (u + 1) * P], words, ident[:])
             h_bf[ch] = sb("h_bf%d" % ch, [P, CHUNK * PACK], BF16)
-            nc.scalar.activation(
-                h_bf[ch][:].rearrange("p (j u e) -> p j u e", u=2, e=2),
-                turned[:, 0 : 2 * P].bitcast(BF16).rearrange("p (u j e) -> p j u e", u=2, e=2),
-                ACT.Relu,
-            )
+            dst = h_bf[ch][:].rearrange("p (j u e) -> p j u e", u=2, e=2)
+            src = turned[:, 0 : 2 * P].bitcast(BF16).rearrange("p (u j e) -> p j u e", u=2, e=2)
+            if ch in RV:
+                nc.vector.tensor_scalar(dst, src, 0.0, None, ALU.max)
+            else:
+                nc.scalar.activation(dst, src, ACT.Relu)
 
         def second_layer(ch):
             h_q = sb("h_q%d" % ch, [P, CHUNK], U32)
             h_s = sb("h_s%d" % ch, [P, CHUNK], U8)
             nc.vector.quantize_mx(out=h_q[:].bitcast(FP8X4), scales=h_s[:], in_=h_bf[ch][:])
-            pieces = [(0, 2, "v"), (2, 4, "s")] if ch == 3 else [(0, 4, "v" if ch == 2 else "s")]
+            pieces = [(0, 2, "v"), (2, 4, "s")] if ch == 3 else [(0, 4, YE[ch])]
             for t0, t1, engine in pieces:
                 y_acc = bank("y_acc%d%d" % (ch, t0))
                 width = (t1 - t0) * CHUNK
@@ -263,35 +263,35 @@ def tile_list_pnet_none_kernel(
             for g in range(G):
                 neighbour_pass(ch, g, 1)
         gather_words(1)
+        quantize_c(0)
         take_first(0)
-        take_first(1)
         take_max(0, 1)
+        take_first(1)
         take_max(1, 1)
+        neighbours(2)
+        own_product(1)
+        own_product(0)
         take_max(0, 2)
         take_max(1, 2)
-        neighbours(2)
-        quantize_c(0)
-        own_product(0)
         take_first(2)
+        neighbours(3)
         take_max(2, 1)
         add_own(0)
         take_max(2, 2)
-        neighbours(3)
-        own_product(1)
-        quantize_c(1)
         turn_and_relu(0)
+        quantize_c(1)
+        own_product(2)
         take_first(3)
         add_own(1)
+        own_product(3)
         take_max(3, 1)
-        own_product(2)
+        add_own(2)
+        turn_and_relu(2)
+        second_layer(0)
         turn_and_relu(1)
         take_max(3, 2)
-        second_layer(0)
-        add_own(2)
-        own_product(3)
-        turn_and_relu(2)
-        second_layer(1)
+        second_layer(2)
         add_own(3)
         turn_and_relu(3)
-        second_layer(2)
+        second_layer(1)
         second_layer(3)

@@ -4,8 +4,8 @@ import concourse.mybir as mybir
 from concourse.masks import make_identity
 
 K, R, N, T, J = 1024, 512, 512, 2048, 512
-G = 3
-FLOPS = 2 * K * R * J * (G + 1) + 2 * R * N * J
+NEIGHBOURS = 3
+FLOPS = 2 * K * R * J * (NEIGHBOURS + 1) + 2 * R * N * J
 
 F32 = mybir.dt.float32
 BF16 = mybir.dt.bfloat16
@@ -22,15 +22,22 @@ P = 128
 PACK = 4
 K_PASS = P * PACK
 PASSES = K // K_PASS
+BLOCKS = K_PASS // 32
+QUADRANT = 32
+SHIFT = 16
+LIST_ROWS = 16
 HALF = 256
 CHUNK = 128
-QUADS = 4
-SHIFT = 16
-YE = "svs"
-WV = [(0, 1)]
-CV = [(1, 0)]
-RV = [3]
-W1P = 1
+LAST = J // CHUNK - 1
+
+W_ON_VECTOR = (0, 1)
+C_ON_VECTOR = (1, 0)
+RELU_ON_VECTOR = (2, 3)
+
+SUM_BANK = ((4, 1, 4), (7, 5, 3), (0, 6, 7), (5, 2, 3))
+OWN_BANK = (1, 1, 6, 7)
+TURNED_BANK = (0, 5, 6, 0)
+Y_BANK = ((3,), (2,), (7,), (7, 6))
 
 
 def tile_list_pnet_none_kernel(
@@ -41,194 +48,202 @@ def tile_list_pnet_none_kernel(
         keep = ctx.enter_context(tc.tile_pool(name="keep", bufs=1))
         psum = ctx.enter_context(tc.psum_pool(name="psum", bufs=1))
 
-        def sb(name, shape, dtype):
-            return keep.tile(shape, dtype, name=name, align_bytes=64)
+        def sbuf(name, shape, dtype, reuse=None):
+            return keep.tile(shape, dtype, name=name, tag=reuse or name, align_bytes=64)
 
-        taken = []
+        def bank(name, index):
+            return psum.tile([P, 512], F32, name=name, tag="bank%d" % index)
 
-        def bank(name):
-            taken.append(name)
-            return psum.tile([P, 512], F32, name=name, tag="bank%d" % (len(taken) % 8))
-
-        offsets = keep.tile([P, G * J // 16], U16, name="offsets")
+        offsets = keep.tile([P, NEIGHBOURS * J // LIST_ROWS], U16, name="offsets")
         nc.sync.dma_start(offsets[:], offs)
 
-        tab_s = sb("tab_s", [P, T // 4], I32)
-        nc.vector.memset(tab_s[:], 0)
-        nc.sync.dma_start(tab_s[0:P:4, :], tab_scales.rearrange("a q t -> (a q) t").bitcast(I32))
-
-        def load_f32(name, src, a, pieces=1):
-            raw = sb(name, [P, PACK, src.shape[1]], F32)
-            rows = src[a * K_PASS : (a + 1) * K_PASS, :].rearrange("(p i) x -> p i x", i=PACK)
-            step = src.shape[1] // pieces
-            for x in range(0, src.shape[1], step):
-                nc.sync.dma_start(raw[:, :, x : x + step], rows[:, :, x : x + step])
-            return raw
-
-        planes = sb("planes", [P, PASSES, G * J // 4], I32)
-        wc_s = sb("wc_s", [P, PASSES, R // 4], I32)
-        wd_s = sb("wd_s", [P, N // 4], I32)
-        nc.vector.memset(wc_s[:], 0)
+        tab_s = sbuf("tab_s", [P, T // 4], I32)
+        wd_s = sbuf("wd_s", [P, N // 4], I32)
         nc.vector.memset(wd_s[:], 0)
-        nc.vector.memset(planes[:], 0)
+        nc.vector.memset(tab_s[:], 0)
 
-        w_raw = [load_f32("w_raw0", w, 0)]
-        tab_w = sb("tab_w", [P, T], I32)
+        def load_wd_scales(quad):
+            rows = wd_scales[0, 4 * quad : 4 * quad + 4, :]
+            nc.sync.dma_start(wd_s[QUADRANT * quad : QUADRANT * quad + 4, :], rows.bitcast(I32))
+
+        load_wd_scales(0)
+        for r in range(4):
+            rows = tab_scales[:, r:BLOCKS:4, :].rearrange("a quad t -> quad a t")
+            queue = nc.sync if r < 2 else nc.scalar
+            queue.dma_start(tab_s[r:P:SHIFT, :], rows.bitcast(I32))
+
+        moved_s = sbuf("moved_s", [P, NEIGHBOURS * J // 4], I32)
+        wc_s = sbuf("wc_s", [P, PASSES, R // 4], I32)
+        warm = sbuf("warm", [P, 2], F32)
+        nc.vector.memset(warm[:, 0:1], 0.0)
+        nc.scalar.activation(warm[:, 1:2], warm[:, 0:1], ACT.Copy)
+        nc.vector.memset(wc_s[:], 0)
+        nc.vector.memset(moved_s[:], 0)
+
+        def rows_by_partition(src, a, cols):
+            return src[a * K_PASS : (a + 1) * K_PASS, cols].rearrange("(p i) x -> p i x", i=PACK)
+
+        w_raw = [sbuf("w_raw%d" % a, [P, PACK, R], F32) for a in range(PASSES)]
+        tab_w = sbuf("tab_w", [P, T], I32)
+        nc.sync.dma_start(w_raw[0][:], rows_by_partition(w, 0, slice(0, R)))
         nc.sync.dma_start(tab_w[:], tab_words[0].rearrange("p t b -> p (t b)").bitcast(I32))
-        w_raw.append(load_f32("w_raw1", w, 1, W1P))
-        c_raw = [load_f32("c_raw%d" % a, c, a) for a in range(PASSES)]
-        wc_w = sb("wc_w", [P, PASSES, R // 2], I32)
+        nc.sync.dma_start(w_raw[1][:], rows_by_partition(w, 1, slice(0, R)))
+
+        ident = sbuf("ident", [P, P], F32)
+        nc.vector.memset(ident[:], 0.0)
+        make_identity(nc, ident[:], nomemset=True)
+
+        picked_s = sbuf("picked_s", [P, NEIGHBOURS * J], U8)
+        nc.vector.tensor_copy(picked_s[:], tab_s[:].bitcast(U8).indirect(offsets[:]))
+        nc.sync.dma_start(moved_s[0 : P - SHIFT, :], picked_s[SHIFT:P, :].bitcast(I32))
+        tab_planes = [picked_s[:], moved_s[:].bitcast(U8)]
+
+        c_raw = [sbuf("c_raw%d" % a, [P, PACK, J], F32) for a in range(PASSES)]
+
+        def load_c(half):
+            cols = slice(half * HALF, (half + 1) * HALF)
+            for a in range(PASSES):
+                nc.sync.dma_start(c_raw[a][:, :, cols], rows_by_partition(c, a, cols))
+
+        load_c(0)
+        wc_w = sbuf("wc_w", [P, PASSES, R // 2], I32)
         nc.sync.dma_start(wc_w[:], wc_words.rearrange("a p b -> p a b").bitcast(I32))
-        for q in range(QUADS):
-            rows = wc_scales[:, 4 * q : 4 * q + 4, :].rearrange("a r n -> r a n")
-            nc.sync.dma_start(wc_s[32 * q : 32 * q + 4, :, :], rows.bitcast(I32))
-        wd_w = sb("wd_w", [P, N], I32)
+        for quad in range(P // QUADRANT):
+            rows = wc_scales[:, 4 * quad : 4 * quad + 4, :].rearrange("a q r -> q a r")
+            nc.gpsimd.dma_start(wc_s[QUADRANT * quad : QUADRANT * quad + 4, :, :], rows.bitcast(I32))
+        load_c(1)
+        wd_w = sbuf("wd_w", [P, N], I32)
         nc.sync.dma_start(wd_w[:], wd_words[0].rearrange("p n b -> p (n b)").bitcast(I32))
-        for q in range(QUADS):
-            nc.sync.dma_start(wd_s[32 * q : 32 * q + 4, :], wd_scales[0, 4 * q : 4 * q + 4, :].bitcast(I32))
-        ident = sb("ident", [P, P], F32)
-        make_identity(nc, ident[:])
+        for quad in range(1, P // QUADRANT):
+            load_wd_scales(quad)
 
-        picked_s0 = sb("picked_s0", [P, G * J], U8)
-        nc.vector.tensor_copy(picked_s0[:], tab_s[:].bitcast(U8).indirect(offsets[:]))
-        for a in range(PASSES):
-            for r in range(4):
-                rows = picked_s0[64 * a + 4 * r : 64 * (a + 1) : 16, :]
-                nc.scalar.dma_start(planes[r:P:32, a, :], rows.bitcast(I32))
-        picked_s = [planes[:, a, :].bitcast(U8) for a in range(PASSES)]
-
-        def round_and_interleave(raw, h, grouped, on_vector):
+        def round_and_interleave(raw, half, grouped, on_vector):
             dst = grouped.rearrange("p (y x i) -> p y i x", x=4, i=PACK)
-            src = raw[:, :, h * HALF : (h + 1) * HALF].rearrange("p i (y x) -> p y i x", x=4)
+            src = raw[:, :, half * HALF : (half + 1) * HALF].rearrange("p i (y x) -> p y i x", x=4)
             if on_vector:
                 nc.vector.tensor_copy(dst, src)
             else:
                 nc.scalar.activation(dst, src, ACT.Copy)
 
-        w_bf = [sb("w_bf%d" % a, [P, R * PACK], BF16) for a in range(PASSES)]
-        w_q = [sb("w_q%d" % a, [P, R], U32) for a in range(PASSES)]
-        w_s = [sb("w_s%d" % a, [P, R], U8) for a in range(PASSES)]
+        w_bf = [sbuf("w_bf%d" % a, [P, R * PACK], BF16) for a in range(PASSES)]
+        w_q = [sbuf("w_q%d" % a, [P, R], U32) for a in range(PASSES)]
+        w_s = [sbuf("w_s%d" % a, [P, R], U8) for a in range(PASSES)]
 
         def quantize_w(a):
-            for h in range(2):
-                round_and_interleave(w_raw[a], h, w_bf[a][:, h * HALF * PACK : (h + 1) * HALF * PACK], (a, h) in WV)
+            for half in range(R // HALF):
+                grouped = w_bf[a][:, half * HALF * PACK : (half + 1) * HALF * PACK]
+                round_and_interleave(w_raw[a], half, grouped, (a, half) == W_ON_VECTOR)
             nc.vector.quantize_mx(out=w_q[a][:].bitcast(FP8X4), scales=w_s[a][:], in_=w_bf[a][:])
 
-        c_q = {}
-        c_s = {}
+        c_q, c_s = {}, {}
 
-        def quantize_c(h):
-            c_bf = sb("c_bf%d" % h, [P, PASSES, HALF * PACK], BF16)
-            c_q[h] = sb("c_q%d" % h, [P, PASSES * HALF], U32)
-            c_s[h] = sb("c_s%d" % h, [P, PASSES * HALF], U8)
+        def quantize_c(half):
+            c_bf = sbuf("c_bf%d" % half, [P, PASSES, HALF * PACK], BF16)
+            c_q[half] = sbuf("c_q%d" % half, [P, PASSES * HALF], U32)
+            c_s[half] = sbuf("c_s%d" % half, [P, PASSES * HALF], U8)
             for a in range(PASSES):
-                round_and_interleave(c_raw[a], h, c_bf[:, a, :], (a, h) in CV)
+                round_and_interleave(c_raw[a], half, c_bf[:, a, :], (a, half) == C_ON_VECTOR)
             nc.vector.quantize_mx(
-                out=c_q[h][:].bitcast(FP8X4), scales=c_s[h][:], in_=c_bf[:].rearrange("p a x -> p (a x)")
+                out=c_q[half][:].bitcast(FP8X4), scales=c_s[half][:], in_=c_bf[:].rearrange("p a x -> p (a x)")
             )
 
-        parted = {}
+        pairs, parted = {}, {}
 
-        def gather_words(h):
-            pairs = {}
-            for g in range(G + 1):
-                if g < G:
-                    pairs[g] = sb("pairs%d%d" % (g, h), [P, HALF], U32)
-                    col = (g * J + h * HALF) // 16
-                    nc.vector.tensor_copy(
-                        pairs[g][:], tab_w[:].bitcast(U32).indirect(offsets[:, col : col + HALF // 16])
-                    )
-                if g > 0:
-                    parted[g - 1, h] = sb("parted%d%d" % (g - 1, h), [P, PASSES, 2 * HALF], U8)
-                    nc.vector.tensor_copy(
-                        parted[g - 1, h][:].bitcast(U16),
-                        pairs[g - 1][:].bitcast(U16).rearrange("p (j d) -> p d j", d=PASSES),
-                    )
+        def gather_words(g, half, reuse=None):
+            pairs[g, half] = sbuf("pairs%d%d" % (g, half), [P, HALF], U32, reuse)
+            col = (g * J + half * HALF) // LIST_ROWS
+            picks = offsets[:, col : col + HALF // LIST_ROWS]
+            nc.vector.tensor_copy(pairs[g, half][:], tab_w[:].bitcast(U32).indirect(picks))
+
+        def part_words(g, half):
+            parted[g, half] = sbuf("parted%d%d" % (g, half), [P, PASSES, 2 * HALF], U8)
+            nc.vector.tensor_copy(
+                parted[g, half][:].bitcast(U16),
+                pairs[g, half][:].bitcast(U16).rearrange("p (j a) -> p a j", a=PASSES),
+            )
 
         sums = {}
 
         def neighbour_pass(ch, g, a):
-            h, j0 = divmod(ch * CHUNK, HALF)
+            half, j0 = divmod(ch * CHUNK, HALF)
             if a == 0:
-                sums[ch, g] = bank("sum%d%d" % (ch, g))
-            s0 = g * J + ch * CHUNK
+                sums[ch, g] = bank("sum%d%d" % (ch, g), SUM_BANK[ch][g])
+            m0 = g * J + ch * CHUNK
             nc.tensor.matmul_mx(
                 out=sums[ch, g][:],
-                lhsT=parted[g, h][:, a, 2 * j0 : 2 * (j0 + CHUNK)].bitcast(FP4X4),
-                lhsT_scale=picked_s[a][:, s0 : s0 + CHUNK],
+                lhsT=parted[g, half][:, a, 2 * j0 : 2 * (j0 + CHUNK)].bitcast(FP4X4),
+                lhsT_scale=tab_planes[a][:, m0 : m0 + CHUNK],
                 rhs=w_q[a][:].bitcast(FP8X4),
                 rhs_scale=w_s[a][:],
                 start=(a == 0),
                 stop=(a == PASSES - 1),
             )
 
-        def by_word(acc):
+        def neighbour_sum(ch, g):
+            for a in range(PASSES):
+                neighbour_pass(ch, g, a)
+
+        def psum_view(acc):
             return acc[:].rearrange("j (p u e) -> j u p e", u=2, e=2)
 
-        def split(flat):
+        def sbuf_view(flat):
             return flat[:].rearrange("j (u p e) -> j u p e", u=2, e=2)
 
-        best = {}
+        best, own, z, h_bf = {}, {}, {}, {}
 
         def take_first(ch):
-            best[ch] = sb("first%d" % ch, [P, R], F32)
-            nc.scalar.activation(split(best[ch]), by_word(sums[ch, 0]), ACT.Copy)
+            best[ch] = sbuf("first%d" % ch, [P, R], F32)
+            nc.scalar.activation(sbuf_view(best[ch]), psum_view(sums[ch, 0]), ACT.Copy)
 
         def take_max(ch, g):
-            more = sb("max%d%d" % (ch, g), [P, R], F32)
-            nc.vector.tensor_tensor(split(more), by_word(sums[ch, g]), split(best[ch]), ALU.max)
-            best[ch] = more
+            larger = sbuf("max%d%d" % (ch, g), [P, R], F32)
+            nc.vector.tensor_tensor(sbuf_view(larger), psum_view(sums[ch, g]), sbuf_view(best[ch]), ALU.max)
+            best[ch] = larger
 
-        own = {}
-
-        def own_product(ch):
-            h, j0 = divmod(ch * CHUNK, HALF)
-            own[ch] = bank("own%d" % ch)
+        def own_sum(ch):
+            half, j0 = divmod(ch * CHUNK, HALF)
+            own[ch] = bank("own%d" % ch, OWN_BANK[ch])
             for a in range(PASSES):
                 cols = slice(a * HALF + j0, a * HALF + j0 + CHUNK)
                 nc.tensor.matmul_mx(
                     out=own[ch][:],
-                    lhsT=c_q[h][:, cols].bitcast(FP8X4),
-                    lhsT_scale=c_s[h][:, cols],
+                    lhsT=c_q[half][:, cols].bitcast(FP8X4),
+                    lhsT_scale=c_s[half][:, cols],
                     rhs=wc_w[:, a, :].bitcast(U8).bitcast(FP4X4),
                     rhs_scale=wc_s[:, a, :].bitcast(U8),
                     start=(a == 0),
                     stop=(a == PASSES - 1),
                 )
 
-        z = {}
-
         def add_own(ch):
-            z[ch] = sb("z%d" % ch, [P, R], BF16)
-            nc.vector.tensor_tensor(split(z[ch]), by_word(own[ch]), split(best[ch]), ALU.add)
-
-        h_bf = {}
+            z[ch] = sbuf("z%d" % ch, [P, R], BF16)
+            nc.vector.tensor_tensor(sbuf_view(z[ch]), psum_view(own[ch]), sbuf_view(best[ch]), ALU.add)
 
         def turn_and_relu(ch):
-            turned = bank("turned%d" % ch)
+            h_bf[ch] = sbuf("h_bf%d" % ch, [P, CHUNK * PACK], BF16)
+            turned = bank("turned%d" % ch, TURNED_BANK[ch])
             for u in range(2):
                 words = z[ch][:].bitcast(F32)[:, u * P : (u + 1) * P]
                 nc.tensor.transpose(turned[:, u * P : (u + 1) * P], words, ident[:])
-            h_bf[ch] = sb("h_bf%d" % ch, [P, CHUNK * PACK], BF16)
             dst = h_bf[ch][:].rearrange("p (j u e) -> p j u e", u=2, e=2)
             src = turned[:, 0 : 2 * P].bitcast(BF16).rearrange("p (u j e) -> p j u e", u=2, e=2)
-            if ch in RV:
+            if ch in RELU_ON_VECTOR:
                 nc.vector.tensor_scalar(dst, src, 0.0, None, ALU.max)
             else:
                 nc.scalar.activation(dst, src, ACT.Relu)
 
         def second_layer(ch):
-            h_q = sb("h_q%d" % ch, [P, CHUNK], U32)
-            h_s = sb("h_s%d" % ch, [P, CHUNK], U8)
+            h_q = sbuf("h_q%d" % ch, [P, CHUNK], U32)
+            h_s = sbuf("h_s%d" % ch, [P, CHUNK], U8)
             nc.vector.quantize_mx(out=h_q[:].bitcast(FP8X4), scales=h_s[:], in_=h_bf[ch][:])
-            pieces = [(0, 2, "v"), (2, 4, "s")] if ch == 3 else [(0, 4, YE[ch])]
-            for t0, t1, engine in pieces:
-                y_acc = bank("y_acc%d%d" % (ch, t0))
-                width = (t1 - t0) * CHUNK
-                for nt in range(t0, t1):
-                    cols = slice(nt * P, (nt + 1) * P)
+            tiles = N // P // len(Y_BANK[ch])
+            for piece, index in enumerate(Y_BANK[ch]):
+                t0 = piece * tiles
+                y_acc = bank("y_acc%d%d" % (ch, t0), index)
+                for t in range(tiles):
+                    cols = slice((t0 + t) * P, (t0 + t + 1) * P)
                     nc.tensor.matmul_mx(
-                        out=y_acc[:, (nt - t0) * CHUNK : (nt - t0 + 1) * CHUNK],
+                        out=y_acc[:, t * CHUNK : (t + 1) * CHUNK],
                         lhsT=wd_w[:, cols].bitcast(FP8X4),
                         lhsT_scale=wd_s[:].bitcast(U8)[:, cols],
                         rhs=h_q[:].bitcast(FP8X4),
@@ -236,62 +251,66 @@ def tile_list_pnet_none_kernel(
                         start=True,
                         stop=True,
                     )
-                y = sb("y%d%d" % (ch, t0), [P, width], F32)
-                rows = out[t0 * P : t1 * P, ch * CHUNK : (ch + 1) * CHUNK].rearrange("(t p) j -> p t j", p=P)
-                if engine == "v":
-                    nc.vector.tensor_copy(y[:], y_acc[:, 0:width])
-                    nc.sync.dma_start(rows, y[:].rearrange("p (t j) -> p t j", j=CHUNK))
-                elif ch == 3:
-                    nc.scalar.activation(y[:], y_acc[:, 0:width], ACT.Copy)
-                    nc.scalar.dma_start(rows, y[:].rearrange("p (t j) -> p t j", j=CHUNK))
+                y = sbuf("y%d%d" % (ch, t0), [P, tiles * CHUNK], F32)
+                rows = out[t0 * P : (t0 + tiles) * P, ch * CHUNK : (ch + 1) * CHUNK].rearrange("(t p) j -> p t j", p=P)
+                if ch == LAST and piece == 0:
+                    nc.vector.tensor_copy(y[:], y_acc[:, 0 : tiles * CHUNK])
                 else:
-                    nc.scalar.activation(y[:], y_acc[:, 0:width], ACT.Copy)
-                    nc.sync.dma_start(rows, y[:].rearrange("p (t j) -> p t j", j=CHUNK))
-
-        def neighbours(ch):
-            for g in range(G):
-                for a in range(PASSES):
-                    neighbour_pass(ch, g, a)
+                    nc.scalar.activation(y[:], y_acc[:, 0 : tiles * CHUNK], ACT.Copy)
+                queue = nc.scalar if ch == LAST and piece == 1 else nc.sync
+                queue.dma_start(rows, y[:].rearrange("p (t j) -> p t j", j=CHUNK))
 
         quantize_w(0)
-        gather_words(0)
+        for g in range(NEIGHBOURS):
+            gather_words(g, 0)
+        for g in range(NEIGHBOURS):
+            part_words(g, 0)
         for ch in (0, 1):
-            for g in range(G):
+            for g in range(NEIGHBOURS):
                 neighbour_pass(ch, g, 0)
         quantize_w(1)
+        for g in (0, 1):
+            gather_words(g, 1)
         for ch in (0, 1):
-            for g in range(G):
+            for g in range(NEIGHBOURS):
                 neighbour_pass(ch, g, 1)
-        gather_words(1)
+        for g in (0, 1):
+            part_words(g, 1)
+        gather_words(2, 1, "w_bf1")
+        part_words(2, 1)
+
         quantize_c(0)
-        take_first(0)
-        take_max(0, 1)
-        take_first(1)
-        take_max(1, 1)
-        neighbours(2)
-        own_product(1)
-        own_product(0)
-        take_max(0, 2)
-        take_max(1, 2)
-        take_first(2)
-        neighbours(3)
-        take_max(2, 1)
-        add_own(0)
-        take_max(2, 2)
-        turn_and_relu(0)
+        for ch in (0, 1):
+            take_first(ch)
+        for g in (1, 2):
+            for ch in (0, 1):
+                take_max(ch, g)
+        for ch in (2, 3):
+            for g in (0, 1):
+                neighbour_sum(ch, g)
+        for ch in (0, 1):
+            own_sum(ch)
         quantize_c(1)
-        own_product(2)
+
+        neighbour_sum(2, 2)
+        take_first(2)
+        for ch in (0, 1):
+            add_own(ch)
+        take_max(2, 1)
+        for ch in (2, 3):
+            own_sum(ch)
+        neighbour_sum(3, 2)
         take_first(3)
-        add_own(1)
-        own_product(3)
+        for ch in (0, 1):
+            turn_and_relu(ch)
+        take_max(2, 2)
         take_max(3, 1)
         add_own(2)
-        turn_and_relu(2)
-        second_layer(0)
-        turn_and_relu(1)
+        for ch in (0, 1):
+            second_layer(ch)
         take_max(3, 2)
-        second_layer(2)
         add_own(3)
-        turn_and_relu(3)
-        second_layer(1)
-        second_layer(3)
+        for ch in (2, 3):
+            turn_and_relu(ch)
+        for ch in (2, 3):
+            second_layer(ch)

@@ -30,14 +30,14 @@ HALF = 256
 CHUNK = 128
 LAST = J // CHUNK - 1
 
-W_ON_VECTOR = (0, 1)
-C_ON_VECTOR = (1, 0)
-RELU_ON_VECTOR = (2, 3)
-
-SUM_BANK = ((4, 1, 4), (7, 5, 3), (0, 6, 7), (5, 2, 3))
-OWN_BANK = (1, 1, 6, 7)
-TURNED_BANK = (0, 5, 6, 0)
-Y_BANK = ((3,), (2,), (7,), (7, 6))
+RELU_ON_VECTOR = (3,)
+ADD_ON_TENSOR = (3,)
+FINAL = 3
+GROUPS = ((0, 1), (2,), (3,))
+C_ENGINE = ("SS", "SS")
+C_BF_TAG = ("c_bf0", "c_bf1")
+Y_ON_VECTOR = ((3, 0), (0, 0))
+BANKS = 8
 
 
 def tile_list_pnet_none_kernel(
@@ -51,128 +51,140 @@ def tile_list_pnet_none_kernel(
         def sbuf(name, shape, dtype, reuse=None):
             return keep.tile(shape, dtype, name=name, tag=reuse or name, align_bytes=64)
 
-        def bank(name, index):
-            return psum.tile([P, 512], F32, name=name, tag="bank%d" % index)
+        taken = []
+
+        def bank(name):
+            taken.append(name)
+            return psum.tile([P, 512], F32, name=name, tag="bank%d" % ((len(taken) - 1) % BANKS))
 
         offsets = keep.tile([P, NEIGHBOURS * J // LIST_ROWS], U16, name="offsets")
         nc.sync.dma_start(offsets[:], offs)
 
         tab_s = sbuf("tab_s", [P, T // 4], I32)
-        wd_s = sbuf("wd_s", [P, N // 4], I32)
-        nc.vector.memset(wd_s[:], 0)
-        nc.vector.memset(tab_s[:], 0)
-
-        def load_wd_scales(quad):
-            rows = wd_scales[0, 4 * quad : 4 * quad + 4, :]
-            nc.sync.dma_start(wd_s[QUADRANT * quad : QUADRANT * quad + 4, :], rows.bitcast(I32))
-
-        load_wd_scales(0)
+        nc.vector.memset(tab_s[:, 0 : T // 8], 0)
+        nc.gpsimd.memset(tab_s[:, T // 8 : T // 4], 0)
         for r in range(4):
             rows = tab_scales[:, r:BLOCKS:4, :].rearrange("a quad t -> quad a t")
-            queue = nc.sync if r < 2 else nc.scalar
-            queue.dma_start(tab_s[r:P:SHIFT, :], rows.bitcast(I32))
+            nc.sync.dma_start(tab_s[r:P:SHIFT, :], rows.bitcast(I32))
 
-        moved_s = sbuf("moved_s", [P, NEIGHBOURS * J // 4], I32)
-        wc_s = sbuf("wc_s", [P, PASSES, R // 4], I32)
-        warm = sbuf("warm", [P, 2], F32)
-        nc.vector.memset(warm[:, 0:1], 0.0)
-        nc.scalar.activation(warm[:, 1:2], warm[:, 0:1], ACT.Copy)
-        nc.vector.memset(wc_s[:], 0)
-        nc.vector.memset(moved_s[:], 0)
+        def load_raw(name, src, a, half):
+            raw = sbuf("%s_raw%d%d" % (name, a, half), [P, PACK, HALF], F32)
+            rows = src[a * K_PASS : (a + 1) * K_PASS, half * HALF : (half + 1) * HALF]
+            nc.sync.dma_start(raw[:], rows.rearrange("(p i) x -> p i x", i=PACK))
+            return raw
 
-        def rows_by_partition(src, a, cols):
-            return src[a * K_PASS : (a + 1) * K_PASS, cols].rearrange("(p i) x -> p i x", i=PACK)
-
-        w_raw = [sbuf("w_raw%d" % a, [P, PACK, R], F32) for a in range(PASSES)]
+        w_raw = {}
+        for half in range(2):
+            w_raw[0, half] = load_raw("w", w, 0, half)
         tab_w = sbuf("tab_w", [P, T], I32)
-        nc.sync.dma_start(w_raw[0][:], rows_by_partition(w, 0, slice(0, R)))
         nc.sync.dma_start(tab_w[:], tab_words[0].rearrange("p t b -> p (t b)").bitcast(I32))
-        nc.sync.dma_start(w_raw[1][:], rows_by_partition(w, 1, slice(0, R)))
+        for half in range(2):
+            w_raw[1, half] = load_raw("w", w, 1, half)
 
+        wc_s = sbuf("wc_s", [P, PASSES, R // 4], I32)
+        wd_s = sbuf("wd_s", [P, N // 4], I32)
         ident = sbuf("ident", [P, P], F32)
         nc.vector.memset(ident[:], 0.0)
         make_identity(nc, ident[:], nomemset=True)
+        nc.gpsimd.memset(wc_s[:], 0)
+        nc.gpsimd.memset(wd_s[:], 0)
 
-        picked_s = sbuf("picked_s", [P, NEIGHBOURS * J], U8)
-        nc.vector.tensor_copy(picked_s[:], tab_s[:].bitcast(U8).indirect(offsets[:]))
-        nc.sync.dma_start(moved_s[0 : P - SHIFT, :], picked_s[SHIFT:P, :].bitcast(I32))
-        tab_planes = [picked_s[:], moved_s[:].bitcast(U8)]
+        planes = {}
 
-        c_raw = [sbuf("c_raw%d" % a, [P, PACK, J], F32) for a in range(PASSES)]
+        def gather_scales(g0, g1, reuse=None):
+            width = (g1 - g0) * J
+            moved = sbuf("moved_s%d" % g0, [P, width // 4], I32)
+            nc.vector.memset(moved[:], 0)
+            picked = sbuf("picked_s%d" % g0, [P, width], U8, reuse)
+            picks = offsets[:, g0 * J // LIST_ROWS : g1 * J // LIST_ROWS]
+            nc.vector.tensor_copy(picked[:], tab_s[:].bitcast(U8).indirect(picks))
+            for g in range(g0, g1):
+                cols = slice((g - g0) * J, (g - g0 + 1) * J)
+                planes[g] = [picked[:, cols], moved[:].bitcast(U8)[:, cols]]
 
-        def load_c(half):
-            cols = slice(half * HALF, (half + 1) * HALF)
-            for a in range(PASSES):
-                nc.sync.dma_start(c_raw[a][:, :, cols], rows_by_partition(c, a, cols))
+            return moved, picked
 
-        load_c(0)
+        moved, picked = gather_scales(0, NEIGHBOURS)
+        nc.sync.dma_start(moved[0 : P - SHIFT, :], picked[SHIFT:P, :].bitcast(I32))
+
+        c_raw = {(a, 0): load_raw("c", c, a, 0) for a in range(PASSES)}
         wc_w = sbuf("wc_w", [P, PASSES, R // 2], I32)
         nc.sync.dma_start(wc_w[:], wc_words.rearrange("a p b -> p a b").bitcast(I32))
         for quad in range(P // QUADRANT):
             rows = wc_scales[:, 4 * quad : 4 * quad + 4, :].rearrange("a q r -> q a r")
-            nc.gpsimd.dma_start(wc_s[QUADRANT * quad : QUADRANT * quad + 4, :, :], rows.bitcast(I32))
-        load_c(1)
+            nc.sync.dma_start(wc_s[QUADRANT * quad : QUADRANT * quad + 4, :, :], rows.bitcast(I32))
+        for a in range(PASSES):
+            c_raw[a, 1] = load_raw("c", c, a, 1)
         wd_w = sbuf("wd_w", [P, N], I32)
         nc.sync.dma_start(wd_w[:], wd_words[0].rearrange("p n b -> p (n b)").bitcast(I32))
-        for quad in range(1, P // QUADRANT):
-            load_wd_scales(quad)
+        for quad in range(P // QUADRANT):
+            rows = wd_scales[0, 4 * quad : 4 * quad + 4, :]
+            nc.sync.dma_start(wd_s[QUADRANT * quad : QUADRANT * quad + 4, :], rows.bitcast(I32))
 
-        def round_and_interleave(raw, half, grouped, on_vector):
+        def round_and_interleave(raw, grouped, engine="S"):
+            if engine == "G":
+                dst = grouped.rearrange("p (x i) -> p x i", i=PACK)
+                nc.gpsimd.tensor_scalar(dst, raw[:].rearrange("p i x -> p x i"), 1.0, 0.0, ALU.mult, ALU.add)
+                return
             dst = grouped.rearrange("p (y x i) -> p y i x", x=4, i=PACK)
-            src = raw[:, :, half * HALF : (half + 1) * HALF].rearrange("p i (y x) -> p y i x", x=4)
-            if on_vector:
+            src = raw[:].rearrange("p i (y x) -> p y i x", x=4)
+            if engine == "V":
                 nc.vector.tensor_copy(dst, src)
             else:
                 nc.scalar.activation(dst, src, ACT.Copy)
 
-        w_bf = [sbuf("w_bf%d" % a, [P, R * PACK], BF16) for a in range(PASSES)]
         w_q = [sbuf("w_q%d" % a, [P, R], U32) for a in range(PASSES)]
         w_s = [sbuf("w_s%d" % a, [P, R], U8) for a in range(PASSES)]
+        w_bf = [sbuf("w_bf%d" % a, [P, 2, HALF * PACK], BF16) for a in range(PASSES)]
+
+        def round_w(a):
+            for half in range(2):
+                round_and_interleave(w_raw[a, half], w_bf[a][:, half, :])
 
         def quantize_w(a):
-            for half in range(R // HALF):
-                grouped = w_bf[a][:, half * HALF * PACK : (half + 1) * HALF * PACK]
-                round_and_interleave(w_raw[a], half, grouped, (a, half) == W_ON_VECTOR)
-            nc.vector.quantize_mx(out=w_q[a][:].bitcast(FP8X4), scales=w_s[a][:], in_=w_bf[a][:])
+            nc.vector.quantize_mx(
+                out=w_q[a][:].bitcast(FP8X4), scales=w_s[a][:], in_=w_bf[a][:].rearrange("p h x -> p (h x)")
+            )
 
-        c_q, c_s = {}, {}
+        c_bf = {}
+        c_q = [sbuf("c_q%d" % half, [P, PASSES * HALF], U32) for half in range(2)]
+        c_s = [sbuf("c_s%d" % half, [P, PASSES * HALF], U8) for half in range(2)]
+
+        def round_c(a, half):
+            if a == 0:
+                c_bf[half] = sbuf("c_bf%d" % half, [P, PASSES, HALF * PACK], BF16, C_BF_TAG[half])
+            round_and_interleave(c_raw[a, half], c_bf[half][:, a, :], C_ENGINE[half][a])
 
         def quantize_c(half):
-            c_bf = sbuf("c_bf%d" % half, [P, PASSES, HALF * PACK], BF16)
-            c_q[half] = sbuf("c_q%d" % half, [P, PASSES * HALF], U32)
-            c_s[half] = sbuf("c_s%d" % half, [P, PASSES * HALF], U8)
-            for a in range(PASSES):
-                round_and_interleave(c_raw[a], half, c_bf[:, a, :], (a, half) == C_ON_VECTOR)
             nc.vector.quantize_mx(
-                out=c_q[half][:].bitcast(FP8X4), scales=c_s[half][:], in_=c_bf[:].rearrange("p a x -> p (a x)")
+                out=c_q[half][:].bitcast(FP8X4), scales=c_s[half][:], in_=c_bf[half][:].rearrange("p a x -> p (a x)")
             )
 
         pairs, parted = {}, {}
 
-        def gather_words(g, half, reuse=None):
-            pairs[g, half] = sbuf("pairs%d%d" % (g, half), [P, HALF], U32, reuse)
-            col = (g * J + half * HALF) // LIST_ROWS
-            picks = offsets[:, col : col + HALF // LIST_ROWS]
-            nc.vector.tensor_copy(pairs[g, half][:], tab_w[:].bitcast(U32).indirect(picks))
+        def gather_words(g, ch0, ch1, reuse=None):
+            picks = offsets[:, (g * J + ch0 * CHUNK) // LIST_ROWS : (g * J + ch1 * CHUNK) // LIST_ROWS]
+            pairs[g, ch0] = sbuf("pairs%d%d" % (g, ch0), [P, (ch1 - ch0) * CHUNK], U32, reuse)
+            nc.vector.tensor_copy(pairs[g, ch0][:], tab_w[:].bitcast(U32).indirect(picks))
 
-        def part_words(g, half):
-            parted[g, half] = sbuf("parted%d%d" % (g, half), [P, PASSES, 2 * HALF], U8)
+        def part_words(g, ch0, ch1, reuse=None):
+            both = sbuf("parted%d%d" % (g, ch0), [P, PASSES, 2 * (ch1 - ch0) * CHUNK], U8, reuse)
             nc.vector.tensor_copy(
-                parted[g, half][:].bitcast(U16),
-                pairs[g, half][:].bitcast(U16).rearrange("p (j a) -> p a j", a=PASSES),
+                both[:].bitcast(U16), pairs[g, ch0][:].bitcast(U16).rearrange("p (j a) -> p a j", a=PASSES)
             )
+            for ch in range(ch0, ch1):
+                parted[g, ch] = both[:, :, 2 * (ch - ch0) * CHUNK : 2 * (ch - ch0 + 1) * CHUNK]
 
         sums = {}
 
         def neighbour_pass(ch, g, a):
-            half, j0 = divmod(ch * CHUNK, HALF)
             if a == 0:
-                sums[ch, g] = bank("sum%d%d" % (ch, g), SUM_BANK[ch][g])
-            m0 = g * J + ch * CHUNK
+                sums[ch, g] = bank("sum%d%d" % (ch, g))
+            j0 = ch * CHUNK
             nc.tensor.matmul_mx(
                 out=sums[ch, g][:],
-                lhsT=parted[g, half][:, a, 2 * j0 : 2 * (j0 + CHUNK)].bitcast(FP4X4),
-                lhsT_scale=tab_planes[a][:, m0 : m0 + CHUNK],
+                lhsT=parted[g, ch][:, a, :].bitcast(FP4X4),
+                lhsT_scale=planes[g][a][:, j0 : j0 + CHUNK],
                 rhs=w_q[a][:].bitcast(FP8X4),
                 rhs_scale=w_s[a][:],
                 start=(a == 0),
@@ -183,26 +195,33 @@ def tile_list_pnet_none_kernel(
             for a in range(PASSES):
                 neighbour_pass(ch, g, a)
 
-        def psum_view(acc):
-            return acc[:].rearrange("j (p u e) -> j u p e", u=2, e=2)
+        def views(ch, acc, flat):
+            if ch in ADD_ON_TENSOR:
+                return acc[:].rearrange("j (p i) -> j i p", i=PACK), flat[:].rearrange("j (i p) -> j i p", i=PACK)
+            return (
+                acc[:].rearrange("j (p u e) -> j u p e", u=2, e=2),
+                flat[:].rearrange("j (u p e) -> j u p e", u=2, e=2),
+            )
 
-        def sbuf_view(flat):
-            return flat[:].rearrange("j (u p e) -> j u p e", u=2, e=2)
+        best, own, z, turned, firsts = {}, {}, {}, {}, []
 
-        best, own, z, h_bf = {}, {}, {}, {}
+        def copy_out(flat, ch, acc):
+            src, dst = views(ch, acc, flat)
+            nc.scalar.activation(dst, src, ACT.Copy)
+            return flat
 
         def take_first(ch):
-            best[ch] = sbuf("first%d" % ch, [P, R], F32)
-            nc.scalar.activation(sbuf_view(best[ch]), psum_view(sums[ch, 0]), ACT.Copy)
+            best[ch] = copy_out(firsts[0][:, ch, :], ch, sums[ch, 0])
 
-        def take_max(ch, g):
-            larger = sbuf("max%d%d" % (ch, g), [P, R], F32)
-            nc.vector.tensor_tensor(sbuf_view(larger), psum_view(sums[ch, g]), sbuf_view(best[ch]), ALU.max)
+        def take_max(ch, g, reuse=None):
+            larger = sbuf("max%d%d" % (ch, g), [P, R], F32, reuse)
+            src, dst = views(ch, sums[ch, g], larger)
+            nc.vector.tensor_tensor(dst, src, views(ch, sums[ch, g], best[ch])[1], ALU.max)
             best[ch] = larger
 
         def own_sum(ch):
             half, j0 = divmod(ch * CHUNK, HALF)
-            own[ch] = bank("own%d" % ch, OWN_BANK[ch])
+            own[ch] = bank("own%d" % ch)
             for a in range(PASSES):
                 cols = slice(a * HALF + j0, a * HALF + j0 + CHUNK)
                 nc.tensor.matmul_mx(
@@ -217,33 +236,69 @@ def tile_list_pnet_none_kernel(
 
         def add_own(ch):
             z[ch] = sbuf("z%d" % ch, [P, R], BF16)
-            nc.vector.tensor_tensor(sbuf_view(z[ch]), psum_view(own[ch]), sbuf_view(best[ch]), ALU.add)
+            src, dst = views(ch, own[ch], z[ch])
+            nc.vector.tensor_tensor(dst, src, views(ch, own[ch], best[ch])[1], ALU.add)
 
-        def turn_and_relu(ch):
-            h_bf[ch] = sbuf("h_bf%d" % ch, [P, CHUNK * PACK], BF16)
-            turned = bank("turned%d" % ch, TURNED_BANK[ch])
+        def turn_adding(ch, flat, first):
+            for i in range(PACK):
+                cols = slice(i * P, (i + 1) * P)
+                nc.tensor.matmul(
+                    turned[ch][:, cols], flat[:, cols], ident[:], is_transpose=True,
+                    start=(first and i == 0), stop=(not first and i == PACK - 1),
+                )
+
+        def copy_own(ch):
+            z[ch] = copy_out(sbuf("own_sb%d" % ch, [P, R], F32), ch, own[ch])
+
+        def turn_own(ch):
+            turned[ch] = bank("turned%d" % ch)
+            turn_adding(ch, z[ch], True)
+
+        def turn(ch):
+            if ch in ADD_ON_TENSOR:
+                turn_adding(ch, best[ch], False)
+                return
+            turned[ch] = bank("turned%d" % ch)
             for u in range(2):
                 words = z[ch][:].bitcast(F32)[:, u * P : (u + 1) * P]
-                nc.tensor.transpose(turned[:, u * P : (u + 1) * P], words, ident[:])
-            dst = h_bf[ch][:].rearrange("p (j u e) -> p j u e", u=2, e=2)
-            src = turned[:, 0 : 2 * P].bitcast(BF16).rearrange("p (u j e) -> p j u e", u=2, e=2)
+                nc.tensor.transpose(turned[ch][:, u * P : (u + 1) * P], words, ident[:])
+
+        h_bf = {}
+
+        def relu(ch, reuse=None):
+            group = [g for g in GROUPS if ch in g][0]
+            if group not in h_bf:
+                h_bf[group] = sbuf("h_bf%d" % group[0], [P, len(group), CHUNK * PACK], BF16, reuse)
+            flat = h_bf[group][:, ch - group[0], :]
+            if ch in ADD_ON_TENSOR:
+                dst = flat.rearrange("p (j i) -> p j i", i=PACK)
+                src = turned[ch][:].rearrange("p (i j) -> p j i", i=PACK)
+            else:
+                dst = flat.rearrange("p (j u e) -> p j u e", u=2, e=2)
+                src = turned[ch][:, 0 : 2 * P].bitcast(BF16).rearrange("p (u j e) -> p j u e", u=2, e=2)
             if ch in RELU_ON_VECTOR:
                 nc.vector.tensor_scalar(dst, src, 0.0, None, ALU.max)
             else:
                 nc.scalar.activation(dst, src, ACT.Relu)
 
-        def second_layer(ch):
-            h_q = sbuf("h_q%d" % ch, [P, CHUNK], U32)
-            h_s = sbuf("h_s%d" % ch, [P, CHUNK], U8)
-            nc.vector.quantize_mx(out=h_q[:].bitcast(FP8X4), scales=h_s[:], in_=h_bf[ch][:])
-            tiles = N // P // len(Y_BANK[ch])
-            for piece, index in enumerate(Y_BANK[ch]):
+        def second_layer(group):
+            width = len(group) * CHUNK
+            last = FINAL in group
+            h_q = sbuf("h_q%d" % group[0], [P, width], U32)
+            h_s = sbuf("h_s%d" % group[0], [P, width], U8)
+            nc.vector.quantize_mx(
+                out=h_q[:].bitcast(FP8X4), scales=h_s[:], in_=h_bf[group][:].rearrange("p c x -> p (c x)")
+            )
+            pieces = 2 if last else len(group)
+            tiles = N // P // pieces
+            done = []
+            for piece in range(pieces):
                 t0 = piece * tiles
-                y_acc = bank("y_acc%d%d" % (ch, t0), index)
+                y_acc = bank("y_acc%d%d" % (group[0], t0))
                 for t in range(tiles):
                     cols = slice((t0 + t) * P, (t0 + t + 1) * P)
                     nc.tensor.matmul_mx(
-                        out=y_acc[:, t * CHUNK : (t + 1) * CHUNK],
+                        out=y_acc[:, t * width : (t + 1) * width],
                         lhsT=wd_w[:, cols].bitcast(FP8X4),
                         lhsT_scale=wd_s[:].bitcast(U8)[:, cols],
                         rhs=h_q[:].bitcast(FP8X4),
@@ -251,66 +306,90 @@ def tile_list_pnet_none_kernel(
                         start=True,
                         stop=True,
                     )
-                y = sbuf("y%d%d" % (ch, t0), [P, tiles * CHUNK], F32)
-                rows = out[t0 * P : (t0 + tiles) * P, ch * CHUNK : (ch + 1) * CHUNK].rearrange("(t p) j -> p t j", p=P)
-                if ch == LAST and piece == 0:
-                    nc.vector.tensor_copy(y[:], y_acc[:, 0 : tiles * CHUNK])
+                done.append((group, piece, tiles, y_acc))
+            return done
+
+        def store(job):
+            group, piece, tiles, y_acc = job
+            width, t0, last = len(group) * CHUNK, piece * tiles, FINAL in group
+            if True:
+                y = sbuf("y%d%d" % (group[0], t0), [P, tiles * width], F32)
+                points = slice(group[0] * CHUNK, group[0] * CHUNK + width)
+                rows = out[t0 * P : (t0 + tiles) * P, points].rearrange("(t p) j -> p t j", p=P)
+                if (group[0], piece) in Y_ON_VECTOR:
+                    nc.vector.tensor_copy(y[:], y_acc[:, 0 : tiles * width])
                 else:
-                    nc.scalar.activation(y[:], y_acc[:, 0 : tiles * CHUNK], ACT.Copy)
-                queue = nc.scalar if ch == LAST and piece == 1 else nc.sync
-                queue.dma_start(rows, y[:].rearrange("p (t j) -> p t j", j=CHUNK))
+                    nc.scalar.activation(y[:], y_acc[:, 0 : tiles * width], ACT.Copy)
+                queue = nc.scalar if last and piece == 1 else nc.sync
+                queue.dma_start(rows, y[:].rearrange("p (t j) -> p t j", j=width))
 
+        round_w(0)
         quantize_w(0)
-        for g in range(NEIGHBOURS):
-            gather_words(g, 0)
-        for g in range(NEIGHBOURS):
-            part_words(g, 0)
-        for ch in (0, 1):
-            for g in range(NEIGHBOURS):
-                neighbour_pass(ch, g, 0)
+        gather_words(0, 0, 2, "w_raw01")
+        gather_words(0, 2, 4, "w_bf0")
+        part_words(0, 0, 2)
+        gather_words(1, 0, 4, "w_raw01")
+        part_words(0, 2, 4)
+        for ch in range(4):
+            neighbour_pass(ch, 0, 0)
+        round_w(1)
+        gather_words(2, 0, 2, "w_bf0")
+        part_words(1, 0, 4)
         quantize_w(1)
-        for g in (0, 1):
-            gather_words(g, 1)
+        gather_words(2, 2, 4, "w_raw11")
         for ch in (0, 1):
-            for g in range(NEIGHBOURS):
-                neighbour_pass(ch, g, 1)
+            neighbour_pass(ch, 1, 0)
         for g in (0, 1):
-            part_words(g, 1)
-        gather_words(2, 1, "w_bf1")
-        part_words(2, 1)
-
-        quantize_c(0)
-        for ch in (0, 1):
-            take_first(ch)
-        for g in (1, 2):
             for ch in (0, 1):
-                take_max(ch, g)
+                neighbour_pass(ch, g, 1)
+        for a in range(PASSES):
+            round_c(a, 0)
+        part_words(2, 0, 2, "w_bf1")
+        part_words(2, 2, 4)
+        quantize_c(0)
         for ch in (2, 3):
-            for g in (0, 1):
-                neighbour_sum(ch, g)
-        for ch in (0, 1):
-            own_sum(ch)
-        quantize_c(1)
-
+            neighbour_pass(ch, 0, 1)
+        firsts.append(sbuf("firsts", [P, 4, R], F32, "c_raw10"))
+        for ch in range(4):
+            take_first(ch)
+        for a in range(PASSES):
+            round_c(a, 1)
+        neighbour_sum(0, 2)
+        neighbour_sum(1, 2)
+        take_max(0, 1)
+        take_max(1, 1)
+        own_sum(0)
+        own_sum(1)
+        take_max(0, 2)
+        take_max(1, 2)
+        neighbour_sum(2, 1)
+        neighbour_sum(3, 1)
+        add_own(0)
+        add_own(1)
+        turn(0)
+        turn(1)
         neighbour_sum(2, 2)
-        take_first(2)
-        for ch in (0, 1):
-            add_own(ch)
-        take_max(2, 1)
-        for ch in (2, 3):
-            own_sum(ch)
         neighbour_sum(3, 2)
-        take_first(3)
-        for ch in (0, 1):
-            turn_and_relu(ch)
-        take_max(2, 2)
-        take_max(3, 1)
+        take_max(2, 1)
+        quantize_c(1)
+        relu(0, "c_bf0")
+        relu(1)
+        own_sum(2)
+        own_sum(3)
+        take_max(3, 1, "c_raw11")
+        take_max(2, 2, "c_bf1")
+        y01 = second_layer((0, 1))
         add_own(2)
-        for ch in (0, 1):
-            second_layer(ch)
-        take_max(3, 2)
-        add_own(3)
-        for ch in (2, 3):
-            turn_and_relu(ch)
-        for ch in (2, 3):
-            second_layer(ch)
+        take_max(3, 2, "c_q1")
+        copy_own(3)
+        turn(2)
+        turn_own(3)
+        turn(3)
+        relu(2)
+        for piece in y01:
+            store(piece)
+        y2 = second_layer((2,))
+        relu(3)
+        y3 = second_layer((3,))
+        for piece in y2 + y3:
+            store(piece)

@@ -30,13 +30,14 @@ HALF = 256
 CHUNK = 128
 LAST = J // CHUNK - 1
 
-RELU_ON_VECTOR = (3,)
+RELU_ON_VECTOR = (2,)
 ADD_ON_TENSOR = (3,)
 FINAL = 3
 GROUPS = ((0, 1), (2,), (3,))
 C_ENGINE = ("SS", "SS")
 C_BF_TAG = ("c_bf0", "c_bf1")
-Y_ON_VECTOR = ((3, 0), (0, 0))
+Y_ON_VECTOR = ((3, 0),)
+W_LEAD = 128
 BANKS = 8
 
 
@@ -60,22 +61,26 @@ def tile_list_pnet_none_kernel(
         offsets = keep.tile([P, NEIGHBOURS * J // LIST_ROWS], U16, name="offsets")
         nc.sync.dma_start(offsets[:], offs)
 
+        def load_cols(name, src, a, x0, x1):
+            raw = sbuf(name, [P, PACK, x1 - x0], F32)
+            rows = src[a * K_PASS : (a + 1) * K_PASS, x0:x1]
+            nc.sync.dma_start(raw[:], rows.rearrange("(p i) x -> p i x", i=PACK))
+            return raw
+
+        def load_raw(name, src, a, half):
+            return load_cols("%s_raw%d%d" % (name, a, half), src, a, half * HALF, (half + 1) * HALF)
+
+        w_cut = ((0, W_LEAD, R), (0, HALF, R))
+        w_raw = {(0, 0): load_cols("w_raw00", w, 0, 0, W_LEAD)}
+
         tab_s = sbuf("tab_s", [P, T // 4], I32)
         nc.vector.memset(tab_s[:, 0 : T // 8], 0)
         nc.gpsimd.memset(tab_s[:, T // 8 : T // 4], 0)
         for r in range(4):
             rows = tab_scales[:, r:BLOCKS:4, :].rearrange("a quad t -> quad a t")
-            nc.sync.dma_start(tab_s[r:P:SHIFT, :], rows.bitcast(I32))
+            (nc.sync if r < 2 else nc.scalar).dma_start(tab_s[r:P:SHIFT, :], rows.bitcast(I32))
 
-        def load_raw(name, src, a, half):
-            raw = sbuf("%s_raw%d%d" % (name, a, half), [P, PACK, HALF], F32)
-            rows = src[a * K_PASS : (a + 1) * K_PASS, half * HALF : (half + 1) * HALF]
-            nc.sync.dma_start(raw[:], rows.rearrange("(p i) x -> p i x", i=PACK))
-            return raw
-
-        w_raw = {}
-        for half in range(2):
-            w_raw[0, half] = load_raw("w", w, 0, half)
+        w_raw[0, 1] = load_cols("w_raw01", w, 0, W_LEAD, R)
         tab_w = sbuf("tab_w", [P, T], I32)
         nc.sync.dma_start(tab_w[:], tab_words[0].rearrange("p t b -> p (t b)").bitcast(I32))
         for half in range(2):
@@ -105,7 +110,8 @@ def tile_list_pnet_none_kernel(
             return moved, picked
 
         moved, picked = gather_scales(0, NEIGHBOURS)
-        nc.sync.dma_start(moved[0 : P - SHIFT, :], picked[SHIFT:P, :].bitcast(I32))
+        for r in range(4):
+            nc.sync.dma_start(moved[r:P:QUADRANT, :], picked[SHIFT + r : P : QUADRANT, :].bitcast(I32))
 
         c_raw = {(a, 0): load_raw("c", c, a, 0) for a in range(PASSES)}
         wc_w = sbuf("wc_w", [P, PASSES, R // 2], I32)
@@ -135,15 +141,15 @@ def tile_list_pnet_none_kernel(
 
         w_q = [sbuf("w_q%d" % a, [P, R], U32) for a in range(PASSES)]
         w_s = [sbuf("w_s%d" % a, [P, R], U8) for a in range(PASSES)]
-        w_bf = [sbuf("w_bf%d" % a, [P, 2, HALF * PACK], BF16) for a in range(PASSES)]
+        w_bf = [sbuf("w_bf%d" % a, [P, R * PACK], BF16) for a in range(PASSES)]
 
         def round_w(a):
             for half in range(2):
-                round_and_interleave(w_raw[a, half], w_bf[a][:, half, :])
+                round_and_interleave(w_raw[a, half], w_bf[a][:, w_cut[a][half] * PACK : w_cut[a][half + 1] * PACK])
 
         def quantize_w(a):
             nc.vector.quantize_mx(
-                out=w_q[a][:].bitcast(FP8X4), scales=w_s[a][:], in_=w_bf[a][:].rearrange("p h x -> p (h x)")
+                out=w_q[a][:].bitcast(FP8X4), scales=w_s[a][:], in_=w_bf[a][:]
             )
 
         c_bf = {}
@@ -309,11 +315,11 @@ def tile_list_pnet_none_kernel(
                 done.append((group, piece, tiles, y_acc))
             return done
 
-        def store(job):
+        def store(job, reuse=None):
             group, piece, tiles, y_acc = job
             width, t0, last = len(group) * CHUNK, piece * tiles, FINAL in group
             if True:
-                y = sbuf("y%d%d" % (group[0], t0), [P, tiles * width], F32)
+                y = sbuf("y%d%d" % (group[0], t0), [P, tiles * width], F32, reuse)
                 points = slice(group[0] * CHUNK, group[0] * CHUNK + width)
                 rows = out[t0 * P : (t0 + tiles) * P, points].rearrange("(t p) j -> p t j", p=P)
                 if (group[0], piece) in Y_ON_VECTOR:
@@ -328,24 +334,26 @@ def tile_list_pnet_none_kernel(
         gather_words(0, 0, 2, "w_raw01")
         gather_words(0, 2, 4, "w_bf0")
         part_words(0, 0, 2)
-        gather_words(1, 0, 4, "w_raw01")
         part_words(0, 2, 4)
+        gather_words(1, 0, 2, "w_raw01")
+        gather_words(1, 2, 4, "w_bf0")
+        part_words(1, 0, 2)
+        part_words(1, 2, 4)
         for ch in range(4):
             neighbour_pass(ch, 0, 0)
         round_w(1)
-        gather_words(2, 0, 2, "w_bf0")
-        part_words(1, 0, 4)
-        quantize_w(1)
-        gather_words(2, 2, 4, "w_raw11")
         for ch in (0, 1):
             neighbour_pass(ch, 1, 0)
+        quantize_w(1)
+        gather_words(2, 0, 2, "w_raw11")
+        gather_words(2, 2, 4, "w_bf1")
+        part_words(2, 0, 2)
+        part_words(2, 2, 4)
         for g in (0, 1):
             for ch in (0, 1):
                 neighbour_pass(ch, g, 1)
         for a in range(PASSES):
             round_c(a, 0)
-        part_words(2, 0, 2, "w_bf1")
-        part_words(2, 2, 4)
         quantize_c(0)
         for ch in (2, 3):
             neighbour_pass(ch, 0, 1)
@@ -366,18 +374,18 @@ def tile_list_pnet_none_kernel(
         neighbour_sum(3, 1)
         add_own(0)
         add_own(1)
+        neighbour_sum(2, 2)
         turn(0)
         turn(1)
-        neighbour_sum(2, 2)
         neighbour_sum(3, 2)
-        take_max(2, 1)
         quantize_c(1)
+        take_max(2, 1, "c_raw11")
         relu(0, "c_bf0")
         relu(1)
         own_sum(2)
         own_sum(3)
-        take_max(3, 1, "c_raw11")
-        take_max(2, 2, "c_bf1")
+        take_max(3, 1, "c_bf1")
+        take_max(2, 2)
         y01 = second_layer((0, 1))
         add_own(2)
         take_max(3, 2, "c_q1")

@@ -24,21 +24,15 @@ K_PASS = P * PACK
 PASSES = K // K_PASS
 BLOCKS = K_PASS // 32
 QUADRANT = 32
-SHIFT = 16
 LIST_ROWS = 16
 HALF = 256
 CHUNK = 128
-LAST = J // CHUNK - 1
-
-RELU_ON_VECTOR = (2,)
-ADD_ON_TENSOR = (3,)
-FINAL = 3
-GROUPS = ((0, 1), (2,), (3,))
-C_ENGINE = ("SS", "SS")
-C_BF_TAG = ("c_bf0", "c_bf1")
-Y_ON_VECTOR = ((3, 0),)
-W_LEAD = 128
+CHUNKS = J // CHUNK
+LAST = CHUNKS - 1
 BANKS = 8
+BANK_COLS = 512
+PIECES = 2
+WARM_UPS = 5
 
 
 def tile_list_pnet_none_kernel(
@@ -52,145 +46,132 @@ def tile_list_pnet_none_kernel(
         def sbuf(name, shape, dtype, reuse=None):
             return keep.tile(shape, dtype, name=name, tag=reuse or name, align_bytes=64)
 
-        taken = []
+        accumulators = []
 
-        def bank(name):
-            taken.append(name)
-            return psum.tile([P, 512], F32, name=name, tag="bank%d" % ((len(taken) - 1) % BANKS))
+        def next_bank(name):
+            accumulators.append(name)
+            return psum.tile([P, BANK_COLS], F32, name=name, tag="bank%d" % ((len(accumulators) - 1) % BANKS))
+
+        def plane_rows(plane, quad):
+            return plane[QUADRANT * quad : QUADRANT * quad + 4]
+
+        def load_raw(name, src, a, half):
+            raw = sbuf("%s_raw%d%d" % (name, a, half), [P, PACK, HALF], F32)
+            rows = src[a * K_PASS : (a + 1) * K_PASS, half * HALF : (half + 1) * HALF]
+            nc.sync.dma_start(raw[:], rows.rearrange("(p i) x -> p i x", i=PACK))
+            return raw
 
         offsets = keep.tile([P, NEIGHBOURS * J // LIST_ROWS], U16, name="offsets")
         nc.sync.dma_start(offsets[:], offs)
 
-        def load_cols(name, src, a, x0, x1):
-            raw = sbuf(name, [P, PACK, x1 - x0], F32)
-            rows = src[a * K_PASS : (a + 1) * K_PASS, x0:x1]
-            nc.sync.dma_start(raw[:], rows.rearrange("(p i) x -> p i x", i=PACK))
-            return raw
-
-        def load_raw(name, src, a, half):
-            return load_cols("%s_raw%d%d" % (name, a, half), src, a, half * HALF, (half + 1) * HALF)
-
-        w_cut = ((0, W_LEAD, R), (0, HALF, R))
-        w_raw = {(0, 0): load_cols("w_raw00", w, 0, 0, W_LEAD)}
-
         tab_s = sbuf("tab_s", [P, T // 4], I32)
-        nc.vector.memset(tab_s[:, 0 : T // 8], 0)
-        nc.gpsimd.memset(tab_s[:, T // 8 : T // 4], 0)
-        for r in range(4):
-            rows = tab_scales[:, r:BLOCKS:4, :].rearrange("a quad t -> quad a t")
-            (nc.sync if r < 2 else nc.scalar).dma_start(tab_s[r:P:SHIFT, :], rows.bitcast(I32))
-
-        w_raw[0, 1] = load_cols("w_raw01", w, 0, W_LEAD, R)
-        tab_w = sbuf("tab_w", [P, T], I32)
-        nc.sync.dma_start(tab_w[:], tab_words[0].rearrange("p t b -> p (t b)").bitcast(I32))
-        for half in range(2):
-            w_raw[1, half] = load_raw("w", w, 1, half)
-
+        nc.sync.dma_start(tab_s[0:QUADRANT, :], tab_scales.rearrange("a q t -> (a q) t").bitcast(I32))
         wc_s = sbuf("wc_s", [P, PASSES, R // 4], I32)
         wd_s = sbuf("wd_s", [P, N // 4], I32)
-        ident = sbuf("ident", [P, P], F32)
-        nc.vector.memset(ident[:], 0.0)
-        make_identity(nc, ident[:], nomemset=True)
-        nc.gpsimd.memset(wc_s[:], 0)
-        nc.gpsimd.memset(wd_s[:], 0)
+        nc.vector.memset(wc_s[:], 0)
+        nc.vector.memset(tab_s[2 * QUADRANT : P, :], 0)
+        nc.gpsimd.memset(tab_s[QUADRANT : 2 * QUADRANT, :], 0)
 
-        planes = {}
-
-        def gather_scales(g0, g1, reuse=None):
-            width = (g1 - g0) * J
-            moved = sbuf("moved_s%d" % g0, [P, width // 4], I32)
-            nc.vector.memset(moved[:], 0)
-            picked = sbuf("picked_s%d" % g0, [P, width], U8, reuse)
-            picks = offsets[:, g0 * J // LIST_ROWS : g1 * J // LIST_ROWS]
-            nc.vector.tensor_copy(picked[:], tab_s[:].bitcast(U8).indirect(picks))
-            for g in range(g0, g1):
-                cols = slice((g - g0) * J, (g - g0 + 1) * J)
-                planes[g] = [picked[:, cols], moved[:].bitcast(U8)[:, cols]]
-
-            return moved, picked
-
-        moved, picked = gather_scales(0, NEIGHBOURS)
-        for r in range(4):
-            nc.sync.dma_start(moved[r:P:QUADRANT, :], picked[SHIFT + r : P : QUADRANT, :].bitcast(I32))
-
-        c_raw = {(a, 0): load_raw("c", c, a, 0) for a in range(PASSES)}
-        wc_w = sbuf("wc_w", [P, PASSES, R // 2], I32)
-        nc.sync.dma_start(wc_w[:], wc_words.rearrange("a p b -> p a b").bitcast(I32))
+        w_raw = {(0, 0): load_raw("w", w, 0, 0)}
         for quad in range(P // QUADRANT):
             rows = wc_scales[:, 4 * quad : 4 * quad + 4, :].rearrange("a q r -> q a r")
-            nc.sync.dma_start(wc_s[QUADRANT * quad : QUADRANT * quad + 4, :, :], rows.bitcast(I32))
+            nc.sync.dma_start(plane_rows(wc_s, quad), rows.bitcast(I32))
+        tab_w = sbuf("tab_w", [P, T], I32)
+        nc.sync.dma_start(tab_w[:], tab_words[0].rearrange("p t b -> p (t b)").bitcast(I32))
+        for a, half in ((0, 1), (1, 0), (1, 1)):
+            w_raw[a, half] = load_raw("w", w, a, half)
+
+        ident = sbuf("ident", [P, P], F32)
+        make_identity(nc, ident[:])
+
+        tab_planes = [sbuf("tab_plane%d" % a, [P, NEIGHBOURS * J // 4], I32) for a in range(PASSES)]
+        nc.vector.memset(tab_planes[0][:], 0)
+        nc.gpsimd.memset(tab_planes[1][:], 0)
+        nc.gpsimd.memset(wd_s[:], 0)
+        picked_s = sbuf("picked_s", [P, NEIGHBOURS * J], U8)
+        nc.vector.tensor_copy(picked_s[:], tab_s[:].bitcast(U8).indirect(offsets[:]))
+
+        def move_scales(a):
+            for quad in range(P // QUADRANT):
+                row = BLOCKS * a + 4 * quad
+                nc.sync.dma_start(plane_rows(tab_planes[a], quad), picked_s[row : row + 4, :].bitcast(I32))
+
+        move_scales(0)
+        c_raw = {(a, 0): load_raw("c", c, a, 0) for a in range(PASSES)}
+        move_scales(1)
+        wc_w = sbuf("wc_w", [P, PASSES, R // 2], I32)
+        nc.sync.dma_start(wc_w[:], wc_words.rearrange("a p b -> p a b").bitcast(I32))
         for a in range(PASSES):
             c_raw[a, 1] = load_raw("c", c, a, 1)
         wd_w = sbuf("wd_w", [P, N], I32)
         nc.sync.dma_start(wd_w[:], wd_words[0].rearrange("p n b -> p (n b)").bitcast(I32))
         for quad in range(P // QUADRANT):
-            rows = wd_scales[0, 4 * quad : 4 * quad + 4, :]
-            nc.sync.dma_start(wd_s[QUADRANT * quad : QUADRANT * quad + 4, :], rows.bitcast(I32))
+            nc.sync.dma_start(plane_rows(wd_s, quad), wd_scales[0, 4 * quad : 4 * quad + 4, :].bitcast(I32))
 
-        def round_and_interleave(raw, grouped, engine="S"):
-            if engine == "G":
-                dst = grouped.rearrange("p (x i) -> p x i", i=PACK)
-                nc.gpsimd.tensor_scalar(dst, raw[:].rearrange("p i x -> p x i"), 1.0, 0.0, ALU.mult, ALU.add)
-                return
+        def round_and_interleave(raw, grouped):
             dst = grouped.rearrange("p (y x i) -> p y i x", x=4, i=PACK)
             src = raw[:].rearrange("p i (y x) -> p y i x", x=4)
-            if engine == "V":
-                nc.vector.tensor_copy(dst, src)
-            else:
-                nc.scalar.activation(dst, src, ACT.Copy)
+            nc.scalar.activation(dst, src, ACT.Copy)
 
         w_q = [sbuf("w_q%d" % a, [P, R], U32) for a in range(PASSES)]
         w_s = [sbuf("w_s%d" % a, [P, R], U8) for a in range(PASSES)]
         w_bf = [sbuf("w_bf%d" % a, [P, R * PACK], BF16) for a in range(PASSES)]
 
         def round_w(a):
-            for half in range(2):
-                round_and_interleave(w_raw[a, half], w_bf[a][:, w_cut[a][half] * PACK : w_cut[a][half + 1] * PACK])
+            for half in range(R // HALF):
+                round_and_interleave(w_raw[a, half], w_bf[a][:, half * HALF * PACK : (half + 1) * HALF * PACK])
 
-        def quantize_w(a):
+        def quantize_w(a, r0, r1):
             nc.vector.quantize_mx(
-                out=w_q[a][:].bitcast(FP8X4), scales=w_s[a][:], in_=w_bf[a][:]
+                out=w_q[a][:, r0:r1].bitcast(FP8X4), scales=w_s[a][:, r0:r1], in_=w_bf[a][:, r0 * PACK : r1 * PACK]
             )
 
-        c_bf = {}
-        c_q = [sbuf("c_q%d" % half, [P, PASSES * HALF], U32) for half in range(2)]
-        c_s = [sbuf("c_s%d" % half, [P, PASSES * HALF], U8) for half in range(2)]
+        c_bf, c_q = {}, {}
+        c_s = [sbuf("c_s%d" % half, [P, PASSES * HALF], U8) for half in range(J // HALF)]
 
-        def round_c(a, half):
-            if a == 0:
-                c_bf[half] = sbuf("c_bf%d" % half, [P, PASSES, HALF * PACK], BF16, C_BF_TAG[half])
-            round_and_interleave(c_raw[a, half], c_bf[half][:, a, :], C_ENGINE[half][a])
+        def round_c(half):
+            c_bf[half] = sbuf("c_bf%d" % half, [P, PASSES, HALF * PACK], BF16)
+            for a in range(PASSES):
+                round_and_interleave(c_raw[a, half], c_bf[half][:, a, :])
 
-        def quantize_c(half):
+        def quantize_c(half, reuse=None):
+            c_q[half] = sbuf("c_q%d" % half, [P, PASSES * HALF], U32, reuse)
             nc.vector.quantize_mx(
                 out=c_q[half][:].bitcast(FP8X4), scales=c_s[half][:], in_=c_bf[half][:].rearrange("p a x -> p (a x)")
             )
 
         pairs, parted = {}, {}
 
-        def gather_words(g, ch0, ch1, reuse=None):
-            picks = offsets[:, (g * J + ch0 * CHUNK) // LIST_ROWS : (g * J + ch1 * CHUNK) // LIST_ROWS]
-            pairs[g, ch0] = sbuf("pairs%d%d" % (g, ch0), [P, (ch1 - ch0) * CHUNK], U32, reuse)
-            nc.vector.tensor_copy(pairs[g, ch0][:], tab_w[:].bitcast(U32).indirect(picks))
-
-        def part_words(g, ch0, ch1, reuse=None):
-            both = sbuf("parted%d%d" % (g, ch0), [P, PASSES, 2 * (ch1 - ch0) * CHUNK], U8, reuse)
+        def gather_words(g, half, reuse=None):
+            col = (g * J + half * HALF) // LIST_ROWS
+            pairs[g, half] = sbuf("pairs%d%d" % (g, half), [P, HALF], U32, reuse)
             nc.vector.tensor_copy(
-                both[:].bitcast(U16), pairs[g, ch0][:].bitcast(U16).rearrange("p (j a) -> p a j", a=PASSES)
+                pairs[g, half][:], tab_w[:].bitcast(U32).indirect(offsets[:, col : col + HALF // LIST_ROWS])
             )
-            for ch in range(ch0, ch1):
-                parted[g, ch] = both[:, :, 2 * (ch - ch0) * CHUNK : 2 * (ch - ch0 + 1) * CHUNK]
+
+        def parted_tile(name, reuse=None):
+            return sbuf(name, [P, PASSES, 2 * HALF], U8, reuse)[:]
+
+        def part_words(g, half, dst):
+            parted[g, half] = dst
+            nc.vector.tensor_copy(
+                dst.bitcast(U16), pairs[g, half][:].bitcast(U16).rearrange("p (j a) -> p a j", a=PASSES)
+            )
+
+        def table_operand(ch, g, a):
+            half, j0 = divmod(ch * CHUNK, HALF)
+            return parted[g, half][:, a, 2 * j0 : 2 * (j0 + CHUNK)].bitcast(FP4X4)
 
         sums = {}
 
         def neighbour_pass(ch, g, a):
             if a == 0:
-                sums[ch, g] = bank("sum%d%d" % (ch, g))
-            j0 = ch * CHUNK
+                sums[ch, g] = next_bank("sum%d%d" % (ch, g))
+            m0 = g * J + ch * CHUNK
             nc.tensor.matmul_mx(
                 out=sums[ch, g][:],
-                lhsT=parted[g, ch][:, a, :].bitcast(FP4X4),
-                lhsT_scale=planes[g][a][:, j0 : j0 + CHUNK],
+                lhsT=table_operand(ch, g, a),
+                lhsT_scale=tab_planes[a][:].bitcast(U8)[:, m0 : m0 + CHUNK],
                 rhs=w_q[a][:].bitcast(FP8X4),
                 rhs_scale=w_s[a][:],
                 start=(a == 0),
@@ -201,33 +182,31 @@ def tile_list_pnet_none_kernel(
             for a in range(PASSES):
                 neighbour_pass(ch, g, a)
 
-        def views(ch, acc, flat):
-            if ch in ADD_ON_TENSOR:
-                return acc[:].rearrange("j (p i) -> j i p", i=PACK), flat[:].rearrange("j (i p) -> j i p", i=PACK)
-            return (
-                acc[:].rearrange("j (p u e) -> j u p e", u=2, e=2),
-                flat[:].rearrange("j (u p e) -> j u p e", u=2, e=2),
-            )
+        def psum_view(ch, acc):
+            if ch == LAST:
+                return acc.rearrange("j (p i) -> j i p", i=PACK)
+            return acc.rearrange("j (p u e) -> j u p e", u=2, e=2)
 
-        best, own, z, turned, firsts = {}, {}, {}, {}, []
+        def sbuf_view(ch, flat):
+            if ch == LAST:
+                return flat.rearrange("j (i p) -> j i p", i=PACK)
+            return flat.rearrange("j (u p e) -> j u p e", u=2, e=2)
 
-        def copy_out(flat, ch, acc):
-            src, dst = views(ch, acc, flat)
-            nc.scalar.activation(dst, src, ACT.Copy)
-            return flat
+        best, own, z, turned = {}, {}, {}, {}
 
-        def take_first(ch):
-            best[ch] = copy_out(firsts[0][:, ch, :], ch, sums[ch, 0])
+        def copy_out(ch, flat, acc):
+            nc.scalar.activation(sbuf_view(ch, flat), psum_view(ch, acc[:]), ACT.Copy)
 
         def take_max(ch, g, reuse=None):
-            larger = sbuf("max%d%d" % (ch, g), [P, R], F32, reuse)
-            src, dst = views(ch, sums[ch, g], larger)
-            nc.vector.tensor_tensor(dst, src, views(ch, sums[ch, g], best[ch])[1], ALU.max)
+            larger = sbuf("max%d%d" % (ch, g), [P, R], F32, reuse)[:]
+            nc.vector.tensor_tensor(
+                sbuf_view(ch, larger), psum_view(ch, sums[ch, g][:]), sbuf_view(ch, best[ch]), ALU.max
+            )
             best[ch] = larger
 
         def own_sum(ch):
             half, j0 = divmod(ch * CHUNK, HALF)
-            own[ch] = bank("own%d" % ch)
+            own[ch] = next_bank("own%d" % ch)
             for a in range(PASSES):
                 cols = slice(a * HALF + j0, a * HALF + j0 + CHUNK)
                 nc.tensor.matmul_mx(
@@ -242,69 +221,49 @@ def tile_list_pnet_none_kernel(
 
         def add_own(ch):
             z[ch] = sbuf("z%d" % ch, [P, R], BF16)
-            src, dst = views(ch, own[ch], z[ch])
-            nc.vector.tensor_tensor(dst, src, views(ch, own[ch], best[ch])[1], ALU.add)
-
-        def turn_adding(ch, flat, first):
-            for i in range(PACK):
-                cols = slice(i * P, (i + 1) * P)
-                nc.tensor.matmul(
-                    turned[ch][:, cols], flat[:, cols], ident[:], is_transpose=True,
-                    start=(first and i == 0), stop=(not first and i == PACK - 1),
-                )
-
-        def copy_own(ch):
-            z[ch] = copy_out(sbuf("own_sb%d" % ch, [P, R], F32), ch, own[ch])
-
-        def turn_own(ch):
-            turned[ch] = bank("turned%d" % ch)
-            turn_adding(ch, z[ch], True)
+            nc.vector.tensor_tensor(
+                sbuf_view(ch, z[ch][:]), psum_view(ch, own[ch][:]), sbuf_view(ch, best[ch]), ALU.add
+            )
 
         def turn(ch):
-            if ch in ADD_ON_TENSOR:
-                turn_adding(ch, best[ch], False)
-                return
-            turned[ch] = bank("turned%d" % ch)
+            turned[ch] = next_bank("turned%d" % ch)
             for u in range(2):
                 words = z[ch][:].bitcast(F32)[:, u * P : (u + 1) * P]
                 nc.tensor.transpose(turned[ch][:, u * P : (u + 1) * P], words, ident[:])
 
-        h_bf = {}
+        def turn_adding(flat, opens):
+            for i in range(PACK):
+                cols = slice(i * P, (i + 1) * P)
+                nc.tensor.matmul(
+                    turned[LAST][:, cols],
+                    flat[:, cols],
+                    ident[:],
+                    is_transpose=True,
+                    start=(opens and i == 0),
+                    stop=(not opens and i == PACK - 1),
+                )
 
-        def relu(ch, reuse=None):
-            group = [g for g in GROUPS if ch in g][0]
-            if group not in h_bf:
-                h_bf[group] = sbuf("h_bf%d" % group[0], [P, len(group), CHUNK * PACK], BF16, reuse)
-            flat = h_bf[group][:, ch - group[0], :]
-            if ch in ADD_ON_TENSOR:
-                dst = flat.rearrange("p (j i) -> p j i", i=PACK)
-                src = turned[ch][:].rearrange("p (i j) -> p j i", i=PACK)
-            else:
-                dst = flat.rearrange("p (j u e) -> p j u e", u=2, e=2)
-                src = turned[ch][:, 0 : 2 * P].bitcast(BF16).rearrange("p (u j e) -> p j u e", u=2, e=2)
-            if ch in RELU_ON_VECTOR:
-                nc.vector.tensor_scalar(dst, src, 0.0, None, ALU.max)
-            else:
-                nc.scalar.activation(dst, src, ACT.Relu)
+        def h_tile(first_chunk, chunks, reuse=None):
+            return sbuf("h_bf%d" % first_chunk, [P, chunks, CHUNK * PACK], BF16, reuse)
 
-        def second_layer(group):
-            width = len(group) * CHUNK
-            last = FINAL in group
-            h_q = sbuf("h_q%d" % group[0], [P, width], U32)
-            h_s = sbuf("h_s%d" % group[0], [P, width], U8)
-            nc.vector.quantize_mx(
-                out=h_q[:].bitcast(FP8X4), scales=h_s[:], in_=h_bf[group][:].rearrange("p c x -> p (c x)")
-            )
-            pieces = 2 if last else len(group)
-            tiles = N // P // pieces
-            done = []
-            for piece in range(pieces):
-                t0 = piece * tiles
-                y_acc = bank("y_acc%d%d" % (group[0], t0))
+        def turned_pairs(ch, flat):
+            dst = flat.rearrange("p (j u e) -> p j u e", u=2, e=2)
+            src = turned[ch][:, 0 : 2 * P].bitcast(BF16).rearrange("p (u j e) -> p j u e", u=2, e=2)
+            return dst, src
+
+        def second_layer(first_chunk, chunks, h_bf):
+            width = chunks * CHUNK
+            h_q = sbuf("h_q%d" % first_chunk, [P, width], U32)
+            h_s = sbuf("h_s%d" % first_chunk, [P, width], U8)
+            nc.vector.quantize_mx(out=h_q[:].bitcast(FP8X4), scales=h_s[:], in_=h_bf[:].rearrange("p c x -> p (c x)"))
+            tiles = N // P // PIECES
+            y_accs = []
+            for piece in range(PIECES):
+                y_accs.append(next_bank("y_acc%d%d" % (first_chunk, piece)))
                 for t in range(tiles):
-                    cols = slice((t0 + t) * P, (t0 + t + 1) * P)
+                    cols = slice((piece * tiles + t) * P, (piece * tiles + t + 1) * P)
                     nc.tensor.matmul_mx(
-                        out=y_acc[:, t * width : (t + 1) * width],
+                        out=y_accs[piece][:, t * width : (t + 1) * width],
                         lhsT=wd_w[:, cols].bitcast(FP8X4),
                         lhsT_scale=wd_s[:].bitcast(U8)[:, cols],
                         rhs=h_q[:].bitcast(FP8X4),
@@ -312,92 +271,110 @@ def tile_list_pnet_none_kernel(
                         start=True,
                         stop=True,
                     )
-                done.append((group, piece, tiles, y_acc))
-            return done
+            return y_accs
 
-        def store(job, reuse=None):
-            group, piece, tiles, y_acc = job
-            width, t0, last = len(group) * CHUNK, piece * tiles, FINAL in group
-            if True:
-                y = sbuf("y%d%d" % (group[0], t0), [P, tiles * width], F32, reuse)
-                points = slice(group[0] * CHUNK, group[0] * CHUNK + width)
-                rows = out[t0 * P : (t0 + tiles) * P, points].rearrange("(t p) j -> p t j", p=P)
-                if (group[0], piece) in Y_ON_VECTOR:
-                    nc.vector.tensor_copy(y[:], y_acc[:, 0 : tiles * width])
+        def store(first_chunk, chunks, y_accs):
+            width = chunks * CHUNK
+            tiles = N // P // PIECES
+            for piece in range(PIECES):
+                y = sbuf("y%d%d" % (first_chunk, piece), [P, tiles * width], F32)
+                rows = out[piece * tiles * P : (piece + 1) * tiles * P, first_chunk * CHUNK : first_chunk * CHUNK + width]
+                if first_chunk == LAST and piece == 0:
+                    nc.vector.tensor_copy(y[:], y_accs[piece][:, 0 : tiles * width])
                 else:
-                    nc.scalar.activation(y[:], y_acc[:, 0 : tiles * width], ACT.Copy)
-                queue = nc.scalar if last and piece == 1 else nc.sync
-                queue.dma_start(rows, y[:].rearrange("p (t j) -> p t j", j=width))
+                    nc.scalar.activation(y[:], y_accs[piece][:, 0 : tiles * width], ACT.Copy)
+                queue = nc.scalar if first_chunk == LAST and piece == 1 else nc.sync
+                queue.dma_start(rows.rearrange("(t p) j -> p t j", p=P), y[:].rearrange("p (t j) -> p t j", j=width))
 
         round_w(0)
-        quantize_w(0)
-        gather_words(0, 0, 2, "w_raw01")
-        gather_words(0, 2, 4, "w_bf0")
-        part_words(0, 0, 2)
-        part_words(0, 2, 4)
-        gather_words(1, 0, 2, "w_raw01")
-        gather_words(1, 2, 4, "w_bf0")
-        part_words(1, 0, 2)
-        part_words(1, 2, 4)
-        for ch in range(4):
-            neighbour_pass(ch, 0, 0)
+        quantize_w(0, 0, HALF)
+        gather_words(0, 0, "w_raw00")
+        gather_words(0, 1)
+        for half in range(2):
+            part_words(0, half, parted_tile("parted0%d" % half))
+        gather_words(1, 0, "w_raw00")
+        warm = psum.tile([P, BANK_COLS], F32, name="warm", tag="bank%d" % (BANKS - 1))
+        for n in range(WARM_UPS):
+            nc.tensor.matmul_mx(
+                out=warm[:, 0:HALF],
+                lhsT=table_operand(0, 0, 0),
+                lhsT_scale=w_s[0][:, 0:CHUNK],
+                rhs=w_q[0][:, 0:HALF].bitcast(FP8X4),
+                rhs_scale=w_s[0][:, 0:HALF],
+                start=True,
+                stop=True,
+            )
+        quantize_w(0, HALF, R)
+        gather_words(1, 1, "w_raw01")
+        part_words(1, 0, parted_tile("parted10", "w_bf0"))
+        part_words(1, 1, parted_tile("parted11"))
+        first_sums = [(ch, g) for g in (0, 1) for ch in (0, 1)]
+        for ch, g in first_sums:
+            neighbour_pass(ch, g, 0)
         round_w(1)
-        for ch in (0, 1):
-            neighbour_pass(ch, 1, 0)
-        quantize_w(1)
-        gather_words(2, 0, 2, "w_raw11")
-        gather_words(2, 2, 4, "w_bf1")
-        part_words(2, 0, 2)
-        part_words(2, 2, 4)
-        for g in (0, 1):
-            for ch in (0, 1):
-                neighbour_pass(ch, g, 1)
-        for a in range(PASSES):
-            round_c(a, 0)
-        quantize_c(0)
+        gather_words(2, 0, "w_raw00")
+        quantize_w(1, 0, R)
+        gather_words(2, 1, "w_raw11")
+        parted2 = sbuf("parted2", [P, J // HALF, PASSES, 2 * HALF], U8, "picked_s")
+        for half in range(2):
+            part_words(2, half, parted2[:, half, :, :])
+        for ch, g in first_sums:
+            neighbour_pass(ch, g, 1)
+        round_c(0)
+        quantize_c(0, "parted00")
         for ch in (2, 3):
-            neighbour_pass(ch, 0, 1)
-        firsts.append(sbuf("firsts", [P, 4, R], F32, "c_raw10"))
-        for ch in range(4):
-            take_first(ch)
-        for a in range(PASSES):
-            round_c(a, 1)
-        neighbour_sum(0, 2)
-        neighbour_sum(1, 2)
-        take_max(0, 1)
-        take_max(1, 1)
-        own_sum(0)
-        own_sum(1)
-        take_max(0, 2)
-        take_max(1, 2)
-        neighbour_sum(2, 1)
-        neighbour_sum(3, 1)
-        add_own(0)
-        add_own(1)
+            neighbour_sum(ch, 0)
+        firsts = sbuf("firsts", [P, CHUNKS, R], F32)
+        for ch in range(CHUNKS):
+            best[ch] = firsts[:, ch, :]
+            copy_out(ch, best[ch], sums[ch, 0])
+        round_c(1)
+
+        for ch in (0, 1):
+            neighbour_sum(ch, 2)
+        for ch in (0, 1):
+            take_max(ch, 1)
+        for ch in (0, 1):
+            own_sum(ch)
+        for ch in (0, 1):
+            take_max(ch, 2)
+        for ch in (2, 3):
+            neighbour_sum(ch, 1)
+        for ch in (0, 1):
+            add_own(ch)
         neighbour_sum(2, 2)
-        turn(0)
-        turn(1)
+        for ch in (0, 1):
+            turn(ch)
         neighbour_sum(3, 2)
+
+        take_max(2, 1)
         quantize_c(1)
-        take_max(2, 1, "c_raw11")
-        relu(0, "c_bf0")
-        relu(1)
-        own_sum(2)
-        own_sum(3)
-        take_max(3, 1, "c_bf1")
-        take_max(2, 2)
-        y01 = second_layer((0, 1))
+        h01 = h_tile(0, 2, "c_bf0")
+        for ch in (0, 1):
+            nc.scalar.activation(*turned_pairs(ch, h01[:, ch, :]), ACT.Relu)
+        for ch in (2, 3):
+            own_sum(ch)
+        take_max(3, 1, "c_raw11")
+        take_max(2, 2, "c_bf1")
+        y01 = second_layer(0, 2, h01)
         add_own(2)
         take_max(3, 2, "c_q1")
-        copy_own(3)
+        own_last = sbuf("own_last", [P, R], F32)
+        copy_out(LAST, own_last[:], own[LAST])
         turn(2)
-        turn_own(3)
-        turn(3)
-        relu(2)
-        for piece in y01:
-            store(piece)
-        y2 = second_layer((2,))
-        relu(3)
-        y3 = second_layer((3,))
-        for piece in y2 + y3:
-            store(piece)
+        turned[LAST] = next_bank("turned%d" % LAST)
+        turn_adding(own_last, True)
+        turn_adding(best[LAST], False)
+        h2 = h_tile(2, 1)
+        nc.vector.tensor_scalar(*turned_pairs(2, h2[:, 0, :]), 0.0, None, ALU.max)
+        store(0, 2, y01)
+        y2 = second_layer(2, 1, h2)
+        h3 = h_tile(LAST, 1)
+        nc.scalar.activation(
+            h3[:, 0, :].rearrange("p (j i) -> p j i", i=PACK),
+            turned[LAST][:].rearrange("p (i j) -> p j i", i=PACK),
+            ACT.Relu,
+        )
+        y3 = second_layer(LAST, 1, h3)
+        store(2, 1, y2)
+        store(LAST, 1, y3)

@@ -32,7 +32,6 @@ LAST = CHUNKS - 1
 BANKS = 8
 BANK_COLS = 512
 PIECES = 2
-WARM_UPS = 5
 
 
 def tile_list_pnet_none_kernel(
@@ -293,17 +292,6 @@ def tile_list_pnet_none_kernel(
         for half in range(2):
             part_words(0, half, parted_tile("parted0%d" % half))
         gather_words(1, 0, "w_raw00")
-        warm = psum.tile([P, BANK_COLS], F32, name="warm", tag="bank%d" % (BANKS - 1))
-        for n in range(WARM_UPS):
-            nc.tensor.matmul_mx(
-                out=warm[:, 0:HALF],
-                lhsT=table_operand(0, 0, 0),
-                lhsT_scale=w_s[0][:, 0:CHUNK],
-                rhs=w_q[0][:, 0:HALF].bitcast(FP8X4),
-                rhs_scale=w_s[0][:, 0:HALF],
-                start=True,
-                stop=True,
-            )
         quantize_w(0, HALF, R)
         gather_words(1, 1, "w_raw01")
         part_words(1, 0, parted_tile("parted10", "w_bf0"))

@@ -45,14 +45,21 @@ def tile_list_pnet_none_kernel(
         def sbuf(name, shape, dtype, reuse=None):
             return keep.tile(shape, dtype, name=name, tag=reuse or name, align_bytes=64)
 
-        accumulators = []
+        takes_over = {
+            "sum21": "sum00", "sum31": "sum10", "own0": "sum01", "own1": "sum11", "sum22": "sum20", "sum32": "sum30",
+            "turned0": "sum02", "turned1": "sum12", "own2": "own0", "own3": "own1", "y_acc00": "sum21", "y_acc01": "sum31",
+            "turned2": "turned0", "turned3": "turned1", "y_acc20": "sum22", "y_acc21": "own2", "y_acc30": "own3",
+            "y_acc31": "sum32",
+        }
+        bank_of = {}
 
         def next_bank(name):
-            accumulators.append(name)
-            return psum.tile([P, BANK_COLS], F32, name=name, tag="bank%d" % ((len(accumulators) - 1) % BANKS))
+            bank_of[name] = bank_of[takes_over[name]] if name in takes_over else len(set(bank_of.values()))
+            assert bank_of[name] < BANKS
+            return psum.tile([P, BANK_COLS], F32, name=name, tag="bank%d" % bank_of[name])
 
-        def plane_rows(plane, quad):
-            return plane[QUADRANT * quad : QUADRANT * quad + 4]
+        def plane_rows(plane, r):
+            return plane[r:P:QUADRANT]
 
         def load_raw(name, src, a, half):
             raw = sbuf("%s_raw%d%d" % (name, a, half), [P, PACK, HALF], F32)
@@ -72,12 +79,11 @@ def tile_list_pnet_none_kernel(
         nc.gpsimd.memset(tab_s[QUADRANT : 2 * QUADRANT, :], 0)
 
         w_raw = {(0, 0): load_raw("w", w, 0, 0)}
-        for quad in range(P // QUADRANT):
-            rows = wc_scales[:, 4 * quad : 4 * quad + 4, :].rearrange("a q r -> q a r")
-            nc.sync.dma_start(plane_rows(wc_s, quad), rows.bitcast(I32))
         tab_w = sbuf("tab_w", [P, T], I32)
         nc.sync.dma_start(tab_w[:], tab_words[0].rearrange("p t b -> p (t b)").bitcast(I32))
-        for a, half in ((0, 1), (1, 0), (1, 1)):
+        for r in range(4):
+            nc.sync.dma_start(plane_rows(wc_s, r), wc_scales[:, r:BLOCKS:4, :].rearrange("a q r -> q a r").bitcast(I32))
+        for a, half in ((0, 1), (1, 0)):
             w_raw[a, half] = load_raw("w", w, a, half)
 
         ident = sbuf("ident", [P, P], F32)
@@ -91,25 +97,26 @@ def tile_list_pnet_none_kernel(
         nc.vector.tensor_copy(picked_s[:], tab_s[:].bitcast(U8).indirect(offsets[:]))
 
         def move_scales(a):
-            for quad in range(P // QUADRANT):
-                row = BLOCKS * a + 4 * quad
-                nc.sync.dma_start(plane_rows(tab_planes[a], quad), picked_s[row : row + 4, :].bitcast(I32))
+            for r in range(4):
+                rows = picked_s[BLOCKS * a + r : BLOCKS * (a + 1) : 4, :]
+                nc.sync.dma_start(plane_rows(tab_planes[a], r), rows.bitcast(I32))
 
         move_scales(0)
-        c_raw = {(a, 0): load_raw("c", c, a, 0) for a in range(PASSES)}
+        w_raw[1, 1] = load_raw("w", w, 1, 1)
         move_scales(1)
+        c_raw = {(a, 0): load_raw("c", c, a, 0) for a in range(PASSES)}
         wc_w = sbuf("wc_w", [P, PASSES, R // 2], I32)
         nc.sync.dma_start(wc_w[:], wc_words.rearrange("a p b -> p a b").bitcast(I32))
         for a in range(PASSES):
             c_raw[a, 1] = load_raw("c", c, a, 1)
         wd_w = sbuf("wd_w", [P, N], I32)
         nc.sync.dma_start(wd_w[:], wd_words[0].rearrange("p n b -> p (n b)").bitcast(I32))
-        for quad in range(P // QUADRANT):
-            nc.sync.dma_start(plane_rows(wd_s, quad), wd_scales[0, 4 * quad : 4 * quad + 4, :].bitcast(I32))
+        for r in range(4):
+            nc.sync.dma_start(plane_rows(wd_s, r), wd_scales[0, r:BLOCKS:4, :].bitcast(I32))
 
         def round_and_interleave(raw, grouped):
             dst = grouped.rearrange("p (y x i) -> p y i x", x=4, i=PACK)
-            src = raw[:].rearrange("p i (y x) -> p y i x", x=4)
+            src = raw.rearrange("p i (y x) -> p y i x", x=4)
             nc.scalar.activation(dst, src, ACT.Copy)
 
         w_q = [sbuf("w_q%d" % a, [P, R], U32) for a in range(PASSES)]
@@ -118,25 +125,26 @@ def tile_list_pnet_none_kernel(
 
         def round_w(a):
             for half in range(R // HALF):
-                round_and_interleave(w_raw[a, half], w_bf[a][:, half * HALF * PACK : (half + 1) * HALF * PACK])
+                round_and_interleave(w_raw[a, half][:], w_bf[a][:, half * HALF * PACK : (half + 1) * HALF * PACK])
 
         def quantize_w(a, r0, r1):
             nc.vector.quantize_mx(
                 out=w_q[a][:, r0:r1].bitcast(FP8X4), scales=w_s[a][:, r0:r1], in_=w_bf[a][:, r0 * PACK : r1 * PACK]
             )
 
-        c_bf, c_q = {}, {}
-        c_s = [sbuf("c_s%d" % half, [P, PASSES * HALF], U8) for half in range(J // HALF)]
+        c_width = {0: 2 * CHUNK, 2: CHUNK, 3: CHUNK}
+        c_bf = {ch: sbuf("c_bf%d" % ch, [P, PASSES, width * PACK], BF16) for ch, width in c_width.items()}
+        c_q, c_s = {}, {}
 
-        def round_c(half):
-            c_bf[half] = sbuf("c_bf%d" % half, [P, PASSES, HALF * PACK], BF16)
-            for a in range(PASSES):
-                round_and_interleave(c_raw[a, half], c_bf[half][:, a, :])
+        def round_c(a, group):
+            half, j0 = divmod(group * CHUNK, HALF)
+            round_and_interleave(c_raw[a, half][:, :, j0 : j0 + c_width[group]], c_bf[group][:, a, :])
 
-        def quantize_c(half, reuse=None):
-            c_q[half] = sbuf("c_q%d" % half, [P, PASSES * HALF], U32, reuse)
+        def quantize_c(group, reuse=None):
+            c_q[group] = sbuf("c_q%d" % group, [P, PASSES * c_width[group]], U32, reuse)
+            c_s[group] = sbuf("c_s%d" % group, [P, PASSES * c_width[group]], U8)
             nc.vector.quantize_mx(
-                out=c_q[half][:].bitcast(FP8X4), scales=c_s[half][:], in_=c_bf[half][:].rearrange("p a x -> p (a x)")
+                out=c_q[group][:].bitcast(FP8X4), scales=c_s[group][:], in_=c_bf[group][:].rearrange("p a x -> p (a x)")
             )
 
         pairs, parted = {}, {}
@@ -196,22 +204,23 @@ def tile_list_pnet_none_kernel(
         def copy_out(ch, flat, acc):
             nc.scalar.activation(sbuf_view(ch, flat), psum_view(ch, acc[:]), ACT.Copy)
 
-        def take_max(ch, g, reuse=None):
-            larger = sbuf("max%d%d" % (ch, g), [P, R], F32, reuse)[:]
+        def take_max(ch, g, larger=None):
+            if larger is None:
+                larger = sbuf("max%d%d" % (ch, g), [P, R], F32)[:]
             nc.vector.tensor_tensor(
                 sbuf_view(ch, larger), psum_view(ch, sums[ch, g][:]), sbuf_view(ch, best[ch]), ALU.max
             )
             best[ch] = larger
 
         def own_sum(ch):
-            half, j0 = divmod(ch * CHUNK, HALF)
+            group = max(first for first in c_width if first <= ch)
             own[ch] = next_bank("own%d" % ch)
             for a in range(PASSES):
-                cols = slice(a * HALF + j0, a * HALF + j0 + CHUNK)
+                col = a * c_width[group] + (ch - group) * CHUNK
                 nc.tensor.matmul_mx(
                     out=own[ch][:],
-                    lhsT=c_q[half][:, cols].bitcast(FP8X4),
-                    lhsT_scale=c_s[half][:, cols],
+                    lhsT=c_q[group][:, col : col + CHUNK].bitcast(FP8X4),
+                    lhsT_scale=c_s[group][:, col : col + CHUNK],
                     rhs=wc_w[:, a, :].bitcast(U8).bitcast(FP4X4),
                     rhs_scale=wc_s[:, a, :].bitcast(U8),
                     start=(a == 0),
@@ -291,16 +300,16 @@ def tile_list_pnet_none_kernel(
         gather_words(0, 1)
         for half in range(2):
             part_words(0, half, parted_tile("parted0%d" % half))
-        gather_words(1, 0, "w_raw00")
         quantize_w(0, HALF, R)
-        gather_words(1, 1, "w_raw01")
-        part_words(1, 0, parted_tile("parted10", "w_bf0"))
+        gather_words(1, 0, "w_raw01")
+        gather_words(1, 1, "w_bf0")
+        part_words(1, 0, parted_tile("parted10"))
         part_words(1, 1, parted_tile("parted11"))
         first_sums = [(ch, g) for g in (0, 1) for ch in (0, 1)]
         for ch, g in first_sums:
             neighbour_pass(ch, g, 0)
         round_w(1)
-        gather_words(2, 0, "w_raw00")
+        gather_words(2, 0, "w_raw01")
         quantize_w(1, 0, R)
         gather_words(2, 1, "w_raw11")
         parted2 = sbuf("parted2", [P, J // HALF, PASSES, 2 * HALF], U8, "picked_s")
@@ -308,45 +317,50 @@ def tile_list_pnet_none_kernel(
             part_words(2, half, parted2[:, half, :, :])
         for ch, g in first_sums:
             neighbour_pass(ch, g, 1)
-        round_c(0)
-        quantize_c(0, "parted00")
+        for a in range(PASSES):
+            round_c(a, 0)
+        best[0] = sbuf("first0", [P, R], F32)[:]
+        nc.vector.tensor_copy(sbuf_view(0, best[0]), psum_view(0, sums[0, 0][:]))
         for ch in (2, 3):
             neighbour_sum(ch, 0)
-        firsts = sbuf("firsts", [P, CHUNKS, R], F32)
-        for ch in range(CHUNKS):
-            best[ch] = firsts[:, ch, :]
+        firsts = sbuf("firsts", [P, CHUNKS - 1, R], F32, "c_raw10")
+        for ch in (1, 2, 3):
+            best[ch] = firsts[:, ch - 1, :]
             copy_out(ch, best[ch], sums[ch, 0])
-        round_c(1)
-
+        for a in range(PASSES):
+            for group in (2, 3):
+                round_c(a, group)
         for ch in (0, 1):
             neighbour_sum(ch, 2)
-        for ch in (0, 1):
-            take_max(ch, 1)
+        take_max(0, 1)
+        quantize_c(0)
+        take_max(1, 1)
         for ch in (0, 1):
             own_sum(ch)
-        for ch in (0, 1):
-            take_max(ch, 2)
+        take_max(0, 2, sbuf("max02", [P, R], F32, "c_bf0")[:])
+        take_max(1, 2)
         for ch in (2, 3):
             neighbour_sum(ch, 1)
         for ch in (0, 1):
             add_own(ch)
-        neighbour_sum(2, 2)
+        for ch in (2, 3):
+            neighbour_sum(ch, 2)
         for ch in (0, 1):
             turn(ch)
-        neighbour_sum(3, 2)
-
-        take_max(2, 1)
-        quantize_c(1)
-        h01 = h_tile(0, 2, "c_bf0")
+        for group in (2, 3):
+            quantize_c(group)
+        h01 = h_tile(0, 2, "c_raw11")
         for ch in (0, 1):
             nc.scalar.activation(*turned_pairs(ch, h01[:, ch, :]), ACT.Relu)
         for ch in (2, 3):
             own_sum(ch)
-        take_max(3, 1, "c_raw11")
-        take_max(2, 2, "c_bf1")
+        late = sbuf("late", [P, 2, R], F32, "c_bf2")
+        for ch in (2, 3):
+            take_max(ch, 1, late[:, ch - 2, :])
+        take_max(2, 2)
         y01 = second_layer(0, 2, h01)
         add_own(2)
-        take_max(3, 2, "c_q1")
+        take_max(3, 2, sbuf("max32", [P, R], F32, "c_q2")[:])
         own_last = sbuf("own_last", [P, R], F32)
         copy_out(LAST, own_last[:], own[LAST])
         turn(2)

@@ -28,6 +28,8 @@ LIST_ROWS = 16
 HALF = 256
 CHUNK = 128
 CHUNKS = J // CHUNK
+ADDED = (2,)
+WARM_UPS = 5
 LAST = CHUNKS - 1
 BANKS = 8
 BANK_COLS = 512
@@ -46,7 +48,7 @@ def tile_list_pnet_none_kernel(
             return keep.tile(shape, dtype, name=name, tag=reuse or name, align_bytes=64)
 
         takes_over = {
-            "sum21": "sum00", "sum31": "sum10", "own0": "sum01", "own1": "sum11", "sum22": "sum20", "sum32": "sum30",
+            "sum31": "warm", "sum02": "sum00", "sum12": "sum10", "own0": "sum01", "own1": "sum11", "sum22": "sum20", "sum32": "sum30",
             "turned0": "sum02", "turned1": "sum12", "own2": "own0", "own3": "own1", "y_acc00": "sum21", "y_acc01": "sum31",
             "turned2": "turned0", "turned3": "turned1", "y_acc20": "sum22", "y_acc21": "own2", "y_acc30": "own3",
             "y_acc31": "sum32",
@@ -79,11 +81,11 @@ def tile_list_pnet_none_kernel(
         nc.gpsimd.memset(tab_s[QUADRANT : 2 * QUADRANT, :], 0)
 
         w_raw = {(0, 0): load_raw("w", w, 0, 0)}
-        tab_w = sbuf("tab_w", [P, T], I32)
-        nc.sync.dma_start(tab_w[:], tab_words[0].rearrange("p t b -> p (t b)").bitcast(I32))
         for r in range(4):
             nc.sync.dma_start(plane_rows(wc_s, r), wc_scales[:, r:BLOCKS:4, :].rearrange("a q r -> q a r").bitcast(I32))
-        for a, half in ((0, 1), (1, 0)):
+        tab_w = sbuf("tab_w", [P, T], I32)
+        nc.sync.dma_start(tab_w[:], tab_words[0].rearrange("p t b -> p (t b)").bitcast(I32))
+        for a, half in ((0, 1), (1, 0), (1, 1)):
             w_raw[a, half] = load_raw("w", w, a, half)
 
         ident = sbuf("ident", [P, P], F32)
@@ -91,8 +93,8 @@ def tile_list_pnet_none_kernel(
 
         tab_planes = [sbuf("tab_plane%d" % a, [P, NEIGHBOURS * J // 4], I32) for a in range(PASSES)]
         nc.vector.memset(tab_planes[0][:], 0)
-        nc.gpsimd.memset(tab_planes[1][:], 0)
-        nc.gpsimd.memset(wd_s[:], 0)
+        nc.vector.memset(tab_planes[1][:], 0)
+        nc.vector.memset(wd_s[:], 0)
         picked_s = sbuf("picked_s", [P, NEIGHBOURS * J], U8)
         nc.vector.tensor_copy(picked_s[:], tab_s[:].bitcast(U8).indirect(offsets[:]))
 
@@ -102,9 +104,8 @@ def tile_list_pnet_none_kernel(
                 nc.sync.dma_start(plane_rows(tab_planes[a], r), rows.bitcast(I32))
 
         move_scales(0)
-        w_raw[1, 1] = load_raw("w", w, 1, 1)
-        move_scales(1)
         c_raw = {(a, 0): load_raw("c", c, a, 0) for a in range(PASSES)}
+        move_scales(1)
         wc_w = sbuf("wc_w", [P, PASSES, R // 2], I32)
         nc.sync.dma_start(wc_w[:], wc_words.rearrange("a p b -> p a b").bitcast(I32))
         for a in range(PASSES):
@@ -190,12 +191,12 @@ def tile_list_pnet_none_kernel(
                 neighbour_pass(ch, g, a)
 
         def psum_view(ch, acc):
-            if ch == LAST:
+            if ch in ADDED:
                 return acc.rearrange("j (p i) -> j i p", i=PACK)
             return acc.rearrange("j (p u e) -> j u p e", u=2, e=2)
 
         def sbuf_view(ch, flat):
-            if ch == LAST:
+            if ch in ADDED:
                 return flat.rearrange("j (i p) -> j i p", i=PACK)
             return flat.rearrange("j (u p e) -> j u p e", u=2, e=2)
 
@@ -239,11 +240,11 @@ def tile_list_pnet_none_kernel(
                 words = z[ch][:].bitcast(F32)[:, u * P : (u + 1) * P]
                 nc.tensor.transpose(turned[ch][:, u * P : (u + 1) * P], words, ident[:])
 
-        def turn_adding(flat, opens):
+        def turn_adding(ch, flat, opens):
             for i in range(PACK):
                 cols = slice(i * P, (i + 1) * P)
                 nc.tensor.matmul(
-                    turned[LAST][:, cols],
+                    turned[ch][:, cols],
                     flat[:, cols],
                     ident[:],
                     is_transpose=True,
@@ -287,7 +288,7 @@ def tile_list_pnet_none_kernel(
             for piece in range(PIECES):
                 y = sbuf("y%d%d" % (first_chunk, piece), [P, tiles * width], F32)
                 rows = out[piece * tiles * P : (piece + 1) * tiles * P, first_chunk * CHUNK : first_chunk * CHUNK + width]
-                if first_chunk == LAST and piece == 0:
+                if (first_chunk, piece) in ((0, 0), (2, 1), (LAST, 0)):
                     nc.vector.tensor_copy(y[:], y_accs[piece][:, 0 : tiles * width])
                 else:
                     nc.scalar.activation(y[:], y_accs[piece][:, 0 : tiles * width], ACT.Copy)
@@ -296,6 +297,17 @@ def tile_list_pnet_none_kernel(
 
         round_w(0)
         quantize_w(0, 0, HALF)
+        warm = next_bank("warm")
+        for i in range(WARM_UPS):
+            nc.tensor.matmul_mx(
+                out=warm[:, 0:HALF],
+                lhsT=w_q[0][:, 0:CHUNK].bitcast(FP8X4),
+                lhsT_scale=w_s[0][:, 0:CHUNK],
+                rhs=w_q[0][:, 0:HALF].bitcast(FP8X4),
+                rhs_scale=w_s[0][:, 0:HALF],
+                start=True,
+                stop=True,
+            )
         gather_words(0, 0, "w_raw00")
         gather_words(0, 1)
         for half in range(2):
@@ -305,9 +317,9 @@ def tile_list_pnet_none_kernel(
         gather_words(1, 1, "w_bf0")
         part_words(1, 0, parted_tile("parted10"))
         part_words(1, 1, parted_tile("parted11"))
-        first_sums = [(ch, g) for g in (0, 1) for ch in (0, 1)]
-        for ch, g in first_sums:
-            neighbour_pass(ch, g, 0)
+        for g in (0, 1):
+            for ch in range(CHUNKS):
+                neighbour_pass(ch, g, 0)
         round_w(1)
         gather_words(2, 0, "w_raw01")
         quantize_w(1, 0, R)
@@ -315,68 +327,71 @@ def tile_list_pnet_none_kernel(
         parted2 = sbuf("parted2", [P, J // HALF, PASSES, 2 * HALF], U8, "picked_s")
         for half in range(2):
             part_words(2, half, parted2[:, half, :, :])
-        for ch, g in first_sums:
+        for ch, g in ((0, 0), (1, 0), (0, 1), (1, 1), (2, 0), (3, 0)):
             neighbour_pass(ch, g, 1)
         for a in range(PASSES):
             round_c(a, 0)
-        best[0] = sbuf("first0", [P, R], F32)[:]
-        nc.vector.tensor_copy(sbuf_view(0, best[0]), psum_view(0, sums[0, 0][:]))
-        for ch in (2, 3):
-            neighbour_sum(ch, 0)
-        firsts = sbuf("firsts", [P, CHUNKS - 1, R], F32, "c_raw10")
-        for ch in (1, 2, 3):
-            best[ch] = firsts[:, ch - 1, :]
+        quantize_c(0, "parted00")
+        firsts = sbuf("firsts", [P, CHUNKS, R], F32)
+        for ch in range(CHUNKS):
+            best[ch] = firsts[:, ch, :]
             copy_out(ch, best[ch], sums[ch, 0])
         for a in range(PASSES):
             for group in (2, 3):
                 round_c(a, group)
         for ch in (0, 1):
             neighbour_sum(ch, 2)
-        take_max(0, 1)
-        quantize_c(0)
-        take_max(1, 1)
+        for ch in (0, 1):
+            take_max(ch, 1)
         for ch in (0, 1):
             own_sum(ch)
-        take_max(0, 2, sbuf("max02", [P, R], F32, "c_bf0")[:])
-        take_max(1, 2)
+        for ch in (0, 1):
+            take_max(ch, 2)
         for ch in (2, 3):
-            neighbour_sum(ch, 1)
+            neighbour_pass(ch, 1, 1)
         for ch in (0, 1):
             add_own(ch)
-        for ch in (2, 3):
-            neighbour_sum(ch, 2)
         for ch in (0, 1):
             turn(ch)
         for group in (2, 3):
             quantize_c(group)
-        h01 = h_tile(0, 2, "c_raw11")
+        h01 = h_tile(0, 2, "c_bf0")
         for ch in (0, 1):
             nc.scalar.activation(*turned_pairs(ch, h01[:, ch, :]), ACT.Relu)
-        for ch in (2, 3):
-            own_sum(ch)
-        late = sbuf("late", [P, 2, R], F32, "c_bf2")
-        for ch in (2, 3):
-            take_max(ch, 1, late[:, ch - 2, :])
-        take_max(2, 2)
+        neighbour_sum(2, 2)
+        own_sum(2)
+        neighbour_sum(3, 2)
+        own_sum(3)
+        take_max(2, 1)
+        take_max(3, 1, sbuf("max31", [P, R], F32, "c_bf2")[:])
+        take_max(2, 2, sbuf("max22", [P, R], F32, "c_bf3")[:])
+        own_sb = sbuf("own_sb", [P, R], F32)
+        copy_out(2, own_sb[:], own[2])
+        turned[2] = next_bank("turned2")
+        turn_adding(2, own_sb, True)
+        turn_adding(2, best[2], False)
         y01 = second_layer(0, 2, h01)
-        add_own(2)
-        take_max(3, 2, sbuf("max32", [P, R], F32, "c_q2")[:])
-        own_last = sbuf("own_last", [P, R], F32)
-        copy_out(LAST, own_last[:], own[LAST])
-        turn(2)
-        turned[LAST] = next_bank("turned%d" % LAST)
-        turn_adding(own_last, True)
-        turn_adding(best[LAST], False)
+        larger = sbuf("max32", [P, R], F32, "c_q2")
+        z[LAST] = sbuf("z%d" % LAST, [P, R], BF16)
+        for u in range(2):
+            nc.vector.tensor_tensor(
+                sbuf_view(LAST, larger[:])[:, u], psum_view(LAST, sums[LAST, 2][:])[:, u], sbuf_view(LAST, best[LAST])[:, u], ALU.max
+            )
+        for u in range(2):
+            nc.vector.tensor_tensor(
+                sbuf_view(LAST, z[LAST][:])[:, u], psum_view(LAST, own[LAST][:])[:, u], sbuf_view(LAST, larger[:])[:, u], ALU.add
+            )
+        turn(LAST)
         h2 = h_tile(2, 1)
-        nc.vector.tensor_scalar(*turned_pairs(2, h2[:, 0, :]), 0.0, None, ALU.max)
+        nc.scalar.activation(
+            h2[:, 0, :].rearrange("p (j i) -> p j i", i=PACK),
+            turned[2][:].rearrange("p (i j) -> p j i", i=PACK),
+            ACT.Relu,
+        )
         store(0, 2, y01)
         y2 = second_layer(2, 1, h2)
         h3 = h_tile(LAST, 1)
-        nc.scalar.activation(
-            h3[:, 0, :].rearrange("p (j i) -> p j i", i=PACK),
-            turned[LAST][:].rearrange("p (i j) -> p j i", i=PACK),
-            ACT.Relu,
-        )
+        nc.vector.tensor_scalar(*turned_pairs(LAST, h3[:, 0, :]), 0.0, None, ALU.max)
         y3 = second_layer(LAST, 1, h3)
         store(2, 1, y2)
         store(LAST, 1, y3)

@@ -115,10 +115,13 @@ def tile_list_pnet_none_kernel(
         for r in range(4):
             nc.sync.dma_start(plane_rows(wd_s, r), wd_scales[0, r:BLOCKS:4, :].bitcast(I32))
 
-        def round_and_interleave(raw, grouped):
+        def round_and_interleave(raw, grouped, on_vector=False):
             dst = grouped.rearrange("p (y x i) -> p y i x", x=4, i=PACK)
             src = raw.rearrange("p i (y x) -> p y i x", x=4)
-            nc.scalar.activation(dst, src, ACT.Copy)
+            if on_vector:
+                nc.vector.tensor_copy(dst, src)
+            else:
+                nc.scalar.activation(dst, src, ACT.Copy)
 
         w_q = [sbuf("w_q%d" % a, [P, R], U32) for a in range(PASSES)]
         w_s = [sbuf("w_s%d" % a, [P, R], U8) for a in range(PASSES)]
@@ -297,21 +300,21 @@ def tile_list_pnet_none_kernel(
 
         round_w(0)
         quantize_w(0, 0, HALF)
+        gather_words(0, 0, "w_raw00")
+        gather_words(0, 1)
+        for half in range(2):
+            part_words(0, half, parted_tile("parted0%d" % half))
         warm = next_bank("warm")
         for i in range(WARM_UPS):
             nc.tensor.matmul_mx(
                 out=warm[:, 0:HALF],
-                lhsT=w_q[0][:, 0:CHUNK].bitcast(FP8X4),
+                lhsT=parted[0, 0][:, 0, 0 : 2 * CHUNK].bitcast(FP4X4),
                 lhsT_scale=w_s[0][:, 0:CHUNK],
                 rhs=w_q[0][:, 0:HALF].bitcast(FP8X4),
                 rhs_scale=w_s[0][:, 0:HALF],
                 start=True,
                 stop=True,
             )
-        gather_words(0, 0, "w_raw00")
-        gather_words(0, 1)
-        for half in range(2):
-            part_words(0, half, parted_tile("parted0%d" % half))
         quantize_w(0, HALF, R)
         gather_words(1, 0, "w_raw01")
         gather_words(1, 1, "w_bf0")
@@ -329,8 +332,10 @@ def tile_list_pnet_none_kernel(
             part_words(2, half, parted2[:, half, :, :])
         for ch, g in ((0, 0), (1, 0), (0, 1), (1, 1), (2, 0), (3, 0)):
             neighbour_pass(ch, g, 1)
-        for a in range(PASSES):
-            round_c(a, 0)
+        round_c(0, 0)
+        for ch in (0, 1):
+            cols = slice(ch * CHUNK, (ch + 1) * CHUNK)
+            round_and_interleave(c_raw[1, 0][:, :, cols], c_bf[0][:, 1, ch * R : (ch + 1) * R], ch == 1)
         quantize_c(0, "parted00")
         firsts = sbuf("firsts", [P, CHUNKS, R], F32)
         for ch in range(CHUNKS):

@@ -29,7 +29,7 @@ HALF = 256
 CHUNK = 128
 CHUNKS = J // CHUNK
 ADDED = (2,)
-WARM_UPS = 5
+WARM_UPS = 6
 LAST = CHUNKS - 1
 BANKS = 8
 BANK_COLS = 512
@@ -48,10 +48,10 @@ def tile_list_pnet_none_kernel(
             return keep.tile(shape, dtype, name=name, tag=reuse or name, align_bytes=64)
 
         takes_over = {
-            "sum31": "warm", "sum02": "sum00", "sum12": "sum10", "own0": "sum01", "own1": "sum11", "sum22": "sum20", "sum32": "sum30",
-            "turned0": "sum02", "turned1": "sum12", "own2": "own0", "own3": "own1", "y_acc00": "sum21", "y_acc01": "sum31",
-            "turned2": "turned0", "turned3": "turned1", "y_acc20": "sum22", "y_acc21": "own2", "y_acc30": "own3",
-            "y_acc31": "sum32",
+            "sum31": "warm", "sum02": "sum00", "sum12": "sum10", "own0": "sum01", "own1": "sum11", "sum22": "sum12",
+            "sum32": "own1", "turned0": "sum02", "turned1": "sum20", "own2": "own0", "own3": "sum30",
+            "y_acc00": "sum21", "y_acc01": "sum31", "turned2": "turned0", "turned3": "turned1", "y_acc20": "sum22",
+            "y_acc21": "own2", "y_acc30": "own3", "y_acc31": "sum32",
         }
         bank_of = {}
 
@@ -85,11 +85,12 @@ def tile_list_pnet_none_kernel(
             nc.sync.dma_start(plane_rows(wc_s, r), wc_scales[:, r:BLOCKS:4, :].rearrange("a q r -> q a r").bitcast(I32))
         tab_w = sbuf("tab_w", [P, T], I32)
         nc.sync.dma_start(tab_w[:], tab_words[0].rearrange("p t b -> p (t b)").bitcast(I32))
-        for a, half in ((0, 1), (1, 0), (1, 1)):
+        for a, half in ((0, 1), (1, 0)):
             w_raw[a, half] = load_raw("w", w, a, half)
 
         ident = sbuf("ident", [P, P], F32)
-        make_identity(nc, ident[:])
+        nc.vector.memset(ident[:], 0.0)
+        make_identity(nc, ident[:], nomemset=True)
 
         tab_planes = [sbuf("tab_plane%d" % a, [P, NEIGHBOURS * J // 4], I32) for a in range(PASSES)]
         nc.vector.memset(tab_planes[0][:], 0)
@@ -104,8 +105,10 @@ def tile_list_pnet_none_kernel(
                 nc.sync.dma_start(plane_rows(tab_planes[a], r), rows.bitcast(I32))
 
         move_scales(0)
-        c_raw = {(a, 0): load_raw("c", c, a, 0) for a in range(PASSES)}
+        w_raw[1, 1] = load_raw("w", w, 1, 1)
+        c_raw = {(0, 0): load_raw("c", c, 0, 0)}
         move_scales(1)
+        c_raw[1, 0] = load_raw("c", c, 1, 0)
         wc_w = sbuf("wc_w", [P, PASSES, R // 2], I32)
         nc.sync.dma_start(wc_w[:], wc_words.rearrange("a p b -> p a b").bitcast(I32))
         for a in range(PASSES):
@@ -125,16 +128,22 @@ def tile_list_pnet_none_kernel(
 
         w_q = [sbuf("w_q%d" % a, [P, R], U32) for a in range(PASSES)]
         w_s = [sbuf("w_s%d" % a, [P, R], U8) for a in range(PASSES)]
-        w_bf = [sbuf("w_bf%d" % a, [P, R * PACK], BF16) for a in range(PASSES)]
+        w_bf = {
+            (0, 0): sbuf("w_bf00", [P, HALF * PACK], BF16),
+            (0, HALF): sbuf("w_bf01", [P, HALF * PACK], BF16),
+            (1, 0): sbuf("w_bf1", [P, R * PACK], BF16),
+        }
 
         def round_w(a):
             for half in range(R // HALF):
-                round_and_interleave(w_raw[a, half][:], w_bf[a][:, half * HALF * PACK : (half + 1) * HALF * PACK])
+                if a == 0:
+                    grouped = w_bf[0, half * HALF][:]
+                else:
+                    grouped = w_bf[1, 0][:, half * HALF * PACK : (half + 1) * HALF * PACK]
+                round_and_interleave(w_raw[a, half][:], grouped)
 
         def quantize_w(a, r0, r1):
-            nc.vector.quantize_mx(
-                out=w_q[a][:, r0:r1].bitcast(FP8X4), scales=w_s[a][:, r0:r1], in_=w_bf[a][:, r0 * PACK : r1 * PACK]
-            )
+            nc.vector.quantize_mx(out=w_q[a][:, r0:r1].bitcast(FP8X4), scales=w_s[a][:, r0:r1], in_=w_bf[a, r0][:])
 
         c_width = {0: 2 * CHUNK, 2: CHUNK, 3: CHUNK}
         c_bf = {ch: sbuf("c_bf%d" % ch, [P, PASSES, width * PACK], BF16) for ch, width in c_width.items()}
@@ -153,25 +162,20 @@ def tile_list_pnet_none_kernel(
 
         pairs, parted = {}, {}
 
-        def gather_words(g, half, reuse=None):
-            col = (g * J + half * HALF) // LIST_ROWS
-            pairs[g, half] = sbuf("pairs%d%d" % (g, half), [P, HALF], U32, reuse)
-            nc.vector.tensor_copy(
-                pairs[g, half][:], tab_w[:].bitcast(U32).indirect(offsets[:, col : col + HALF // LIST_ROWS])
-            )
+        def gather_words(g, j0, j1, reuse=None):
+            pairs[g, j0] = sbuf("pairs%d_%d" % (g, j0), [P, j1 - j0], U32, reuse)
+            cols = slice((g * J + j0) // LIST_ROWS, (g * J + j1) // LIST_ROWS)
+            nc.vector.tensor_copy(pairs[g, j0][:], tab_w[:].bitcast(U32).indirect(offsets[:, cols]))
 
-        def parted_tile(name, reuse=None):
-            return sbuf(name, [P, PASSES, 2 * HALF], U8, reuse)[:]
+        def part_words(g, j0, j1):
+            words = pairs[g, j0][:].bitcast(U16).rearrange("p (j a) -> p a j", a=PASSES)
+            nc.vector.tensor_copy(parted[g][:, :, 2 * j0 : 2 * j1].bitcast(U16), words)
 
-        def part_words(g, half, dst):
-            parted[g, half] = dst
-            nc.vector.tensor_copy(
-                dst.bitcast(U16), pairs[g, half][:].bitcast(U16).rearrange("p (j a) -> p a j", a=PASSES)
-            )
+        def parted_tile(g, reuse=None):
+            parted[g] = sbuf("parted%d" % g, [P, PASSES, 2 * J], U8, reuse)
 
         def table_operand(ch, g, a):
-            half, j0 = divmod(ch * CHUNK, HALF)
-            return parted[g, half][:, a, 2 * j0 : 2 * (j0 + CHUNK)].bitcast(FP4X4)
+            return parted[g][:, a, 2 * ch * CHUNK : 2 * (ch + 1) * CHUNK].bitcast(FP4X4)
 
         sums = {}
 
@@ -237,11 +241,11 @@ def tile_list_pnet_none_kernel(
                 sbuf_view(ch, z[ch][:]), psum_view(ch, own[ch][:]), sbuf_view(ch, best[ch]), ALU.add
             )
 
-        def turn(ch):
-            turned[ch] = next_bank("turned%d" % ch)
+        def turn(ch, place):
+            turned[ch] = place
             for u in range(2):
                 words = z[ch][:].bitcast(F32)[:, u * P : (u + 1) * P]
-                nc.tensor.transpose(turned[ch][:, u * P : (u + 1) * P], words, ident[:])
+                nc.tensor.transpose(place[:, u * P : (u + 1) * P], words, ident[:])
 
         def turn_adding(ch, flat, opens):
             for i in range(PACK):
@@ -260,7 +264,7 @@ def tile_list_pnet_none_kernel(
 
         def turned_pairs(ch, flat):
             dst = flat.rearrange("p (j u e) -> p j u e", u=2, e=2)
-            src = turned[ch][:, 0 : 2 * P].bitcast(BF16).rearrange("p (u j e) -> p j u e", u=2, e=2)
+            src = turned[ch].bitcast(BF16).rearrange("p (u j e) -> p j u e", u=2, e=2)
             return dst, src
 
         def second_layer(first_chunk, chunks, h_bf):
@@ -300,15 +304,15 @@ def tile_list_pnet_none_kernel(
 
         round_w(0)
         quantize_w(0, 0, HALF)
-        gather_words(0, 0, "w_raw00")
-        gather_words(0, 1)
-        for half in range(2):
-            part_words(0, half, parted_tile("parted0%d" % half))
+        gather_words(0, 0, J)
+        gather_words(1, 0, HALF)
+        parted_tile(0)
+        part_words(0, 0, J)
         warm = next_bank("warm")
         for i in range(WARM_UPS):
             nc.tensor.matmul_mx(
                 out=warm[:, 0:HALF],
-                lhsT=parted[0, 0][:, 0, 0 : 2 * CHUNK].bitcast(FP4X4),
+                lhsT=w_q[0][:, 0:CHUNK].bitcast(FP8X4),
                 lhsT_scale=w_s[0][:, 0:CHUNK],
                 rhs=w_q[0][:, 0:HALF].bitcast(FP8X4),
                 rhs_scale=w_s[0][:, 0:HALF],
@@ -316,38 +320,41 @@ def tile_list_pnet_none_kernel(
                 stop=True,
             )
         quantize_w(0, HALF, R)
-        gather_words(1, 0, "w_raw01")
-        gather_words(1, 1, "w_bf0")
-        part_words(1, 0, parted_tile("parted10"))
-        part_words(1, 1, parted_tile("parted11"))
+        gather_words(1, HALF, J, "w_raw01")
+        parted_tile(1, "w_bf01")
+        part_words(1, 0, HALF)
+        part_words(1, HALF, J)
+        opened = ((0, 0), (1, 0), (0, 1), (1, 1), (2, 0), (3, 0))
         for g in (0, 1):
             for ch in range(CHUNKS):
                 neighbour_pass(ch, g, 0)
         round_w(1)
-        gather_words(2, 0, "w_raw01")
+        gather_words(2, 0, HALF, "pairs1_0")
         quantize_w(1, 0, R)
-        gather_words(2, 1, "w_raw11")
-        parted2 = sbuf("parted2", [P, J // HALF, PASSES, 2 * HALF], U8, "picked_s")
-        for half in range(2):
-            part_words(2, half, parted2[:, half, :, :])
-        for ch, g in ((0, 0), (1, 0), (0, 1), (1, 1), (2, 0), (3, 0)):
+        gather_words(2, HALF, J, "w_raw11")
+        parted_tile(2, "picked_s")
+        part_words(2, 0, HALF)
+        part_words(2, HALF, J)
+        for ch, g in opened:
             neighbour_pass(ch, g, 1)
         round_c(0, 0)
-        for ch in (0, 1):
-            cols = slice(ch * CHUNK, (ch + 1) * CHUNK)
-            round_and_interleave(c_raw[1, 0][:, :, cols], c_bf[0][:, 1, ch * R : (ch + 1) * R], ch == 1)
-        quantize_c(0, "parted00")
+        round_and_interleave(c_raw[1, 0][:, :, CHUNK:HALF], c_bf[0][:, 1, R : 2 * R], True)
         firsts = sbuf("firsts", [P, CHUNKS, R], F32)
         for ch in range(CHUNKS):
             best[ch] = firsts[:, ch, :]
+        for ch in (0, 1):
+            copy_out(ch, best[ch], sums[ch, 0])
+        round_and_interleave(c_raw[1, 0][:, :, 0:CHUNK], c_bf[0][:, 1, 0:R])
+        for ch in (2, 3):
             copy_out(ch, best[ch], sums[ch, 0])
         for a in range(PASSES):
             for group in (2, 3):
                 round_c(a, group)
         for ch in (0, 1):
             neighbour_sum(ch, 2)
-        for ch in (0, 1):
-            take_max(ch, 1)
+        take_max(0, 1)
+        take_max(1, 1)
+        quantize_c(0)
         for ch in (0, 1):
             own_sum(ch)
         for ch in (0, 1):
@@ -357,26 +364,27 @@ def tile_list_pnet_none_kernel(
         for ch in (0, 1):
             add_own(ch)
         for ch in (0, 1):
-            turn(ch)
-        for group in (2, 3):
-            quantize_c(group)
+            turn(ch, next_bank("turned%d" % ch)[:, 0 : 2 * P])
         h01 = h_tile(0, 2, "c_bf0")
         for ch in (0, 1):
             nc.scalar.activation(*turned_pairs(ch, h01[:, ch, :]), ACT.Relu)
         neighbour_sum(2, 2)
+        seconds = sbuf("seconds", [P, 2, R], F32, "c_q0")
+        quantize_c(2)
+        take_max(2, 1, seconds[:, 0, :])
+        quantize_c(3)
+        take_max(2, 2)
+        take_max(3, 1, seconds[:, 1, :])
         own_sum(2)
         neighbour_sum(3, 2)
         own_sum(3)
-        take_max(2, 1)
-        take_max(3, 1, sbuf("max31", [P, R], F32, "c_bf2")[:])
-        take_max(2, 2, sbuf("max22", [P, R], F32, "c_bf3")[:])
         own_sb = sbuf("own_sb", [P, R], F32)
         copy_out(2, own_sb[:], own[2])
         turned[2] = next_bank("turned2")
         turn_adding(2, own_sb, True)
         turn_adding(2, best[2], False)
         y01 = second_layer(0, 2, h01)
-        larger = sbuf("max32", [P, R], F32, "c_q2")
+        larger = sbuf("max32", [P, R], F32)
         z[LAST] = sbuf("z%d" % LAST, [P, R], BF16)
         for u in range(2):
             nc.vector.tensor_tensor(
@@ -386,7 +394,7 @@ def tile_list_pnet_none_kernel(
             nc.vector.tensor_tensor(
                 sbuf_view(LAST, z[LAST][:])[:, u], psum_view(LAST, own[LAST][:])[:, u], sbuf_view(LAST, larger[:])[:, u], ALU.add
             )
-        turn(LAST)
+        turn(LAST, next_bank("turned3")[:, 0 : 2 * P])
         h2 = h_tile(2, 1)
         nc.scalar.activation(
             h2[:, 0, :].rearrange("p (j i) -> p j i", i=PACK),

@@ -33,6 +33,8 @@ WARM_UPS = 6
 LAST = CHUNKS - 1
 BANKS = 8
 BANK_COLS = 512
+HALVES = ((0, 2), (2, 2))
+THIRDS = ((0, 1), (1, 1), (2, 2))
 PIECES = 2
 
 
@@ -50,7 +52,7 @@ def tile_list_pnet_none_kernel(
         takes_over = {
             "sum31": "warm", "sum02": "sum00", "sum12": "sum10", "own0": "sum01", "own1": "sum11", "sum22": "sum12",
             "sum32": "own1", "turned0": "sum02", "turned1": "sum20", "own2": "own0", "own3": "sum30",
-            "y_acc00": "sum21", "y_acc01": "sum31", "turned2": "turned0", "turned3": "turned1", "y_acc20": "sum22",
+            "y_acc00": "sum21", "y_acc01": "sum31", "turned2": "turned0", "turned3": "turned1", "y_acc02": "sum22", "y_acc20": "turned2",
             "y_acc21": "own2", "y_acc30": "own3", "y_acc31": "sum32",
         }
         bank_of = {}
@@ -128,22 +130,15 @@ def tile_list_pnet_none_kernel(
 
         w_q = [sbuf("w_q%d" % a, [P, R], U32) for a in range(PASSES)]
         w_s = [sbuf("w_s%d" % a, [P, R], U8) for a in range(PASSES)]
-        w_bf = {
-            (0, 0): sbuf("w_bf00", [P, HALF * PACK], BF16),
-            (0, HALF): sbuf("w_bf01", [P, HALF * PACK], BF16),
-            (1, 0): sbuf("w_bf1", [P, R * PACK], BF16),
-        }
+        w_bf = {key: sbuf("w_bf%d%d" % key, [P, HALF * PACK], BF16) for key in w_raw}
 
         def round_w(a):
             for half in range(R // HALF):
-                if a == 0:
-                    grouped = w_bf[0, half * HALF][:]
-                else:
-                    grouped = w_bf[1, 0][:, half * HALF * PACK : (half + 1) * HALF * PACK]
-                round_and_interleave(w_raw[a, half][:], grouped)
+                round_and_interleave(w_raw[a, half][:], w_bf[a, half][:])
 
-        def quantize_w(a, r0, r1):
-            nc.vector.quantize_mx(out=w_q[a][:, r0:r1].bitcast(FP8X4), scales=w_s[a][:, r0:r1], in_=w_bf[a, r0][:])
+        def quantize_w(a, half):
+            cols = slice(half * HALF, (half + 1) * HALF)
+            nc.vector.quantize_mx(out=w_q[a][:, cols].bitcast(FP8X4), scales=w_s[a][:, cols], in_=w_bf[a, half][:])
 
         c_width = {0: 2 * CHUNK, 2: CHUNK, 3: CHUNK}
         c_bf = {ch: sbuf("c_bf%d" % ch, [P, PASSES, width * PACK], BF16) for ch, width in c_width.items()}
@@ -267,17 +262,16 @@ def tile_list_pnet_none_kernel(
             src = turned[ch].bitcast(BF16).rearrange("p (u j e) -> p j u e", u=2, e=2)
             return dst, src
 
-        def second_layer(first_chunk, chunks, h_bf):
+        def second_layer(first_chunk, chunks, h_bf, pieces):
             width = chunks * CHUNK
             h_q = sbuf("h_q%d" % first_chunk, [P, width], U32)
             h_s = sbuf("h_s%d" % first_chunk, [P, width], U8)
             nc.vector.quantize_mx(out=h_q[:].bitcast(FP8X4), scales=h_s[:], in_=h_bf[:].rearrange("p c x -> p (c x)"))
-            tiles = N // P // PIECES
             y_accs = []
-            for piece in range(PIECES):
+            for piece, (t0, tiles) in enumerate(pieces):
                 y_accs.append(next_bank("y_acc%d%d" % (first_chunk, piece)))
                 for t in range(tiles):
-                    cols = slice((piece * tiles + t) * P, (piece * tiles + t + 1) * P)
+                    cols = slice((t0 + t) * P, (t0 + t + 1) * P)
                     nc.tensor.matmul_mx(
                         out=y_accs[piece][:, t * width : (t + 1) * width],
                         lhsT=wd_w[:, cols].bitcast(FP8X4),
@@ -289,12 +283,11 @@ def tile_list_pnet_none_kernel(
                     )
             return y_accs
 
-        def store(first_chunk, chunks, y_accs):
+        def store(first_chunk, chunks, y_accs, pieces):
             width = chunks * CHUNK
-            tiles = N // P // PIECES
-            for piece in range(PIECES):
+            for piece, (t0, tiles) in enumerate(pieces):
                 y = sbuf("y%d%d" % (first_chunk, piece), [P, tiles * width], F32)
-                rows = out[piece * tiles * P : (piece + 1) * tiles * P, first_chunk * CHUNK : first_chunk * CHUNK + width]
+                rows = out[t0 * P : (t0 + tiles) * P, first_chunk * CHUNK : first_chunk * CHUNK + width]
                 if (first_chunk, piece) in ((0, 0), (2, 1), (LAST, 0)):
                     nc.vector.tensor_copy(y[:], y_accs[piece][:, 0 : tiles * width])
                 else:
@@ -303,7 +296,7 @@ def tile_list_pnet_none_kernel(
                 queue.dma_start(rows.rearrange("(t p) j -> p t j", p=P), y[:].rearrange("p (t j) -> p t j", j=width))
 
         round_w(0)
-        quantize_w(0, 0, HALF)
+        quantize_w(0, 0)
         gather_words(0, 0, J)
         gather_words(1, 0, HALF)
         parted_tile(0)
@@ -319,7 +312,7 @@ def tile_list_pnet_none_kernel(
                 start=True,
                 stop=True,
             )
-        quantize_w(0, HALF, R)
+        quantize_w(0, 1)
         gather_words(1, HALF, J, "w_raw01")
         parted_tile(1, "w_bf01")
         part_words(1, 0, HALF)
@@ -330,7 +323,8 @@ def tile_list_pnet_none_kernel(
                 neighbour_pass(ch, g, 0)
         round_w(1)
         gather_words(2, 0, HALF, "pairs1_0")
-        quantize_w(1, 0, R)
+        quantize_w(1, 0)
+        quantize_w(1, 1)
         gather_words(2, HALF, J, "w_raw11")
         parted_tile(2, "picked_s")
         part_words(2, 0, HALF)
@@ -383,7 +377,7 @@ def tile_list_pnet_none_kernel(
         turned[2] = next_bank("turned2")
         turn_adding(2, own_sb, True)
         turn_adding(2, best[2], False)
-        y01 = second_layer(0, 2, h01)
+        y01 = second_layer(0, 2, h01, THIRDS)
         larger = sbuf("max32", [P, R], F32)
         z[LAST] = sbuf("z%d" % LAST, [P, R], BF16)
         for u in range(2):
@@ -401,10 +395,10 @@ def tile_list_pnet_none_kernel(
             turned[2][:].rearrange("p (i j) -> p j i", i=PACK),
             ACT.Relu,
         )
-        store(0, 2, y01)
-        y2 = second_layer(2, 1, h2)
+        store(0, 2, y01, THIRDS)
+        y2 = second_layer(2, 1, h2, HALVES)
         h3 = h_tile(LAST, 1)
         nc.vector.tensor_scalar(*turned_pairs(LAST, h3[:, 0, :]), 0.0, None, ALU.max)
-        y3 = second_layer(LAST, 1, h3)
-        store(2, 1, y2)
-        store(LAST, 1, y3)
+        y3 = second_layer(LAST, 1, h3, HALVES)
+        store(2, 1, y2, HALVES)
+        store(LAST, 1, y3, HALVES)

@@ -29,12 +29,13 @@ HALF = 256
 CHUNK = 128
 CHUNKS = J // CHUNK
 ADDED = (2,)
-WARM_UPS = 6
+WARM_UPS = 5
 LAST = CHUNKS - 1
 BANKS = 8
 BANK_COLS = 512
 HALVES = ((0, 2), (2, 2))
 THIRDS = ((0, 1), (1, 1), (2, 2))
+LAST_PIECES = ((0, 1), (1, 1), (2, 2))
 PIECES = 2
 
 
@@ -53,7 +54,7 @@ def tile_list_pnet_none_kernel(
             "sum31": "warm", "sum02": "sum00", "sum12": "sum10", "own0": "sum01", "own1": "sum11", "sum22": "sum12",
             "sum32": "own1", "turned0": "sum02", "turned1": "sum20", "own2": "own0", "own3": "sum30",
             "y_acc00": "sum21", "y_acc01": "sum31", "turned2": "turned0", "turned3": "turned1", "y_acc02": "sum22", "y_acc20": "turned2",
-            "y_acc21": "own2", "y_acc30": "own3", "y_acc31": "sum32",
+            "y_acc21": "own2", "y_acc30": "own3", "y_acc31": "sum32", "y_acc32": "y_acc00",
         }
         bank_of = {}
 
@@ -87,7 +88,7 @@ def tile_list_pnet_none_kernel(
             nc.sync.dma_start(plane_rows(wc_s, r), wc_scales[:, r:BLOCKS:4, :].rearrange("a q r -> q a r").bitcast(I32))
         tab_w = sbuf("tab_w", [P, T], I32)
         nc.sync.dma_start(tab_w[:], tab_words[0].rearrange("p t b -> p (t b)").bitcast(I32))
-        for a, half in ((0, 1), (1, 0)):
+        for a, half in ((0, 1), (1, 0), (1, 1)):
             w_raw[a, half] = load_raw("w", w, a, half)
 
         ident = sbuf("ident", [P, P], F32)
@@ -107,10 +108,8 @@ def tile_list_pnet_none_kernel(
                 nc.sync.dma_start(plane_rows(tab_planes[a], r), rows.bitcast(I32))
 
         move_scales(0)
-        w_raw[1, 1] = load_raw("w", w, 1, 1)
-        c_raw = {(0, 0): load_raw("c", c, 0, 0)}
+        c_raw = {(a, 0): load_raw("c", c, a, 0) for a in range(PASSES)}
         move_scales(1)
-        c_raw[1, 0] = load_raw("c", c, 1, 0)
         wc_w = sbuf("wc_w", [P, PASSES, R // 2], I32)
         nc.sync.dma_start(wc_w[:], wc_words.rearrange("a p b -> p a b").bitcast(I32))
         for a in range(PASSES):
@@ -288,7 +287,7 @@ def tile_list_pnet_none_kernel(
             for piece, (t0, tiles) in enumerate(pieces):
                 y = sbuf("y%d%d" % (first_chunk, piece), [P, tiles * width], F32)
                 rows = out[t0 * P : (t0 + tiles) * P, first_chunk * CHUNK : first_chunk * CHUNK + width]
-                if (first_chunk, piece) in ((0, 0), (2, 1), (LAST, 0)):
+                if (first_chunk, piece) in ((0, 0), (2, 1), (LAST, 0), (LAST, 2)):
                     nc.vector.tensor_copy(y[:], y_accs[piece][:, 0 : tiles * width])
                 else:
                     nc.scalar.activation(y[:], y_accs[piece][:, 0 : tiles * width], ACT.Copy)
@@ -305,7 +304,7 @@ def tile_list_pnet_none_kernel(
         for i in range(WARM_UPS):
             nc.tensor.matmul_mx(
                 out=warm[:, 0:HALF],
-                lhsT=w_q[0][:, 0:CHUNK].bitcast(FP8X4),
+                lhsT=table_operand(0, 0, 0),
                 lhsT_scale=w_s[0][:, 0:CHUNK],
                 rhs=w_q[0][:, 0:HALF].bitcast(FP8X4),
                 rhs_scale=w_s[0][:, 0:HALF],
@@ -326,7 +325,7 @@ def tile_list_pnet_none_kernel(
         quantize_w(1, 0)
         quantize_w(1, 1)
         gather_words(2, HALF, J, "w_raw11")
-        parted_tile(2, "picked_s")
+        parted_tile(2, "w_bf11")
         part_words(2, 0, HALF)
         part_words(2, HALF, J)
         for ch, g in opened:
@@ -336,19 +335,17 @@ def tile_list_pnet_none_kernel(
         firsts = sbuf("firsts", [P, CHUNKS, R], F32)
         for ch in range(CHUNKS):
             best[ch] = firsts[:, ch, :]
-        for ch in (0, 1):
-            copy_out(ch, best[ch], sums[ch, 0])
         round_and_interleave(c_raw[1, 0][:, :, 0:CHUNK], c_bf[0][:, 1, 0:R])
-        for ch in (2, 3):
+        for ch in range(CHUNKS):
             copy_out(ch, best[ch], sums[ch, 0])
         for a in range(PASSES):
             for group in (2, 3):
                 round_c(a, group)
         for ch in (0, 1):
             neighbour_sum(ch, 2)
+        quantize_c(0)
         take_max(0, 1)
         take_max(1, 1)
-        quantize_c(0)
         for ch in (0, 1):
             own_sum(ch)
         for ch in (0, 1):
@@ -399,6 +396,6 @@ def tile_list_pnet_none_kernel(
         y2 = second_layer(2, 1, h2, HALVES)
         h3 = h_tile(LAST, 1)
         nc.vector.tensor_scalar(*turned_pairs(LAST, h3[:, 0, :]), 0.0, None, ALU.max)
-        y3 = second_layer(LAST, 1, h3, HALVES)
+        y3 = second_layer(LAST, 1, h3, LAST_PIECES)
         store(2, 1, y2, HALVES)
-        store(LAST, 1, y3, HALVES)
+        store(LAST, 1, y3, LAST_PIECES)

@@ -28,15 +28,14 @@ LIST_ROWS = 16
 HALF = 256
 CHUNK = 128
 CHUNKS = J // CHUNK
-ADDED = (2,)
-WARM_UPS = 5
+ADDED = 2
 LAST = CHUNKS - 1
+WARM_UPS = 7
 BANKS = 8
 BANK_COLS = 512
-HALVES = ((0, 2), (2, 2))
-THIRDS = ((0, 1), (1, 1), (2, 2))
-LAST_PIECES = ((0, 1), (1, 1), (2, 2))
-PIECES = 2
+TWO_PIECES = ((0, 2), (2, 2))
+THREE_PIECES = ((0, 1), (1, 1), (2, 2))
+VECTOR_PIECES = ((0, 0), (2, 1), (LAST, 0), (LAST, 2))
 
 
 def tile_list_pnet_none_kernel(
@@ -51,10 +50,13 @@ def tile_list_pnet_none_kernel(
             return keep.tile(shape, dtype, name=name, tag=reuse or name, align_bytes=64)
 
         takes_over = {
-            "sum31": "warm", "sum02": "sum00", "sum12": "sum10", "own0": "sum01", "own1": "sum11", "sum22": "sum12",
-            "sum32": "own1", "turned0": "sum02", "turned1": "sum20", "own2": "own0", "own3": "sum30",
-            "y_acc00": "sum21", "y_acc01": "sum31", "turned2": "turned0", "turned3": "turned1", "y_acc02": "sum22", "y_acc20": "turned2",
-            "y_acc21": "own2", "y_acc30": "own3", "y_acc31": "sum32", "y_acc32": "y_acc00",
+            "sum31": "warm",
+            "sum02": "sum00", "sum12": "sum10", "sum22": "sum12", "sum32": "own1",
+            "own0": "sum01", "own1": "sum11", "own2": "own0", "own3": "sum30",
+            "turned0": "sum02", "turned1": "sum20", "turned2": "turned0", "turned3": "turned1",
+            "y_acc00": "sum21", "y_acc01": "sum31", "y_acc02": "sum22",
+            "y_acc20": "turned2", "y_acc21": "own2",
+            "y_acc30": "own3", "y_acc31": "sum32", "y_acc32": "y_acc00",
         }
         bank_of = {}
 
@@ -147,8 +149,8 @@ def tile_list_pnet_none_kernel(
             half, j0 = divmod(group * CHUNK, HALF)
             round_and_interleave(c_raw[a, half][:, :, j0 : j0 + c_width[group]], c_bf[group][:, a, :])
 
-        def quantize_c(group, reuse=None):
-            c_q[group] = sbuf("c_q%d" % group, [P, PASSES * c_width[group]], U32, reuse)
+        def quantize_c(group):
+            c_q[group] = sbuf("c_q%d" % group, [P, PASSES * c_width[group]], U32)
             c_s[group] = sbuf("c_s%d" % group, [P, PASSES * c_width[group]], U8)
             nc.vector.quantize_mx(
                 out=c_q[group][:].bitcast(FP8X4), scales=c_s[group][:], in_=c_bf[group][:].rearrange("p a x -> p (a x)")
@@ -192,12 +194,12 @@ def tile_list_pnet_none_kernel(
                 neighbour_pass(ch, g, a)
 
         def psum_view(ch, acc):
-            if ch in ADDED:
+            if ch == ADDED:
                 return acc.rearrange("j (p i) -> j i p", i=PACK)
             return acc.rearrange("j (p u e) -> j u p e", u=2, e=2)
 
         def sbuf_view(ch, flat):
-            if ch in ADDED:
+            if ch == ADDED:
                 return flat.rearrange("j (i p) -> j i p", i=PACK)
             return flat.rearrange("j (u p e) -> j u p e", u=2, e=2)
 
@@ -235,11 +237,11 @@ def tile_list_pnet_none_kernel(
                 sbuf_view(ch, z[ch][:]), psum_view(ch, own[ch][:]), sbuf_view(ch, best[ch]), ALU.add
             )
 
-        def turn(ch, place):
-            turned[ch] = place
+        def turn(ch):
+            turned[ch] = next_bank("turned%d" % ch)[:, 0 : 2 * P]
             for u in range(2):
                 words = z[ch][:].bitcast(F32)[:, u * P : (u + 1) * P]
-                nc.tensor.transpose(place[:, u * P : (u + 1) * P], words, ident[:])
+                nc.tensor.transpose(turned[ch][:, u * P : (u + 1) * P], words, ident[:])
 
         def turn_adding(ch, flat, opens):
             for i in range(PACK):
@@ -287,11 +289,12 @@ def tile_list_pnet_none_kernel(
             for piece, (t0, tiles) in enumerate(pieces):
                 y = sbuf("y%d%d" % (first_chunk, piece), [P, tiles * width], F32)
                 rows = out[t0 * P : (t0 + tiles) * P, first_chunk * CHUNK : first_chunk * CHUNK + width]
-                if (first_chunk, piece) in ((0, 0), (2, 1), (LAST, 0), (LAST, 2)):
+                on_vector = (first_chunk, piece) in VECTOR_PIECES
+                if on_vector:
                     nc.vector.tensor_copy(y[:], y_accs[piece][:, 0 : tiles * width])
                 else:
                     nc.scalar.activation(y[:], y_accs[piece][:, 0 : tiles * width], ACT.Copy)
-                queue = nc.scalar if first_chunk == LAST and piece == 1 else nc.sync
+                queue = nc.scalar if first_chunk == LAST and not on_vector else nc.sync
                 queue.dma_start(rows.rearrange("(t p) j -> p t j", p=P), y[:].rearrange("p (t j) -> p t j", j=width))
 
         round_w(0)
@@ -301,10 +304,10 @@ def tile_list_pnet_none_kernel(
         parted_tile(0)
         part_words(0, 0, J)
         warm = next_bank("warm")
-        for i in range(WARM_UPS):
+        for _ in range(WARM_UPS):
             nc.tensor.matmul_mx(
                 out=warm[:, 0:HALF],
-                lhsT=table_operand(0, 0, 0),
+                lhsT=pairs[0, 0][:].bitcast(U8)[:, 0 : 2 * CHUNK].bitcast(FP4X4),
                 lhsT_scale=w_s[0][:, 0:CHUNK],
                 rhs=w_q[0][:, 0:HALF].bitcast(FP8X4),
                 rhs_scale=w_s[0][:, 0:HALF],
@@ -316,7 +319,6 @@ def tile_list_pnet_none_kernel(
         parted_tile(1, "w_bf01")
         part_words(1, 0, HALF)
         part_words(1, HALF, J)
-        opened = ((0, 0), (1, 0), (0, 1), (1, 1), (2, 0), (3, 0))
         for g in (0, 1):
             for ch in range(CHUNKS):
                 neighbour_pass(ch, g, 0)
@@ -328,15 +330,18 @@ def tile_list_pnet_none_kernel(
         parted_tile(2, "w_bf11")
         part_words(2, 0, HALF)
         part_words(2, HALF, J)
-        for ch, g in opened:
-            neighbour_pass(ch, g, 1)
+
+        for g in (0, 1):
+            for ch in (0, 1):
+                neighbour_pass(ch, g, 1)
+        for ch in (2, 3):
+            neighbour_pass(ch, 0, 1)
         round_c(0, 0)
-        round_and_interleave(c_raw[1, 0][:, :, CHUNK:HALF], c_bf[0][:, 1, R : 2 * R], True)
+        round_and_interleave(c_raw[1, 0][:, :, CHUNK:HALF], c_bf[0][:, 1, CHUNK * PACK : HALF * PACK], on_vector=True)
+        round_and_interleave(c_raw[1, 0][:, :, 0:CHUNK], c_bf[0][:, 1, 0 : CHUNK * PACK])
         firsts = sbuf("firsts", [P, CHUNKS, R], F32)
         for ch in range(CHUNKS):
             best[ch] = firsts[:, ch, :]
-        round_and_interleave(c_raw[1, 0][:, :, 0:CHUNK], c_bf[0][:, 1, 0:R])
-        for ch in range(CHUNKS):
             copy_out(ch, best[ch], sums[ch, 0])
         for a in range(PASSES):
             for group in (2, 3):
@@ -344,8 +349,8 @@ def tile_list_pnet_none_kernel(
         for ch in (0, 1):
             neighbour_sum(ch, 2)
         quantize_c(0)
-        take_max(0, 1)
-        take_max(1, 1)
+        for ch in (0, 1):
+            take_max(ch, 1)
         for ch in (0, 1):
             own_sum(ch)
         for ch in (0, 1):
@@ -355,10 +360,11 @@ def tile_list_pnet_none_kernel(
         for ch in (0, 1):
             add_own(ch)
         for ch in (0, 1):
-            turn(ch, next_bank("turned%d" % ch)[:, 0 : 2 * P])
+            turn(ch)
         h01 = h_tile(0, 2, "c_bf0")
         for ch in (0, 1):
             nc.scalar.activation(*turned_pairs(ch, h01[:, ch, :]), ACT.Relu)
+
         neighbour_sum(2, 2)
         seconds = sbuf("seconds", [P, 2, R], F32, "c_q0")
         quantize_c(2)
@@ -370,32 +376,30 @@ def tile_list_pnet_none_kernel(
         neighbour_sum(3, 2)
         own_sum(3)
         own_sb = sbuf("own_sb", [P, R], F32)
-        copy_out(2, own_sb[:], own[2])
-        turned[2] = next_bank("turned2")
-        turn_adding(2, own_sb, True)
-        turn_adding(2, best[2], False)
-        y01 = second_layer(0, 2, h01, THIRDS)
+        copy_out(ADDED, own_sb[:], own[ADDED])
+        turned[ADDED] = next_bank("turned%d" % ADDED)
+        turn_adding(ADDED, own_sb, True)
+        turn_adding(ADDED, best[ADDED], False)
+        y01 = second_layer(0, 2, h01, THREE_PIECES)
         larger = sbuf("max32", [P, R], F32)
         z[LAST] = sbuf("z%d" % LAST, [P, R], BF16)
-        for u in range(2):
-            nc.vector.tensor_tensor(
-                sbuf_view(LAST, larger[:])[:, u], psum_view(LAST, sums[LAST, 2][:])[:, u], sbuf_view(LAST, best[LAST])[:, u], ALU.max
-            )
-        for u in range(2):
-            nc.vector.tensor_tensor(
-                sbuf_view(LAST, z[LAST][:])[:, u], psum_view(LAST, own[LAST][:])[:, u], sbuf_view(LAST, larger[:])[:, u], ALU.add
-            )
-        turn(LAST, next_bank("turned3")[:, 0 : 2 * P])
-        h2 = h_tile(2, 1)
+        steps = ((larger, sums[LAST, 2], best[LAST], ALU.max), (z[LAST], own[LAST], larger[:], ALU.add))
+        for result, acc, other, op in steps:
+            for u in range(2):
+                nc.vector.tensor_tensor(
+                    sbuf_view(LAST, result[:])[:, u], psum_view(LAST, acc[:])[:, u], sbuf_view(LAST, other)[:, u], op
+                )
+        turn(LAST)
+        h2 = h_tile(ADDED, 1)
         nc.scalar.activation(
             h2[:, 0, :].rearrange("p (j i) -> p j i", i=PACK),
-            turned[2][:].rearrange("p (i j) -> p j i", i=PACK),
+            turned[ADDED][:].rearrange("p (i j) -> p j i", i=PACK),
             ACT.Relu,
         )
-        store(0, 2, y01, THIRDS)
-        y2 = second_layer(2, 1, h2, HALVES)
+        store(0, 2, y01, THREE_PIECES)
+        y2 = second_layer(ADDED, 1, h2, TWO_PIECES)
         h3 = h_tile(LAST, 1)
         nc.vector.tensor_scalar(*turned_pairs(LAST, h3[:, 0, :]), 0.0, None, ALU.max)
-        y3 = second_layer(LAST, 1, h3, LAST_PIECES)
-        store(2, 1, y2, HALVES)
-        store(LAST, 1, y3, LAST_PIECES)
+        y3 = second_layer(LAST, 1, h3, THREE_PIECES)
+        store(ADDED, 1, y2, TWO_PIECES)
+        store(LAST, 1, y3, THREE_PIECES)

from contextlib import ExitStack

import concourse.mybir as mybir
from concourse.masks import make_identity

K, R, N, T, J = 1024, 512, 512, 2048, 512
NEIGHBOURS = 3
FLOPS = 2 * K * R * J * (NEIGHBOURS + 1) + 2 * R * N * J

F32 = mybir.dt.float32
BF16 = mybir.dt.bfloat16
I32 = mybir.dt.int32
U32 = mybir.dt.uint32
U16 = mybir.dt.uint16
U8 = mybir.dt.uint8
FP8X4 = mybir.dt.float8_e4m3fn_x4
FP4X4 = mybir.dt.float4_e2m1fn_x4
ACT = mybir.ActivationFunctionType
ALU = mybir.AluOpType

P = 128
PACK = 4
K_PASS = P * PACK
PASSES = K // K_PASS
BLOCKS = K_PASS // 32
QUADRANT = 32
LIST_ROWS = 16
HALF = 256
CHUNK = 128
CHUNKS = J // CHUNK
ADDED = 2
LAST = CHUNKS - 1
WARM_UPS = 7
BANKS = 8
BANK_COLS = 512
TWO_PIECES = ((0, 2), (2, 2))
THREE_PIECES = ((0, 1), (1, 1), (2, 2))
VECTOR_PIECES = ((0, 0), (2, 1), (LAST, 0), (LAST, 2))


def tile_list_pnet_none_kernel(
    tc, tab_words, tab_scales, c, w, wc_words, wc_scales, wd_words, wd_scales, offs, out
):
    nc = tc.nc
    with ExitStack() as ctx:
        keep = ctx.enter_context(tc.tile_pool(name="keep", bufs=1))
        psum = ctx.enter_context(tc.psum_pool(name="psum", bufs=1))

        def sbuf(name, shape, dtype, reuse=None):
            return keep.tile(shape, dtype, name=name, tag=reuse or name, align_bytes=64)

        takes_over = {
            "sum31": "warm",
            "sum02": "sum00", "sum12": "sum10", "sum22": "sum12", "sum32": "own1",
            "own0": "sum01", "own1": "sum11", "own2": "own0", "own3": "sum30",
            "turned0": "sum02", "turned1": "sum20", "turned2": "turned0", "turned3": "turned1",
            "y_acc00": "sum21", "y_acc01": "sum31", "y_acc02": "sum22",
            "y_acc20": "turned2", "y_acc21": "own2",
            "y_acc30": "own3", "y_acc31": "sum32", "y_acc32": "y_acc00",
        }
        bank_of = {}

        def next_bank(name):
            bank_of[name] = bank_of[takes_over[name]] if name in takes_over else len(set(bank_of.values()))
            assert bank_of[name] < BANKS
            return psum.tile([P, BANK_COLS], F32, name=name, tag="bank%d" % bank_of[name])

        def plane_rows(plane, r):
            return plane[r:P:QUADRANT]

        def load_raw(name, src, a, half):
            raw = sbuf("%s_raw%d%d" % (name, a, half), [P, PACK, HALF], F32)
            rows = src[a * K_PASS : (a + 1) * K_PASS, half * HALF : (half + 1) * HALF]
            nc.sync.dma_start(raw[:], rows.rearrange("(p i) x -> p i x", i=PACK))
            return raw

        offsets = keep.tile([P, NEIGHBOURS * J // LIST_ROWS], U16, name="offsets")
        nc.sync.dma_start(offsets[:], offs)

        tab_s = sbuf("tab_s", [P, T // 4], I32)
        nc.sync.dma_start(tab_s[0:QUADRANT, :], tab_scales.rearrange("a q t -> (a q) t").bitcast(I32))
        wc_s = sbuf("wc_s", [P, PASSES, R // 4], I32)
        wd_s = sbuf("wd_s", [P, N // 4], I32)
        nc.vector.memset(wc_s[:], 0)
        nc.vector.memset(tab_s[2 * QUADRANT : P, :], 0)
        nc.gpsimd.memset(tab_s[QUADRANT : 2 * QUADRANT, :], 0)

        w_raw = {(0, 0): load_raw("w", w, 0, 0)}
        for r in range(4):
            nc.sync.dma_start(plane_rows(wc_s, r), wc_scales[:, r:BLOCKS:4, :].rearrange("a q r -> q a r").bitcast(I32))
        tab_w = sbuf("tab_w", [P, T], I32)
        nc.sync.dma_start(tab_w[:], tab_words[0].rearrange("p t b -> p (t b)").bitcast(I32))
        for a, half in ((0, 1), (1, 0), (1, 1)):
            w_raw[a, half] = load_raw("w", w, a, half)

        ident = sbuf("ident", [P, P], F32)
        nc.vector.memset(ident[:], 0.0)
        make_identity(nc, ident[:], nomemset=True)

        tab_planes = [sbuf("tab_plane%d" % a, [P, NEIGHBOURS * J // 4], I32) for a in range(PASSES)]
        nc.vector.memset(tab_planes[0][:], 0)
        nc.vector.memset(tab_planes[1][:], 0)
        nc.vector.memset(wd_s[:], 0)
        picked_s = sbuf("picked_s", [P, NEIGHBOURS * J], U8)
        nc.vector.tensor_copy(picked_s[:], tab_s[:].bitcast(U8).indirect(offsets[:]))

        def move_scales(a):
            for r in range(4):
                rows = picked_s[BLOCKS * a + r : BLOCKS * (a + 1) : 4, :]
                nc.sync.dma_start(plane_rows(tab_planes[a], r), rows.bitcast(I32))

        move_scales(0)
        c_raw = {(a, 0): load_raw("c", c, a, 0) for a in range(PASSES)}
        move_scales(1)
        wc_w = sbuf("wc_w", [P, PASSES, R // 2], I32)
        nc.sync.dma_start(wc_w[:], wc_words.rearrange("a p b -> p a b").bitcast(I32))
        for a in range(PASSES):
            c_raw[a, 1] = load_raw("c", c, a, 1)
        wd_w = sbuf("wd_w", [P, N], I32)
        nc.sync.dma_start(wd_w[:], wd_words[0].rearrange("p n b -> p (n b)").bitcast(I32))
        for r in range(4):
            nc.sync.dma_start(plane_rows(wd_s, r), wd_scales[0, r:BLOCKS:4, :].bitcast(I32))

        def round_and_interleave(raw, grouped, on_vector=False):
            dst = grouped.rearrange("p (y x i) -> p y i x", x=4, i=PACK)
            src = raw.rearrange("p i (y x) -> p y i x", x=4)
            if on_vector:
                nc.vector.tensor_copy(dst, src)
            else:
                nc.scalar.activation(dst, src, ACT.Copy)

        w_q = [sbuf("w_q%d" % a, [P, R], U32) for a in range(PASSES)]
        w_s = [sbuf("w_s%d" % a, [P, R], U8) for a in range(PASSES)]
        w_bf = {key: sbuf("w_bf%d%d" % key, [P, HALF * PACK], BF16) for key in w_raw}

        def round_w(a):
            for half in range(R // HALF):
                round_and_interleave(w_raw[a, half][:], w_bf[a, half][:])

        def quantize_w(a, half):
            cols = slice(half * HALF, (half + 1) * HALF)
            nc.vector.quantize_mx(out=w_q[a][:, cols].bitcast(FP8X4), scales=w_s[a][:, cols], in_=w_bf[a, half][:])

        c_width = {0: 2 * CHUNK, 2: CHUNK, 3: CHUNK}
        c_bf = {ch: sbuf("c_bf%d" % ch, [P, PASSES, width * PACK], BF16) for ch, width in c_width.items()}
        c_q, c_s = {}, {}

        def round_c(a, group):
            half, j0 = divmod(group * CHUNK, HALF)
            round_and_interleave(c_raw[a, half][:, :, j0 : j0 + c_width[group]], c_bf[group][:, a, :])

        def quantize_c(group):
            c_q[group] = sbuf("c_q%d" % group, [P, PASSES * c_width[group]], U32)
            c_s[group] = sbuf("c_s%d" % group, [P, PASSES * c_width[group]], U8)
            nc.vector.quantize_mx(
                out=c_q[group][:].bitcast(FP8X4), scales=c_s[group][:], in_=c_bf[group][:].rearrange("p a x -> p (a x)")
            )

        pairs, parted = {}, {}

        def gather_words(g, j0, j1, reuse=None):
            pairs[g, j0] = sbuf("pairs%d_%d" % (g, j0), [P, j1 - j0], U32, reuse)
            cols = slice((g * J + j0) // LIST_ROWS, (g * J + j1) // LIST_ROWS)
            nc.vector.tensor_copy(pairs[g, j0][:], tab_w[:].bitcast(U32).indirect(offsets[:, cols]))

        def part_words(g, j0, j1):
            words = pairs[g, j0][:].bitcast(U16).rearrange("p (j a) -> p a j", a=PASSES)
            nc.vector.tensor_copy(parted[g][:, :, 2 * j0 : 2 * j1].bitcast(U16), words)

        def parted_tile(g, reuse=None):
            parted[g] = sbuf("parted%d" % g, [P, PASSES, 2 * J], U8, reuse)

        def table_operand(ch, g, a):
            return parted[g][:, a, 2 * ch * CHUNK : 2 * (ch + 1) * CHUNK].bitcast(FP4X4)

        sums = {}

        def neighbour_pass(ch, g, a):
            if a == 0:
                sums[ch, g] = next_bank("sum%d%d" % (ch, g))
            m0 = g * J + ch * CHUNK
            nc.tensor.matmul_mx(
                out=sums[ch, g][:],
                lhsT=table_operand(ch, g, a),
                lhsT_scale=tab_planes[a][:].bitcast(U8)[:, m0 : m0 + CHUNK],
                rhs=w_q[a][:].bitcast(FP8X4),
                rhs_scale=w_s[a][:],
                start=(a == 0),
                stop=(a == PASSES - 1),
            )

        def neighbour_sum(ch, g):
            for a in range(PASSES):
                neighbour_pass(ch, g, a)

        def psum_view(ch, acc):
            if ch == ADDED:
                return acc.rearrange("j (p i) -> j i p", i=PACK)
            return acc.rearrange("j (p u e) -> j u p e", u=2, e=2)

        def sbuf_view(ch, flat):
            if ch == ADDED:
                return flat.rearrange("j (i p) -> j i p", i=PACK)
            return flat.rearrange("j (u p e) -> j u p e", u=2, e=2)

        best, own, z, turned = {}, {}, {}, {}

        def copy_out(ch, flat, acc):
            nc.scalar.activation(sbuf_view(ch, flat), psum_view(ch, acc[:]), ACT.Copy)

        def take_max(ch, g, larger=None):
            if larger is None:
                larger = sbuf("max%d%d" % (ch, g), [P, R], F32)[:]
            nc.vector.tensor_tensor(
                sbuf_view(ch, larger), psum_view(ch, sums[ch, g][:]), sbuf_view(ch, best[ch]), ALU.max
            )
            best[ch] = larger

        def own_sum(ch):
            group = max(first for first in c_width if first <= ch)
            own[ch] = next_bank("own%d" % ch)
            for a in range(PASSES):
                col = a * c_width[group] + (ch - group) * CHUNK
                nc.tensor.matmul_mx(
                    out=own[ch][:],
                    lhsT=c_q[group][:, col : col + CHUNK].bitcast(FP8X4),
                    lhsT_scale=c_s[group][:, col : col + CHUNK],
                    rhs=wc_w[:, a, :].bitcast(U8).bitcast(FP4X4),
                    rhs_scale=wc_s[:, a, :].bitcast(U8),
                    start=(a == 0),
                    stop=(a == PASSES - 1),
                )

        def add_own(ch):
            z[ch] = sbuf("z%d" % ch, [P, R], BF16)
            nc.vector.tensor_tensor(
                sbuf_view(ch, z[ch][:]), psum_view(ch, own[ch][:]), sbuf_view(ch, best[ch]), ALU.add
            )

        def turn(ch):
            turned[ch] = next_bank("turned%d" % ch)[:, 0 : 2 * P]
            for u in range(2):
                words = z[ch][:].bitcast(F32)[:, u * P : (u + 1) * P]
                nc.tensor.transpose(turned[ch][:, u * P : (u + 1) * P], words, ident[:])

        def turn_adding(ch, flat, opens):
            for i in range(PACK):
                cols = slice(i * P, (i + 1) * P)
                nc.tensor.matmul(
                    turned[ch][:, cols],
                    flat[:, cols],
                    ident[:],
                    is_transpose=True,
                    start=(opens and i == 0),
                    stop=(not opens and i == PACK - 1),
                )

        def h_tile(first_chunk, chunks, reuse=None):
            return sbuf("h_bf%d" % first_chunk, [P, chunks, CHUNK * PACK], BF16, reuse)

        def turned_pairs(ch, flat):
            dst = flat.rearrange("p (j u e) -> p j u e", u=2, e=2)
            src = turned[ch].bitcast(BF16).rearrange("p (u j e) -> p j u e", u=2, e=2)
            return dst, src

        def second_layer(first_chunk, chunks, h_bf, pieces):
            width = chunks * CHUNK
            h_q = sbuf("h_q%d" % first_chunk, [P, width], U32)
            h_s = sbuf("h_s%d" % first_chunk, [P, width], U8)
            nc.vector.quantize_mx(out=h_q[:].bitcast(FP8X4), scales=h_s[:], in_=h_bf[:].rearrange("p c x -> p (c x)"))
            y_accs = []
            for piece, (t0, tiles) in enumerate(pieces):
                y_accs.append(next_bank("y_acc%d%d" % (first_chunk, piece)))
                for t in range(tiles):
                    cols = slice((t0 + t) * P, (t0 + t + 1) * P)
                    nc.tensor.matmul_mx(
                        out=y_accs[piece][:, t * width : (t + 1) * width],
                        lhsT=wd_w[:, cols].bitcast(FP8X4),
                        lhsT_scale=wd_s[:].bitcast(U8)[:, cols],
                        rhs=h_q[:].bitcast(FP8X4),
                        rhs_scale=h_s[:],
                        start=True,
                        stop=True,
                    )
            return y_accs

        def store(first_chunk, chunks, y_accs, pieces):
            width = chunks * CHUNK
            for piece, (t0, tiles) in enumerate(pieces):
                y = sbuf("y%d%d" % (first_chunk, piece), [P, tiles * width], F32)
                rows = out[t0 * P : (t0 + tiles) * P, first_chunk * CHUNK : first_chunk * CHUNK + width]
                on_vector = (first_chunk, piece) in VECTOR_PIECES
                if on_vector:
                    nc.vector.tensor_copy(y[:], y_accs[piece][:, 0 : tiles * width])
                else:
                    nc.scalar.activation(y[:], y_accs[piece][:, 0 : tiles * width], ACT.Copy)
                queue = nc.scalar if first_chunk == LAST and not on_vector else nc.sync
                queue.dma_start(rows.rearrange("(t p) j -> p t j", p=P), y[:].rearrange("p (t j) -> p t j", j=width))

        round_w(0)
        quantize_w(0, 0)
        gather_words(0, 0, J)
        gather_words(1, 0, HALF)
        parted_tile(0)
        part_words(0, 0, J)
        warm = next_bank("warm")
        for _ in range(WARM_UPS):
            nc.tensor.matmul_mx(
                out=warm[:, 0:HALF],
                lhsT=pairs[0, 0][:].bitcast(U8)[:, 0 : 2 * CHUNK].bitcast(FP4X4),
                lhsT_scale=w_s[0][:, 0:CHUNK],
                rhs=w_q[0][:, 0:HALF].bitcast(FP8X4),
                rhs_scale=w_s[0][:, 0:HALF],
                start=True,
                stop=True,
            )
        quantize_w(0, 1)
        gather_words(1, HALF, J, "w_raw01")
        parted_tile(1, "w_bf01")
        part_words(1, 0, HALF)
        part_words(1, HALF, J)
        for g in (0, 1):
            for ch in range(CHUNKS):
                neighbour_pass(ch, g, 0)
        round_w(1)
        gather_words(2, 0, HALF, "pairs1_0")
        quantize_w(1, 0)
        quantize_w(1, 1)
        gather_words(2, HALF, J, "w_raw11")
        parted_tile(2, "w_bf11")
        part_words(2, 0, HALF)
        part_words(2, HALF, J)

        for g in (0, 1):
            for ch in (0, 1):
                neighbour_pass(ch, g, 1)
        for ch in (2, 3):
            neighbour_pass(ch, 0, 1)
        round_c(0, 0)
        round_and_interleave(c_raw[1, 0][:, :, CHUNK:HALF], c_bf[0][:, 1, CHUNK * PACK : HALF * PACK], on_vector=True)
        round_and_interleave(c_raw[1, 0][:, :, 0:CHUNK], c_bf[0][:, 1, 0 : CHUNK * PACK])
        firsts = sbuf("firsts", [P, CHUNKS, R], F32)
        for ch in range(CHUNKS):
            best[ch] = firsts[:, ch, :]
            copy_out(ch, best[ch], sums[ch, 0])
        for a in range(PASSES):
            for group in (2, 3):
                round_c(a, group)
        for ch in (0, 1):
            neighbour_sum(ch, 2)
        quantize_c(0)
        for ch in (0, 1):
            take_max(ch, 1)
        for ch in (0, 1):
            own_sum(ch)
        for ch in (0, 1):
            take_max(ch, 2)
        for ch in (2, 3):
            neighbour_pass(ch, 1, 1)
        for ch in (0, 1):
            add_own(ch)
        for ch in (0, 1):
            turn(ch)
        h01 = h_tile(0, 2, "c_bf0")
        for ch in (0, 1):
            nc.scalar.activation(*turned_pairs(ch, h01[:, ch, :]), ACT.Relu)

        neighbour_sum(2, 2)
        seconds = sbuf("seconds", [P, 2, R], F32, "c_q0")
        quantize_c(2)
        take_max(2, 1, seconds[:, 0, :])
        quantize_c(3)
        take_max(2, 2)
        take_max(3, 1, seconds[:, 1, :])
        own_sum(2)
        neighbour_sum(3, 2)
        own_sum(3)
        own_sb = sbuf("own_sb", [P, R], F32)
        copy_out(ADDED, own_sb[:], own[ADDED])
        turned[ADDED] = next_bank("turned%d" % ADDED)
        turn_adding(ADDED, own_sb, True)
        turn_adding(ADDED, best[ADDED], False)
        y01 = second_layer(0, 2, h01, THREE_PIECES)
        larger = sbuf("max32", [P, R], F32)
        z[LAST] = sbuf("z%d" % LAST, [P, R], BF16)
        steps = ((larger, sums[LAST, 2], best[LAST], ALU.max), (z[LAST], own[LAST], larger[:], ALU.add))
        for result, acc, other, op in steps:
            for u in range(2):
                nc.vector.tensor_tensor(
                    sbuf_view(LAST, result[:])[:, u], psum_view(LAST, acc[:])[:, u], sbuf_view(LAST, other)[:, u], op
                )
        turn(LAST)
        h2 = h_tile(ADDED, 1)
        nc.scalar.activation(
            h2[:, 0, :].rearrange("p (j i) -> p j i", i=PACK),
            turned[ADDED][:].rearrange("p (i j) -> p j i", i=PACK),
            ACT.Relu,
        )
        store(0, 2, y01, THREE_PIECES)
        y2 = second_layer(ADDED, 1, h2, TWO_PIECES)
        h3 = h_tile(LAST, 1)
        nc.vector.tensor_scalar(*turned_pairs(LAST, h3[:, 0, :]), 0.0, None, ALU.max)
        y3 = second_layer(LAST, 1, h3, THREE_PIECES)
        store(ADDED, 1, y2, TWO_PIECES)
        store(LAST, 1, y3, THREE_PIECES)
